import numpy as np
import ml_dtypes


def mxq(x, axis, fmt="e4m3"):
    dtype, down = {"e4m3": (ml_dtypes.float8_e4m3fn, 7), "e5m2": (ml_dtypes.float8_e5m2, 14)}[fmt]
    v = np.moveaxis(np.asarray(x, np.float32).astype(ml_dtypes.bfloat16).astype(np.float64), axis, -1)
    blocks = v.reshape(v.shape[:-1] + (-1, 32))
    amax = np.abs(blocks).max(-1, keepdims=True)
    byte = np.maximum(np.where(amax > 0, np.frexp(amax)[1] - 1 + 127, 0) - down, 1)
    scale = np.exp2(byte - 127.0)
    codes = (blocks / scale).astype(np.float32).astype(dtype).astype(np.float64)
    return np.moveaxis((codes * scale).reshape(v.shape), -1, axis)


WIDE = False


def mx_kscale(k):
    if not WIDE:
        return np.ones(k)
    levels = np.array([10, -10, 5, -5, 0])
    if k % 512:
        return np.exp2(np.random.permutation(np.resize(levels, k // 32))).repeat(32)
    a = np.empty((k // 512, 16))
    for p in range(k // 512):
        a[p, :8] = np.random.permutation(np.resize(levels, 8))
        for g in range(8):
            far = levels[np.abs(levels - a[p, g]) >= 10]
            a[p, g + 8] = far[np.random.randint(len(far))]
    return np.exp2(a.ravel()).repeat(32)


def f64(x):
    return np.asarray(x).astype(np.float64)


def striped(idx):
    return np.tile(np.asarray(idx).reshape(-1, 16).T, (8, 1)).astype(np.uint16)


def unstriped(offs):
    return offs[:16].T.reshape(-1).astype(np.int64)

def sigmoid(v):
    return 1.0 / (1.0 + np.exp(-v))


def rot(x):
    y = x.reshape(x.shape[0], -1, 2, x.shape[2])
    return np.stack([-y[:, :, 1], y[:, :, 0]], axis=2).reshape(x.shape)


B, N, T, D, NQ = 1, 512, 2048, 512, 256
DV = 512


def sgn(shape):
    return np.random.uniform(0.5, 2.0, shape) * np.where(np.random.standard_normal(shape) < 0, -1.0, 1.0)


def setup_inputs():
    n = np.random.standard_normal
    idx = np.random.permutation(T)[:B * N]
    idx2 = np.random.permutation(1024)[:B * N]
    s = mx_kscale(D)[:, None]
    u = mx_kscale(N)
    ut = np.ones(T)
    ut[idx] = u
    return {
        "qT": (n((B, D, NQ)) * s * (1.00 / np.sqrt(D))).astype(np.float32),
        "kT": (np.clip(np.round(n((D, T)) * 16), -64, 64) / 16 / s).astype(np.float32),
        "cT": (np.repeat(np.round(np.cos(np.arange(D // 2)[:, None] * 0.11 + np.arange(1024)[None] * 0.37) * 64) / 64, 2, axis=0)).astype(np.float32),
        "wT": (np.repeat(np.round(np.sin(np.arange(D // 2)[:, None] * 0.11 + np.arange(1024)[None] * 0.37) * 64) / 64, 2, axis=0)).astype(np.float32),
        "vT": (n((DV, T)) / ut).astype(np.float32),
        "kb": np.tile(n(2048), (128, 1)).astype(np.float32),
        "us": (sgn((B, N, 1)) * u[:, None]).astype(np.float32),
        "offs": striped(idx),
        "offs2": striped(idx2),
    }


def reference(qT, kT, cT, wT, vT, kb, us, offs, offs2):
    idx = unstriped(offs)
    idx2 = unstriped(offs2)
    pick = lambda x, which: x[:, which].reshape(x.shape[0], B, -1).transpose(1, 0, 2)
    kg = pick(f64(kT), idx)
    cg = pick(f64(cT), idx2)
    wg = pick(f64(wT), idx2)
    ug = mxq(kg * cg + rot(kg) * wg, 1, "e4m3")
    qq = mxq(f64(qT), 1, "e4m3")
    a = ug.transpose(0, 2, 1) @ qq
    y = sigmoid(a + pick(f64(kb), idx)[:, :1, :].transpose(0, 2, 1)) * f64(us)
    wq = mxq(y, 1, "e4m3")
    o = wq.transpose(0, 2, 1) @ mxq(pick(f64(vT), idx).transpose(0, 2, 1), 1, "e4m3")
    return o

@@ -1,0 +1,175 @@
+from contextlib import ExitStack
+
+import concourse.mybir as mybir
+from concourse.masks import make_identity
+
+F32 = mybir.dt.float32
+BF16 = mybir.dt.bfloat16
+U32 = mybir.dt.uint32
+U16 = mybir.dt.uint16
+U8 = mybir.dt.uint8
+FP8X4 = mybir.dt.float8_e4m3fn_x4
+ACT = mybir.ActivationFunctionType
+ALU = mybir.AluOpType
+
+P = 128
+PACK = 4
+N, T, T2, D, NQ, DV = 512, 2048, 1024, 512, 256, 512
+
+FLOPS = 2 * N * NQ * D + 2 * N * NQ * DV
+BYTES = 4 * (D * NQ + D * T + 2 * D * T2 + DV * T + T + N + NQ * DV) + 2 * 2 * P * (N // 16)
+
+
+def tile_attend_at_ropesig_f_topk_kernel(tc, qT, kT, cT, wT, vT, kb, us, offs, offs2, out):
+    nc = tc.nc
+    with ExitStack() as ctx:
+        keep = ctx.enter_context(tc.tile_pool(name="keep", bufs=1))
+        psum = ctx.enter_context(tc.psum_pool(name="psum", bufs=1))
+
+        def sb(shape, dtype, name):
+            return keep.tile(shape, dtype, name=name, align_bytes=64)
+
+        tok = sb([P, N // 16], U16, "tok")
+        pos = sb([P, N // 16], U16, "pos")
+        nc.sync.dma_start(tok[:], offs)
+        nc.sync.dma_start(pos[:], offs2)
+
+        k_rows = kT.rearrange("(p j) n -> p j n", j=PACK)
+        c_rows = cT.rearrange("(p j) n -> p j n", j=PACK)
+        w_rows = wT.rearrange("(p j) n -> p j n", j=PACK)
+        k_win = [sb([P, T], F32, f"k_win{j}") for j in range(PACK)]
+        c_win = [sb([P, T2], F32, f"c_win{j}") for j in range(PACK)]
+        w_win = [sb([P, T2], F32, f"w_win{j}") for j in range(PACK)]
+        v_win = [sb([P, T], F32, f"v_win{j}") for j in range(DV // P)]
+        for j in range(PACK):
+            nc.sync.dma_start(k_win[j][:], k_rows[:, j, :])
+            nc.sync.dma_start(c_win[j][:], c_rows[:, j, :])
+            nc.sync.dma_start(w_win[j ^ 1][:], w_rows[:, j ^ 1, :])
+        q_raw = sb([P, PACK, NQ], F32, "q_raw")
+        nc.sync.dma_start(q_raw[:], qT[0].rearrange("(p j) q -> p j q", j=PACK))
+        for b in range(DV // P):
+            nc.sync.dma_start(v_win[b][:], vT[b * P:(b + 1) * P, :])
+
+        warm_in = sb([P, 1], F32, "warm_in")
+        warm_out = sb([P, 1], F32, "warm_out")
+        nc.vector.memset(warm_in[:], 0.0)
+        nc.scalar.activation(warm_out[:], warm_in[:], ACT.Sigmoid)
+
+        kb_win = sb([P, T], F32, "kb_win")
+        nc.vector.memset(kb_win[:], 0.0)
+        nc.scalar.dma_start(kb_win[0:1, :], kb[0:1, :])
+        us_sb = sb([P, PACK], F32, "us_sb")
+        nc.scalar.dma_start(us_sb[:], us[0].rearrange("(p t) o -> p (t o)", t=PACK))
+
+        ident_f = sb([P, P], F32, "ident_f")
+        ident_b = sb([P, P], BF16, "ident_b")
+        make_identity(nc, ident_f[:])
+        make_identity(nc, ident_b[:])
+
+        kb_g = sb([P, N], F32, "kb_g")
+        nc.vector.tensor_copy(kb_g[:], kb_win[:].indirect(tok[:]))
+        kb_ps = psum.tile([P, PACK, P], F32, name="kb_ps")
+        kb_by_t = kb_g[:].rearrange("p (m t) -> p t m", t=PACK)
+        for t in range(PACK):
+            nc.tensor.transpose(kb_ps[:, t, :], kb_by_t[:, t, :], ident_f[:])
+        bias = sb([P, PACK], F32, "bias")
+        nc.scalar.copy(bias[:], kb_ps[:, :, 0])
+
+        u_bf = sb([P, PACK, P, PACK], BF16, "u_bf")
+        for pair in range(2):
+            ev, od = 2 * pair, 2 * pair + 1
+            k_ev = sb([P, N], F32, f"k_ev{pair}")
+            k_od = sb([P, N], F32, f"k_od{pair}")
+            k_neg = sb([P, N], F32, f"k_neg{pair}")
+            kc = sb([P, 2, N], F32, f"kc{pair}")
+            kw = sb([P, 2, N], F32, f"kw{pair}")
+            nc.vector.tensor_copy(k_ev[:], k_win[ev][:].indirect(tok[:]))
+            nc.vector.tensor_tensor(kc[:, 0, :], c_win[ev][:].indirect(pos[:]), k_ev[:], ALU.mult)
+            nc.vector.tensor_tensor(kw[:, 1, :], w_win[od][:].indirect(pos[:]), k_ev[:], ALU.mult)
+            nc.vector.tensor_copy(k_od[:], k_win[od][:].indirect(tok[:]))
+            nc.scalar.activation(k_neg[:], k_od[:], ACT.Copy, scale=-1.0)
+            nc.vector.tensor_tensor(kc[:, 1, :], c_win[od][:].indirect(pos[:]), k_od[:], ALU.mult)
+            nc.vector.tensor_tensor(kw[:, 0, :], w_win[ev][:].indirect(pos[:]), k_neg[:], ALU.mult)
+            nc.vector.tensor_tensor(
+                u_bf[:, :, :, ev:ev + 2].rearrange("p t m j -> p m t j"),
+                kc[:].rearrange("p j (m t) -> p m t j", t=PACK),
+                kw[:].rearrange("p j (m t) -> p m t j", t=PACK),
+                ALU.add,
+            )
+
+        q_bf = sb([P, NQ, PACK], BF16, "q_bf")
+        nc.scalar.copy(q_bf[:], q_raw[:].rearrange("p j q -> p q j"))
+
+        u_codes = sb([P, N], U32, "u_codes")
+        u_scales = sb([P, N], U8, "u_scales")
+        nc.vector.quantize_mx(u_codes[:].bitcast(FP8X4), u_scales[:], u_bf[:].rearrange("p t m j -> p (t m j)"))
+        q_codes = sb([P, NQ], U32, "q_codes")
+        q_scales = sb([P, NQ], U8, "q_scales")
+        nc.vector.quantize_mx(q_codes[:].bitcast(FP8X4), q_scales[:], q_bf[:].rearrange("p q j -> p (q j)"))
+
+        sig = sb([P, PACK, NQ], F32, "sig")
+        s_ps = [psum.tile([P, 2, NQ], F32, name=f"s_ps{i}", tag=f"s_bank{i}") for i in range(2)]
+        for t in range(PACK):
+            cols = slice(t * P, (t + 1) * P)
+            nc.tensor.matmul_mx(
+                s_ps[t // 2][:, t % 2, :], lhsT=u_codes[:, cols].bitcast(FP8X4), lhsT_scale=u_scales[:, cols],
+                rhs=q_codes[:].bitcast(FP8X4), rhs_scale=q_scales[:], start=True, stop=True)
+        for t in range(PACK):
+            nc.scalar.activation(sig[:, t, :], s_ps[t // 2][:, t % 2, :], ACT.Sigmoid, bias=bias[:, t:t + 1])
+
+        v_codes = sb([P, DV], U32, "v_codes")
+        v_scales = sb([P, DV], U8, "v_scales")
+        v_bf = [sb([P, P, PACK], BF16, f"v_bf{b}") for b in range(DV // P)]
+
+        def gather_values(b):
+            v_g = sb([P, PACK, P], BF16, f"v_g{b}")
+            nc.vector.tensor_copy(v_g[:].rearrange("p t m -> p m t"), v_win[b][:].indirect(tok[:]))
+            v_ps = psum.tile([P, PACK, P], BF16, name=f"v_ps{b}", tag=f"v_bank{b % 2}")
+            for t in range(PACK):
+                nc.tensor.transpose(v_ps[:, t, :], v_g[:, t, :], ident_b[:])
+            nc.scalar.copy(v_bf[b][:], v_ps[:].rearrange("p t e -> p e t"))
+
+        def quantize_values(b):
+            cols = slice(b * P, (b + 1) * P)
+            nc.vector.quantize_mx(v_codes[:, cols].bitcast(FP8X4), v_scales[:, cols],
+                                  v_bf[b][:].rearrange("p e t -> p (e t)"))
+
+        y_bf = sb([P, NQ, PACK], BF16, "y_bf")
+        y_codes = sb([P, NQ], U32, "y_codes")
+        y_scales = sb([P, NQ], U8, "y_scales")
+        out_rows = out[0].rearrange("(h p) e -> p h e", p=P)
+
+        def product(bank, h, e0, e1):
+            rows = slice(h * P, (h + 1) * P)
+            nc.tensor.matmul_mx(
+                bank, lhsT=y_codes[:, rows].bitcast(FP8X4), lhsT_scale=y_scales[:, rows],
+                rhs=v_codes[:, e0:e1].bitcast(FP8X4), rhs_scale=v_scales[:, e0:e1], start=True, stop=True)
+
+        gather_values(0)
+        gather_values(1)
+        nc.vector.tensor_tensor(
+            y_bf[:], sig[:].rearrange("p t q -> p q t"),
+            us_sb[:].unsqueeze(1).to_broadcast([P, NQ, PACK]), ALU.mult)
+        gather_values(2)
+        nc.vector.quantize_mx(y_codes[:].bitcast(FP8X4), y_scales[:], y_bf[:].rearrange("p q t -> p (q t)"))
+        quantize_values(0)
+        quantize_values(1)
+        gather_values(3)
+        quantize_values(2)
+        quantize_values(3)
+
+        for i, (e0, e1) in enumerate(((0, 2 * P), (2 * P, 3 * P))):
+            o_ps = psum.tile([P, 2, e1 - e0], F32, name=f"o_ps{i}", tag=f"s_bank{i}")
+            o_sb = sb([P, 2, e1 - e0], F32, f"o_sb{i}")
+            for h in range(2):
+                product(o_ps[:, h, :], h, e0, e1)
+            nc.scalar.copy(o_sb[:], o_ps[:])
+            nc.sync.dma_start(out_rows[:, :, e0:e1], o_sb[:])
+
+        o_last = sb([P, 2, P], F32, "o_last")
+        last_ps = [psum.tile([P, P], F32, name=f"last_ps{h}") for h in range(2)]
+        for h in range(2):
+            product(last_ps[h][:], h, 3 * P, DV)
+        nc.scalar.copy(o_last[:, 0, :], last_ps[0][:])
+        nc.vector.tensor_copy(o_last[:, 1, :], last_ps[1][:])
+        nc.sync.dma_start(out_rows[:, :, 3 * P:DV], o_last[:])

@@ -26,8 +26,8 @@ def tile_attend_at_ropesig_f_topk_kernel(tc, qT, kT, cT, wT, vT, kb, us, offs, o
         keep = ctx.enter_context(tc.tile_pool(name="keep", bufs=1))
         psum = ctx.enter_context(tc.psum_pool(name="psum", bufs=1))
 
-        def sb(shape, dtype, name):
-            return keep.tile(shape, dtype, name=name, align_bytes=64)
+        def sb(shape, dtype, name, slot=None):
+            return keep.tile(shape, dtype, name=name, tag=slot or name, align_bytes=64)
 
         tok = sb([P, N // 16], U16, "tok")
         pos = sb([P, N // 16], U16, "pos")
@@ -41,71 +41,77 @@ def tile_attend_at_ropesig_f_topk_kernel(tc, qT, kT, cT, wT, vT, kb, us, offs, o
         c_win = [sb([P, T2], F32, f"c_win{j}") for j in range(PACK)]
         w_win = [sb([P, T2], F32, f"w_win{j}") for j in range(PACK)]
         v_win = [sb([P, T], F32, f"v_win{j}") for j in range(DV // P)]
-        for j in range(PACK):
-            nc.sync.dma_start(k_win[j][:], k_rows[:, j, :])
-            nc.sync.dma_start(c_win[j][:], c_rows[:, j, :])
-            nc.sync.dma_start(w_win[j ^ 1][:], w_rows[:, j ^ 1, :])
+        for ev in (0, 2):
+            od = ev + 1
+            nc.sync.dma_start(k_win[ev][:], k_rows[:, ev, :])
+            nc.sync.dma_start(k_win[od][:], k_rows[:, od, :])
+            nc.sync.dma_start(c_win[ev][:], c_rows[:, ev, :])
+            nc.sync.dma_start(w_win[od][:], w_rows[:, od, :])
+            nc.sync.dma_start(c_win[od][:], c_rows[:, od, :])
+            nc.sync.dma_start(w_win[ev][:], w_rows[:, ev, :])
         q_raw = sb([P, PACK, NQ], F32, "q_raw")
         nc.sync.dma_start(q_raw[:], qT[0].rearrange("(p j) q -> p j q", j=PACK))
         for b in range(DV // P):
             nc.sync.dma_start(v_win[b][:], vT[b * P:(b + 1) * P, :])
 
-        warm_in = sb([P, 1], F32, "warm_in")
-        warm_out = sb([P, 1], F32, "warm_out")
-        nc.vector.memset(warm_in[:], 0.0)
-        nc.scalar.activation(warm_out[:], warm_in[:], ACT.Sigmoid)
-
         kb_win = sb([P, T], F32, "kb_win")
-        nc.vector.memset(kb_win[:], 0.0)
+        nc.vector.memset(kb_win[:, :T // 2], 0.0)
+        nc.gpsimd.memset(kb_win[:, T // 2:], 0.0)
         nc.scalar.dma_start(kb_win[0:1, :], kb[0:1, :])
         us_sb = sb([P, PACK], F32, "us_sb")
-        nc.scalar.dma_start(us_sb[:], us[0].rearrange("(p t) o -> p (t o)", t=PACK))
+        nc.gpsimd.dma_start(us_sb[:], us[0].rearrange("(p t) o -> p (t o)", t=PACK))
+        warm = sb([P, 1], F32, "warm")
+        nc.scalar.activation(warm[:], us_sb[:, 0:1], ACT.Sigmoid)
 
         ident_f = sb([P, P], F32, "ident_f")
         ident_b = sb([P, P], BF16, "ident_b")
         make_identity(nc, ident_f[:])
         make_identity(nc, ident_b[:])
 
-        kb_g = sb([P, N], F32, "kb_g")
-        nc.vector.tensor_copy(kb_g[:], kb_win[:].indirect(tok[:]))
-        kb_ps = psum.tile([P, PACK, P], F32, name="kb_ps")
-        kb_by_t = kb_g[:].rearrange("p (m t) -> p t m", t=PACK)
-        for t in range(PACK):
-            nc.tensor.transpose(kb_ps[:, t, :], kb_by_t[:, t, :], ident_f[:])
         bias = sb([P, PACK], F32, "bias")
-        nc.scalar.copy(bias[:], kb_ps[:, :, 0])
+
+        def gather_bias():
+            kb_g = sb([P, N], F32, "kb_g")
+            nc.vector.tensor_copy(kb_g[:], kb_win[:].indirect(tok[:]))
+            kb_ps = psum.tile([P, PACK, P], F32, name="kb_ps")
+            kb_by_t = kb_g[:].rearrange("p (m t) -> p t m", t=PACK)
+            for t in range(PACK):
+                nc.tensor.transpose(kb_ps[:, t, :], kb_by_t[:, t, :], ident_f[:])
+            nc.scalar.copy(bias[:], kb_ps[:, :, 0])
 
         u_bf = sb([P, PACK, P, PACK], BF16, "u_bf")
         for pair in range(2):
             ev, od = 2 * pair, 2 * pair + 1
-            k_ev = sb([P, N], F32, f"k_ev{pair}")
-            k_od = sb([P, N], F32, f"k_od{pair}")
+            k_ev = sb([P, N], F32, f"k_ev{pair}", slot=("k_ev0", "k_neg0")[pair])
             k_neg = sb([P, N], F32, f"k_neg{pair}")
-            kc = sb([P, 2, N], F32, f"kc{pair}")
-            kw = sb([P, 2, N], F32, f"kw{pair}")
             nc.vector.tensor_copy(k_ev[:], k_win[ev][:].indirect(tok[:]))
-            nc.vector.tensor_tensor(kc[:, 0, :], c_win[ev][:].indirect(pos[:]), k_ev[:], ALU.mult)
-            nc.vector.tensor_tensor(kw[:, 1, :], w_win[od][:].indirect(pos[:]), k_ev[:], ALU.mult)
+            if pair == 0:
+                gather_bias()
+            k_od = sb([P, N], F32, f"k_od{pair}", slot=("kb_win", "w_win0")[pair])
             nc.vector.tensor_copy(k_od[:], k_win[od][:].indirect(tok[:]))
             nc.scalar.activation(k_neg[:], k_od[:], ACT.Copy, scale=-1.0)
+            prod = sb([P, 2, 2, N], F32, f"prod{pair}", slot=("k_win1", "prod1")[pair])
+            kc, kw = prod[:, 0, :, :], prod[:, 1, :, :]
+            nc.vector.tensor_tensor(kc[:, 0, :], c_win[ev][:].indirect(pos[:]), k_ev[:], ALU.mult)
+            nc.vector.tensor_tensor(kw[:, 1, :], w_win[od][:].indirect(pos[:]), k_ev[:], ALU.mult)
             nc.vector.tensor_tensor(kc[:, 1, :], c_win[od][:].indirect(pos[:]), k_od[:], ALU.mult)
             nc.vector.tensor_tensor(kw[:, 0, :], w_win[ev][:].indirect(pos[:]), k_neg[:], ALU.mult)
             nc.vector.tensor_tensor(
                 u_bf[:, :, :, ev:ev + 2].rearrange("p t m j -> p m t j"),
-                kc[:].rearrange("p j (m t) -> p m t j", t=PACK),
-                kw[:].rearrange("p j (m t) -> p m t j", t=PACK),
+                kc.rearrange("p j (m t) -> p m t j", t=PACK),
+                kw.rearrange("p j (m t) -> p m t j", t=PACK),
                 ALU.add,
             )
 
-        q_bf = sb([P, NQ, PACK], BF16, "q_bf")
+        q_bf = sb([P, NQ, PACK], BF16, "q_bf", slot="w_win0")
         nc.scalar.copy(q_bf[:], q_raw[:].rearrange("p j q -> p q j"))
 
+        q_codes = sb([P, NQ], U32, "q_codes", slot="prod1")
+        q_scales = sb([P, NQ], U8, "q_scales")
+        nc.vector.quantize_mx(q_codes[:].bitcast(FP8X4), q_scales[:], q_bf[:].rearrange("p q j -> p (q j)"))
         u_codes = sb([P, N], U32, "u_codes")
         u_scales = sb([P, N], U8, "u_scales")
         nc.vector.quantize_mx(u_codes[:].bitcast(FP8X4), u_scales[:], u_bf[:].rearrange("p t m j -> p (t m j)"))
-        q_codes = sb([P, NQ], U32, "q_codes")
-        q_scales = sb([P, NQ], U8, "q_scales")
-        nc.vector.quantize_mx(q_codes[:].bitcast(FP8X4), q_scales[:], q_bf[:].rearrange("p q j -> p (q j)"))
 
         sig = sb([P, PACK, NQ], F32, "sig")
         s_ps = [psum.tile([P, 2, NQ], F32, name=f"s_ps{i}", tag=f"s_bank{i}") for i in range(2)]
@@ -122,7 +128,7 @@ def tile_attend_at_ropesig_f_topk_kernel(tc, qT, kT, cT, wT, vT, kb, us, offs, o
         v_bf = [sb([P, P, PACK], BF16, f"v_bf{b}") for b in range(DV // P)]
 
         def gather_values(b):
-            v_g = sb([P, PACK, P], BF16, f"v_g{b}")
+            v_g = sb([P, PACK, P], BF16, f"v_g{b}", slot=("w_win0", "u_bf", "bias", "sig")[b])
             nc.vector.tensor_copy(v_g[:].rearrange("p t m -> p m t"), v_win[b][:].indirect(tok[:]))
             v_ps = psum.tile([P, PACK, P], BF16, name=f"v_ps{b}", tag=f"v_bank{b % 2}")
             for t in range(PACK):
@@ -163,7 +169,10 @@ def tile_attend_at_ropesig_f_topk_kernel(tc, qT, kT, cT, wT, vT, kb, us, offs, o
             o_sb = sb([P, 2, e1 - e0], F32, f"o_sb{i}")
             for h in range(2):
                 product(o_ps[:, h, :], h, e0, e1)
-            nc.scalar.copy(o_sb[:], o_ps[:])
+            if i == 0:
+                nc.scalar.copy(o_sb[:], o_ps[:])
+            else:
+                nc.vector.tensor_copy(o_sb[:], o_ps[:])
             nc.sync.dma_start(out_rows[:, :, e0:e1], o_sb[:])
 
         o_last = sb([P, 2, P], F32, "o_last")

@@ -123,62 +123,68 @@ def tile_attend_at_ropesig_f_topk_kernel(tc, qT, kT, cT, wT, vT, kb, us, offs, o
         for t in range(PACK):
             nc.scalar.activation(sig[:, t, :], s_ps[t // 2][:, t % 2, :], ACT.Sigmoid, bias=bias[:, t:t + 1])
 
-        v_codes = sb([P, DV], U32, "v_codes")
-        v_scales = sb([P, DV], U8, "v_scales")
-        v_bf = [sb([P, P, PACK], BF16, f"v_bf{b}") for b in range(DV // P)]
-
-        def gather_values(b):
+        def gather_values(b, dest):
             v_g = sb([P, PACK, P], BF16, f"v_g{b}", slot=("w_win0", "u_bf", "bias", "sig")[b])
             nc.vector.tensor_copy(v_g[:].rearrange("p t m -> p m t"), v_win[b][:].indirect(tok[:]))
             v_ps = psum.tile([P, PACK, P], BF16, name=f"v_ps{b}", tag=f"v_bank{b % 2}")
             for t in range(PACK):
                 nc.tensor.transpose(v_ps[:, t, :], v_g[:, t, :], ident_b[:])
-            nc.scalar.copy(v_bf[b][:], v_ps[:].rearrange("p t e -> p e t"))
+            return v_ps
 
-        def quantize_values(b):
-            cols = slice(b * P, (b + 1) * P)
-            nc.vector.quantize_mx(v_codes[:, cols].bitcast(FP8X4), v_scales[:, cols],
-                                  v_bf[b][:].rearrange("p e t -> p (e t)"))
+        def interleave_values(dest, v_ps):
+            nc.scalar.copy(dest, v_ps[:].rearrange("p t e -> p e t"))
 
-        y_bf = sb([P, NQ, PACK], BF16, "y_bf")
-        y_codes = sb([P, NQ], U32, "y_codes")
-        y_scales = sb([P, NQ], U8, "y_scales")
+        def quantize(name, source, slot):
+            width = source.shape[1]
+            codes = sb([P, width], U32, f"{name}_codes", slot=slot)
+            scales = sb([P, width], U8, f"{name}_scales")
+            nc.vector.quantize_mx(codes[:].bitcast(FP8X4), scales[:], source.rearrange("p c t -> p (c t)"))
+            return codes, scales
+
+        v_ps0 = gather_values(0, None)
+        v_ps1 = gather_values(1, None)
+        yv_bf = sb([P, NQ + 2 * P, PACK], BF16, "yv_bf", slot="v_win1")
+        interleave_values(yv_bf[:, NQ:NQ + P, :], v_ps0)
+        interleave_values(yv_bf[:, NQ + P:, :], v_ps1)
+        nc.vector.tensor_tensor(
+            yv_bf[:, :NQ, :], sig[:].rearrange("p t q -> p q t"),
+            us_sb[:].unsqueeze(1).to_broadcast([P, NQ, PACK]), ALU.mult)
+        v_ps2 = gather_values(2, None)
+        v2_bf = sb([P, P, PACK], BF16, "v2_bf")
+        interleave_values(v2_bf[:], v_ps2)
+        yv_codes, yv_scales = quantize("yv", yv_bf[:], "v_win2")
+        v_ps3 = gather_values(3, None)
+        v3_bf = sb([P, P, PACK], BF16, "v3_bf")
+        interleave_values(v3_bf[:], v_ps3)
+        v2_codes, v2_scales = quantize("v2", v2_bf[:], "v_win3")
+        v3_codes, v3_scales = quantize("v3", v3_bf[:], None)
+
         out_rows = out[0].rearrange("(h p) e -> p h e", p=P)
 
-        def product(bank, h, e0, e1):
+        def product(bank, h, codes, scales):
             rows = slice(h * P, (h + 1) * P)
             nc.tensor.matmul_mx(
-                bank, lhsT=y_codes[:, rows].bitcast(FP8X4), lhsT_scale=y_scales[:, rows],
-                rhs=v_codes[:, e0:e1].bitcast(FP8X4), rhs_scale=v_scales[:, e0:e1], start=True, stop=True)
+                bank, lhsT=yv_codes[:, rows].bitcast(FP8X4), lhsT_scale=yv_scales[:, rows],
+                rhs=codes.bitcast(FP8X4), rhs_scale=scales, start=True, stop=True)
 
-        gather_values(0)
-        gather_values(1)
-        nc.vector.tensor_tensor(
-            y_bf[:], sig[:].rearrange("p t q -> p q t"),
-            us_sb[:].unsqueeze(1).to_broadcast([P, NQ, PACK]), ALU.mult)
-        gather_values(2)
-        nc.vector.quantize_mx(y_codes[:].bitcast(FP8X4), y_scales[:], y_bf[:].rearrange("p q t -> p (q t)"))
-        quantize_values(0)
-        quantize_values(1)
-        gather_values(3)
-        quantize_values(2)
-        quantize_values(3)
+        o_ps0 = psum.tile([P, 2, 2 * P], F32, name="o_ps0", tag="s_bank0")
+        o_sb0 = sb([P, 2, 2 * P], F32, "o_sb0")
+        for h in range(2):
+            product(o_ps0[:, h, :], h, yv_codes[:, NQ:], yv_scales[:, NQ:])
+        nc.scalar.copy(o_sb0[:], o_ps0[:])
+        nc.sync.dma_start(out_rows[:, :, :2 * P], o_sb0[:])
 
-        for i, (e0, e1) in enumerate(((0, 2 * P), (2 * P, 3 * P))):
-            o_ps = psum.tile([P, 2, e1 - e0], F32, name=f"o_ps{i}", tag=f"s_bank{i}")
-            o_sb = sb([P, 2, e1 - e0], F32, f"o_sb{i}")
-            for h in range(2):
-                product(o_ps[:, h, :], h, e0, e1)
-            if i == 0:
-                nc.scalar.copy(o_sb[:], o_ps[:])
-            else:
-                nc.vector.tensor_copy(o_sb[:], o_ps[:])
-            nc.sync.dma_start(out_rows[:, :, e0:e1], o_sb[:])
+        o_ps1 = psum.tile([P, 2, P], F32, name="o_ps1", tag="s_bank1")
+        o_sb1 = sb([P, 2, P], F32, "o_sb1")
+        for h in range(2):
+            product(o_ps1[:, h, :], h, v2_codes[:], v2_scales[:])
+        nc.vector.tensor_copy(o_sb1[:], o_ps1[:])
+        nc.sync.dma_start(out_rows[:, :, 2 * P:3 * P], o_sb1[:])
 
         o_last = sb([P, 2, P], F32, "o_last")
         last_ps = [psum.tile([P, P], F32, name=f"last_ps{h}") for h in range(2)]
         for h in range(2):
-            product(last_ps[h][:], h, 3 * P, DV)
+            product(last_ps[h][:], h, v3_codes[:], v3_scales[:])
         nc.scalar.copy(o_last[:, 0, :], last_ps[0][:])
         nc.vector.tensor_copy(o_last[:, 1, :], last_ps[1][:])
         nc.sync.dma_start(out_rows[:, :, 3 * P:DV], o_last[:])

@@ -14,10 +14,17 @@ ALU = mybir.AluOpType
 
 P = 128
 PACK = 4
-N, T, T2, D, NQ, DV = 512, 2048, 1024, 512, 256, 512
+N = 512
+T = 2048
+POSITIONS = 1024
+D = 512
+NQ = 256
+DV = 512
+
+FIRST_PLANE_CUTS = (0, 128, 256, 512, 1024, 2048)
 
 FLOPS = 2 * N * NQ * D + 2 * N * NQ * DV
-BYTES = 4 * (D * NQ + D * T + 2 * D * T2 + DV * T + T + N + NQ * DV) + 2 * 2 * P * (N // 16)
+BYTES = 4 * (D * NQ + D * T + 2 * D * POSITIONS + DV * T + T + N + NQ * DV) + 2 * 2 * P * (N // 16)
 
 
 def tile_attend_at_ropesig_f_topk_kernel(tc, qT, kT, cT, wT, vT, kb, us, offs, offs2, out):
@@ -26,42 +33,52 @@ def tile_attend_at_ropesig_f_topk_kernel(tc, qT, kT, cT, wT, vT, kb, us, offs, o
         keep = ctx.enter_context(tc.tile_pool(name="keep", bufs=1))
         psum = ctx.enter_context(tc.psum_pool(name="psum", bufs=1))
 
-        def sb(shape, dtype, name, slot=None):
-            return keep.tile(shape, dtype, name=name, tag=slot or name, align_bytes=64)
+        def sb(shape, dtype, name, buffer_of=None):
+            return keep.tile(shape, dtype, name=name, tag=buffer_of or name, align_bytes=64)
+
+        def quantize(name, source, buffer_of=None):
+            width = source.shape[1]
+            codes = sb([P, width], U32, f"{name}_codes", buffer_of)
+            scales = sb([P, width], U8, f"{name}_scales")
+            nc.vector.quantize_mx(codes[:].bitcast(FP8X4), scales[:], source.rearrange("p c j -> p (c j)"))
+            return codes, scales
 
         tok = sb([P, N // 16], U16, "tok")
         pos = sb([P, N // 16], U16, "pos")
-        nc.sync.dma_start(tok[:], offs)
-        nc.sync.dma_start(pos[:], offs2)
-
+        us_sb = sb([P, PACK], F32, "us_sb")
+        kb_win = sb([P, T], F32, "kb_win")
+        q_raw = sb([P, PACK, NQ], F32, "q_raw")
+        k_win = [sb([P, T], F32, f"k_win{j}") for j in range(PACK)]
+        c_win = [sb([P, POSITIONS], F32, f"c_win{j}") for j in range(PACK)]
+        w_win = [sb([P, POSITIONS], F32, f"w_win{j}") for j in range(PACK)]
+        v_win = [sb([P, T], F32, f"v_win{b}") for b in range(DV // P)]
         k_rows = kT.rearrange("(p j) n -> p j n", j=PACK)
         c_rows = cT.rearrange("(p j) n -> p j n", j=PACK)
         w_rows = wT.rearrange("(p j) n -> p j n", j=PACK)
-        k_win = [sb([P, T], F32, f"k_win{j}") for j in range(PACK)]
-        c_win = [sb([P, T2], F32, f"c_win{j}") for j in range(PACK)]
-        w_win = [sb([P, T2], F32, f"w_win{j}") for j in range(PACK)]
-        v_win = [sb([P, T], F32, f"v_win{j}") for j in range(DV // P)]
+        token_halves = (slice(0, T // 2), slice(T // 2, T))
+
+        nc.vector.memset(kb_win[:, token_halves[0]], 0.0)
+        nc.gpsimd.memset(kb_win[:, token_halves[1]], 0.0)
+        for lo, hi in zip(FIRST_PLANE_CUTS, FIRST_PLANE_CUTS[1:]):
+            nc.sync.dma_start(k_win[0][:, lo:hi], k_rows[:, 0, lo:hi])
+        nc.sync.dma_start(tok[:], offs)
+        nc.sync.dma_start(pos[:], offs2)
+        nc.sync.dma_start(us_sb[:], us[0].rearrange("(p t) o -> p (t o)", t=PACK))
+        nc.sync.dma_start(kb_win[0:1, :], kb[0:1, :])
         for ev in (0, 2):
             od = ev + 1
-            nc.sync.dma_start(k_win[ev][:], k_rows[:, ev, :])
+            if ev > 0:
+                nc.sync.dma_start(k_win[ev][:], k_rows[:, ev, :])
             nc.sync.dma_start(k_win[od][:], k_rows[:, od, :])
             nc.sync.dma_start(c_win[ev][:], c_rows[:, ev, :])
             nc.sync.dma_start(w_win[od][:], w_rows[:, od, :])
             nc.sync.dma_start(c_win[od][:], c_rows[:, od, :])
             nc.sync.dma_start(w_win[ev][:], w_rows[:, ev, :])
-        q_raw = sb([P, PACK, NQ], F32, "q_raw")
+        nc.sync.dma_start(v_win[0][:, token_halves[0]], vT[:P, token_halves[0]])
         nc.sync.dma_start(q_raw[:], qT[0].rearrange("(p j) q -> p j q", j=PACK))
-        for b in range(DV // P):
+        nc.sync.dma_start(v_win[0][:, token_halves[1]], vT[:P, token_halves[1]])
+        for b in range(1, DV // P):
             nc.sync.dma_start(v_win[b][:], vT[b * P:(b + 1) * P, :])
-
-        kb_win = sb([P, T], F32, "kb_win")
-        nc.vector.memset(kb_win[:, :T // 2], 0.0)
-        nc.gpsimd.memset(kb_win[:, T // 2:], 0.0)
-        nc.scalar.dma_start(kb_win[0:1, :], kb[0:1, :])
-        us_sb = sb([P, PACK], F32, "us_sb")
-        nc.gpsimd.dma_start(us_sb[:], us[0].rearrange("(p t) o -> p (t o)", t=PACK))
-        warm = sb([P, 1], F32, "warm")
-        nc.scalar.activation(warm[:], us_sb[:, 0:1], ACT.Sigmoid)
 
         ident_f = sb([P, P], F32, "ident_f")
         ident_b = sb([P, P], BF16, "ident_b")
@@ -82,109 +99,105 @@ def tile_attend_at_ropesig_f_topk_kernel(tc, qT, kT, cT, wT, vT, kb, us, offs, o
         u_bf = sb([P, PACK, P, PACK], BF16, "u_bf")
         for pair in range(2):
             ev, od = 2 * pair, 2 * pair + 1
-            k_ev = sb([P, N], F32, f"k_ev{pair}", slot=("k_ev0", "k_neg0")[pair])
+            k_ev = sb([P, N], F32, f"k_ev{pair}", (None, "k_neg0")[pair])
             k_neg = sb([P, N], F32, f"k_neg{pair}")
             nc.vector.tensor_copy(k_ev[:], k_win[ev][:].indirect(tok[:]))
             if pair == 0:
                 gather_bias()
-            k_od = sb([P, N], F32, f"k_od{pair}", slot=("kb_win", "w_win0")[pair])
+            k_od = sb([P, N], F32, f"k_od{pair}", (None, "w_win0")[pair])
             nc.vector.tensor_copy(k_od[:], k_win[od][:].indirect(tok[:]))
             nc.scalar.activation(k_neg[:], k_od[:], ACT.Copy, scale=-1.0)
-            prod = sb([P, 2, 2, N], F32, f"prod{pair}", slot=("k_win1", "prod1")[pair])
-            kc, kw = prod[:, 0, :, :], prod[:, 1, :, :]
+            kc = sb([P, 2, N], F32, f"kc{pair}")
+            kw = sb([P, 2, N], F32, f"kw{pair}")
             nc.vector.tensor_tensor(kc[:, 0, :], c_win[ev][:].indirect(pos[:]), k_ev[:], ALU.mult)
             nc.vector.tensor_tensor(kw[:, 1, :], w_win[od][:].indirect(pos[:]), k_ev[:], ALU.mult)
             nc.vector.tensor_tensor(kc[:, 1, :], c_win[od][:].indirect(pos[:]), k_od[:], ALU.mult)
             nc.vector.tensor_tensor(kw[:, 0, :], w_win[ev][:].indirect(pos[:]), k_neg[:], ALU.mult)
-            nc.vector.tensor_tensor(
-                u_bf[:, :, :, ev:ev + 2].rearrange("p t m j -> p m t j"),
-                kc.rearrange("p j (m t) -> p m t j", t=PACK),
-                kw.rearrange("p j (m t) -> p m t j", t=PACK),
-                ALU.add,
-            )
+            u_pair = u_bf[:, :, :, ev:ev + 2].rearrange("p t m j -> p m t j")
+            if pair == 0:
+                u_first = sb([P, 2, N], BF16, "u_first")
+                nc.vector.tensor_tensor(u_first[:], kc[:], kw[:], ALU.add)
+                nc.scalar.copy(u_pair, u_first[:].rearrange("p j (m t) -> p m t j", t=PACK))
+            else:
+                nc.vector.tensor_tensor(
+                    u_pair, kc[:].rearrange("p j (m t) -> p m t j", t=PACK),
+                    kw[:].rearrange("p j (m t) -> p m t j", t=PACK), ALU.add)
 
-        q_bf = sb([P, NQ, PACK], BF16, "q_bf", slot="w_win0")
+        q_bf = sb([P, NQ, PACK], BF16, "q_bf", "w_win0")
         nc.scalar.copy(q_bf[:], q_raw[:].rearrange("p j q -> p q j"))
+        q_codes, q_scales = quantize("q", q_bf[:], "kc1")
+        u_halves = [
+            quantize(f"u{half}", u_bf[:, 2 * half:2 * half + 2].rearrange("p t m j -> p (t m) j"))
+            for half in range(2)
+        ]
 
-        q_codes = sb([P, NQ], U32, "q_codes", slot="prod1")
-        q_scales = sb([P, NQ], U8, "q_scales")
-        nc.vector.quantize_mx(q_codes[:].bitcast(FP8X4), q_scales[:], q_bf[:].rearrange("p q j -> p (q j)"))
-        u_codes = sb([P, N], U32, "u_codes")
-        u_scales = sb([P, N], U8, "u_scales")
-        nc.vector.quantize_mx(u_codes[:].bitcast(FP8X4), u_scales[:], u_bf[:].rearrange("p t m j -> p (t m j)"))
+        v0_win = sb([P, T], BF16, "v0_win")
+        for tokens in token_halves:
+            nc.scalar.activation(v0_win[:, tokens], v_win[0][:, tokens], ACT.Copy)
 
-        sig = sb([P, PACK, NQ], F32, "sig")
-        s_ps = [psum.tile([P, 2, NQ], F32, name=f"s_ps{i}", tag=f"s_bank{i}") for i in range(2)]
-        for t in range(PACK):
-            cols = slice(t * P, (t + 1) * P)
-            nc.tensor.matmul_mx(
-                s_ps[t // 2][:, t % 2, :], lhsT=u_codes[:, cols].bitcast(FP8X4), lhsT_scale=u_scales[:, cols],
-                rhs=q_codes[:].bitcast(FP8X4), rhs_scale=q_scales[:], start=True, stop=True)
-        for t in range(PACK):
-            nc.scalar.activation(sig[:, t, :], s_ps[t // 2][:, t % 2, :], ACT.Sigmoid, bias=bias[:, t:t + 1])
+        sig = sb([P, 2, PACK, P], F32, "sig", "v_win0")
+        for h in range(2):
+            rows = slice(h * P, (h + 1) * P)
+            for half, (u_codes, u_scales) in enumerate(u_halves):
+                s_ps = psum.tile([P, 2, P], F32, name=f"s_ps{h}{half}")
+                for tt in range(2):
+                    cols = slice(tt * P, (tt + 1) * P)
+                    nc.tensor.matmul_mx(
+                        s_ps[:, tt, :], lhsT=u_codes[:, cols].bitcast(FP8X4), lhsT_scale=u_scales[:, cols],
+                        rhs=q_codes[:, rows].bitcast(FP8X4), rhs_scale=q_scales[:, rows], start=True, stop=True)
+                for tt in range(2):
+                    t = 2 * half + tt
+                    nc.scalar.activation(sig[:, h, t, :], s_ps[:, tt, :], ACT.Sigmoid, bias=bias[:, t:t + 1])
 
-        def gather_values(b, dest):
-            v_g = sb([P, PACK, P], BF16, f"v_g{b}", slot=("w_win0", "u_bf", "bias", "sig")[b])
-            nc.vector.tensor_copy(v_g[:].rearrange("p t m -> p m t"), v_win[b][:].indirect(tok[:]))
-            v_ps = psum.tile([P, PACK, P], BF16, name=f"v_ps{b}", tag=f"v_bank{b % 2}")
+        def turn_values(b, v_g):
+            v_ps = psum.tile([P, PACK, P], BF16, name=f"v_ps{b}", tag=f"v_bank{(0, 1, 2, 1)[b]}")
             for t in range(PACK):
                 nc.tensor.transpose(v_ps[:, t, :], v_g[:, t, :], ident_b[:])
             return v_ps
 
+        def gather_values(b, buffer_of=None):
+            v_g = sb([P, PACK, P], BF16, f"v_g{b}", buffer_of)
+            nc.vector.tensor_copy(v_g[:].rearrange("p t m -> p m t"), v_win[b][:].indirect(tok[:]))
+            return turn_values(b, v_g)
+
         def interleave_values(dest, v_ps):
             nc.scalar.copy(dest, v_ps[:].rearrange("p t e -> p e t"))
 
-        def quantize(name, source, slot):
-            width = source.shape[1]
-            codes = sb([P, width], U32, f"{name}_codes", slot=slot)
-            scales = sb([P, width], U8, f"{name}_scales")
-            nc.vector.quantize_mx(codes[:].bitcast(FP8X4), scales[:], source.rearrange("p c t -> p (c t)"))
-            return codes, scales
+        v_ps1 = gather_values(1, "kw1")
+        v_g0 = sb([P, PACK, P], BF16, "v_g0", "bias")
+        nc.scalar.activation(v_g0[:].rearrange("p t m -> p m t"), v0_win[:].indirect(tok[:]), ACT.Copy)
+        v_ps0 = turn_values(0, v_g0)
 
-        v_ps0 = gather_values(0, None)
-        v_ps1 = gather_values(1, None)
-        yv_bf = sb([P, NQ + 2 * P, PACK], BF16, "yv_bf", slot="v_win1")
-        interleave_values(yv_bf[:, NQ:NQ + P, :], v_ps0)
+        yv_bf = sb([P, NQ + 2 * P, PACK], BF16, "yv_bf", "v_win1")
+        for h in range(2):
+            nc.vector.tensor_tensor(
+                yv_bf[:, h * P:(h + 1) * P, :], sig[:, h].rearrange("p t r -> p r t"),
+                us_sb[:].unsqueeze(1).to_broadcast([P, P, PACK]), ALU.mult)
         interleave_values(yv_bf[:, NQ + P:, :], v_ps1)
-        nc.vector.tensor_tensor(
-            yv_bf[:, :NQ, :], sig[:].rearrange("p t q -> p q t"),
-            us_sb[:].unsqueeze(1).to_broadcast([P, NQ, PACK]), ALU.mult)
-        v_ps2 = gather_values(2, None)
+        interleave_values(yv_bf[:, NQ:NQ + P, :], v_ps0)
         v2_bf = sb([P, P, PACK], BF16, "v2_bf")
-        interleave_values(v2_bf[:], v_ps2)
-        yv_codes, yv_scales = quantize("yv", yv_bf[:], "v_win2")
-        v_ps3 = gather_values(3, None)
+        interleave_values(v2_bf[:], gather_values(2))
         v3_bf = sb([P, P, PACK], BF16, "v3_bf")
-        interleave_values(v3_bf[:], v_ps3)
-        v2_codes, v2_scales = quantize("v2", v2_bf[:], "v_win3")
-        v3_codes, v3_scales = quantize("v3", v3_bf[:], None)
+        interleave_values(v3_bf[:], gather_values(3))
+
+        yv_codes, yv_scales = quantize("yv", yv_bf[:], "v_win3")
+        v2_codes, v2_scales = quantize("v2", v2_bf[:], "v_win1")
+        v3_codes, v3_scales = quantize("v3", v3_bf[:])
 
         out_rows = out[0].rearrange("(h p) e -> p h e", p=P)
 
-        def product(bank, h, codes, scales):
-            rows = slice(h * P, (h + 1) * P)
-            nc.tensor.matmul_mx(
-                bank, lhsT=yv_codes[:, rows].bitcast(FP8X4), lhsT_scale=yv_scales[:, rows],
-                rhs=codes.bitcast(FP8X4), rhs_scale=scales, start=True, stop=True)
+        def product(name, bank, codes, scales, e0, copy):
+            width = codes.shape[1]
+            o_ps = psum.tile([P, 2, width], F32, name=f"{name}_ps", tag=bank)
+            o_sb = sb([P, 2, width], F32, f"{name}_sb")
+            for h in range(2):
+                rows = slice(h * P, (h + 1) * P)
+                nc.tensor.matmul_mx(
+                    o_ps[:, h, :], lhsT=yv_codes[:, rows].bitcast(FP8X4), lhsT_scale=yv_scales[:, rows],
+                    rhs=codes.bitcast(FP8X4), rhs_scale=scales, start=True, stop=True)
+            copy(o_sb[:], o_ps[:])
+            nc.sync.dma_start(out_rows[:, :, e0:e0 + width], o_sb[:])
 
-        o_ps0 = psum.tile([P, 2, 2 * P], F32, name="o_ps0", tag="s_bank0")
-        o_sb0 = sb([P, 2, 2 * P], F32, "o_sb0")
-        for h in range(2):
-            product(o_ps0[:, h, :], h, yv_codes[:, NQ:], yv_scales[:, NQ:])
-        nc.scalar.copy(o_sb0[:], o_ps0[:])
-        nc.sync.dma_start(out_rows[:, :, :2 * P], o_sb0[:])
-
-        o_ps1 = psum.tile([P, 2, P], F32, name="o_ps1", tag="s_bank1")
-        o_sb1 = sb([P, 2, P], F32, "o_sb1")
-        for h in range(2):
-            product(o_ps1[:, h, :], h, v2_codes[:], v2_scales[:])
-        nc.vector.tensor_copy(o_sb1[:], o_ps1[:])
-        nc.sync.dma_start(out_rows[:, :, 2 * P:3 * P], o_sb1[:])
-
-        o_last = sb([P, 2, P], F32, "o_last")
-        last_ps = [psum.tile([P, P], F32, name=f"last_ps{h}") for h in range(2)]
-        for h in range(2):
-            product(last_ps[h][:], h, v3_codes[:], v3_scales[:])
-        nc.scalar.copy(o_last[:, 0, :], last_ps[0][:])
-        nc.vector.tensor_copy(o_last[:, 1, :], last_ps[1][:])
-        nc.sync.dma_start(out_rows[:, :, 3 * P:DV], o_last[:])
+        product("o01", "s_ps00", yv_codes[:, NQ:], yv_scales[:, NQ:], 0, nc.scalar.copy)
+        product("o2", "s_ps01", v2_codes[:], v2_scales[:], 2 * P, nc.vector.tensor_copy)
+        product("o3", "kb_ps", v3_codes[:], v3_scales[:], 3 * P, nc.vector.tensor_copy)

@@ -20,11 +20,10 @@ POSITIONS = 1024
 D = 512
 NQ = 256
 DV = 512
-
-FIRST_PLANE_CUTS = (0, 128, 256, 512, 1024, 2048)
+RUN = 4
 
 FLOPS = 2 * N * NQ * D + 2 * N * NQ * DV
-BYTES = 4 * (D * NQ + D * T + 2 * D * POSITIONS + DV * T + T + N + NQ * DV) + 2 * 2 * P * (N // 16)
+BYTES = 4 * (D * NQ + D * T + D * POSITIONS + DV * T + T + N + NQ * DV) + 2 * 2 * P * (N // 16)
 
 
 def tile_attend_at_ropesig_f_topk_kernel(tc, qT, kT, cT, wT, vT, kb, us, offs, offs2, out):
@@ -36,12 +35,8 @@ def tile_attend_at_ropesig_f_topk_kernel(tc, qT, kT, cT, wT, vT, kb, us, offs, o
         def sb(shape, dtype, name, buffer_of=None):
             return keep.tile(shape, dtype, name=name, tag=buffer_of or name, align_bytes=64)
 
-        def quantize(name, source, buffer_of=None):
-            width = source.shape[1]
-            codes = sb([P, width], U32, f"{name}_codes", buffer_of)
-            scales = sb([P, width], U8, f"{name}_scales")
-            nc.vector.quantize_mx(codes[:].bitcast(FP8X4), scales[:], source.rearrange("p c j -> p (c j)"))
-            return codes, scales
+        def quantize(codes, scales, source):
+            nc.vector.quantize_mx(codes.bitcast(FP8X4), scales, source.rearrange("p c j -> p (c j)"))
 
         tok = sb([P, N // 16], U16, "tok")
         pos = sb([P, N // 16], U16, "pos")
@@ -49,155 +44,165 @@ def tile_attend_at_ropesig_f_topk_kernel(tc, qT, kT, cT, wT, vT, kb, us, offs, o
         kb_win = sb([P, T], F32, "kb_win")
         q_raw = sb([P, PACK, NQ], F32, "q_raw")
         k_win = [sb([P, T], F32, f"k_win{j}") for j in range(PACK)]
-        c_win = [sb([P, POSITIONS], F32, f"c_win{j}") for j in range(PACK)]
-        w_win = [sb([P, POSITIONS], F32, f"w_win{j}") for j in range(PACK)]
+        c_win = [sb([P, POSITIONS], F32, f"c_win{a}") for a in range(2)]
+        w_win = [sb([P, POSITIONS], F32, f"w_win{a}") for a in range(2)]
         v_win = [sb([P, T], F32, f"v_win{b}") for b in range(DV // P)]
         k_rows = kT.rearrange("(p j) n -> p j n", j=PACK)
         c_rows = cT.rearrange("(p j) n -> p j n", j=PACK)
         w_rows = wT.rearrange("(p j) n -> p j n", j=PACK)
         token_halves = (slice(0, T // 2), slice(T // 2, T))
+        position_halves = (slice(0, POSITIONS // 2), slice(POSITIONS // 2, POSITIONS))
 
         nc.vector.memset(kb_win[:, token_halves[0]], 0.0)
         nc.gpsimd.memset(kb_win[:, token_halves[1]], 0.0)
-        for lo, hi in zip(FIRST_PLANE_CUTS, FIRST_PLANE_CUTS[1:]):
-            nc.sync.dma_start(k_win[0][:, lo:hi], k_rows[:, 0, lo:hi])
-        nc.sync.dma_start(tok[:], offs)
+        for cols in position_halves:
+            nc.sync.dma_start(c_win[0][:, cols], c_rows[:, 0, cols])
         nc.sync.dma_start(pos[:], offs2)
+        nc.sync.dma_start(tok[:], offs)
+        for cols in position_halves:
+            nc.sync.dma_start(w_win[0][:, cols], w_rows[:, 0, cols])
         nc.sync.dma_start(us_sb[:], us[0].rearrange("(p t) o -> p (t o)", t=PACK))
+        nc.sync.dma_start(k_win[0][:, :T // 4], k_rows[:, 0, :T // 4])
         nc.sync.dma_start(kb_win[0:1, :], kb[0:1, :])
-        for ev in (0, 2):
-            od = ev + 1
-            if ev > 0:
-                nc.sync.dma_start(k_win[ev][:], k_rows[:, ev, :])
-            nc.sync.dma_start(k_win[od][:], k_rows[:, od, :])
-            nc.sync.dma_start(c_win[ev][:], c_rows[:, ev, :])
-            nc.sync.dma_start(w_win[od][:], w_rows[:, od, :])
-            nc.sync.dma_start(c_win[od][:], c_rows[:, od, :])
-            nc.sync.dma_start(w_win[ev][:], w_rows[:, ev, :])
-        nc.sync.dma_start(v_win[0][:, token_halves[0]], vT[:P, token_halves[0]])
+        nc.sync.dma_start(k_win[0][:, T // 4:], k_rows[:, 0, T // 4:])
+        nc.sync.dma_start(k_win[1][:], k_rows[:, 1, :])
+        nc.sync.dma_start(c_win[1][:], c_rows[:, 2, :])
+        nc.sync.dma_start(w_win[1][:], w_rows[:, 2, :])
+        nc.sync.dma_start(k_win[2][:], k_rows[:, 2, :])
         nc.sync.dma_start(q_raw[:], qT[0].rearrange("(p j) q -> p j q", j=PACK))
-        nc.sync.dma_start(v_win[0][:, token_halves[1]], vT[:P, token_halves[1]])
+        nc.sync.dma_start(k_win[3][:], k_rows[:, 3, :])
+        for tokens in token_halves:
+            nc.sync.dma_start(v_win[0][:, tokens], vT[:P, tokens])
         for b in range(1, DV // P):
             nc.sync.dma_start(v_win[b][:], vT[b * P:(b + 1) * P, :])
 
-        ident_f = sb([P, P], F32, "ident_f")
-        ident_b = sb([P, P], BF16, "ident_b")
-        make_identity(nc, ident_f[:])
-        make_identity(nc, ident_b[:])
+        ident = sb([P, P], F32, "ident")
+        make_identity(nc, ident[:])
+        warm = sb([P, 1], F32, "warm")
+        nc.scalar.activation(warm[:], ident[:, 0:1], ACT.Sigmoid)
 
+        def gather(dest, window, offsets):
+            nc.vector.tensor_copy(dest, window[:].indirect(offsets[:]))
+
+        rot = [sb([P, 3, N], F32, f"rot{a}") for a in range(2)]
+
+        def gather_w(a):
+            gather(rot[a][:, 2, :], w_win[a], pos)
+            nc.scalar.activation(rot[a][:, 0, :], rot[a][:, 2, :], ACT.Copy, scale=-1.0)
+
+        def twice(x):
+            return x.unsqueeze(1).to_broadcast([P, 2, x.shape[1]])
+
+        def add_pair(dest, x, y):
+            nc.vector.tensor_tensor(
+                dest.rearrange("p (s i) j -> p s j i", i=RUN), x.rearrange("p j (s i) -> p s j i", i=RUN),
+                y.rearrange("p j (s i) -> p s j i", i=RUN), ALU.add)
+
+        gather(rot[0][:, 1, :], c_win[0], pos)
+        gather_w(0)
         bias = sb([P, PACK], F32, "bias")
+        kb_g = sb([P, N], F32, "kb_g")
+        gather(kb_g[:], kb_win, tok)
+        kb_ps = psum.tile([P, PACK, P], F32, name="kb_ps")
+        kb_by_t = kb_g[:].rearrange("p (m t) -> p t m", t=PACK)
+        for t in range(PACK):
+            nc.tensor.transpose(kb_ps[:, t, :], kb_by_t[:, t, :], ident[:])
+        nc.scalar.copy(bias[:], kb_ps[:, :, 0])
 
-        def gather_bias():
-            kb_g = sb([P, N], F32, "kb_g")
-            nc.vector.tensor_copy(kb_g[:], kb_win[:].indirect(tok[:]))
-            kb_ps = psum.tile([P, PACK, P], F32, name="kb_ps")
-            kb_by_t = kb_g[:].rearrange("p (m t) -> p t m", t=PACK)
-            for t in range(PACK):
-                nc.tensor.transpose(kb_ps[:, t, :], kb_by_t[:, t, :], ident_f[:])
-            nc.scalar.copy(bias[:], kb_ps[:, :, 0])
+        u_pairs = sb([P, 2, N, 2], BF16, "u_pairs", "w_win1")
+        k_g0 = sb([P, N], F32, "k_g0", "kb_win")
+        gather(k_g0[:], k_win[0], tok)
+        x0 = sb([P, 2, N], F32, "x0")
+        nc.vector.tensor_tensor(x0[:], twice(k_g0[:]), rot[0][:, 1:3, :], ALU.mult)
+        k_g1 = sb([P, N], F32, "k_g1")
+        gather(k_g1[:], k_win[1], tok)
+        gather(rot[1][:, 1, :], c_win[1], pos)
+        y0 = sb([P, 2, N], F32, "y0", "c_win1")
+        nc.vector.tensor_tensor(y0[:], twice(k_g1[:]), rot[0][:, 0:2, :], ALU.mult)
+        gather_w(1)
+        add_pair(u_pairs[:, 0], x0[:], y0[:])
 
-        u_bf = sb([P, PACK, P, PACK], BF16, "u_bf")
-        for pair in range(2):
-            ev, od = 2 * pair, 2 * pair + 1
-            k_ev = sb([P, N], F32, f"k_ev{pair}", (None, "k_neg0")[pair])
-            k_neg = sb([P, N], F32, f"k_neg{pair}")
-            nc.vector.tensor_copy(k_ev[:], k_win[ev][:].indirect(tok[:]))
-            if pair == 0:
-                gather_bias()
-            k_od = sb([P, N], F32, f"k_od{pair}", (None, "w_win0")[pair])
-            nc.vector.tensor_copy(k_od[:], k_win[od][:].indirect(tok[:]))
-            nc.scalar.activation(k_neg[:], k_od[:], ACT.Copy, scale=-1.0)
-            kc = sb([P, 2, N], F32, f"kc{pair}")
-            kw = sb([P, 2, N], F32, f"kw{pair}")
-            nc.vector.tensor_tensor(kc[:, 0, :], c_win[ev][:].indirect(pos[:]), k_ev[:], ALU.mult)
-            nc.vector.tensor_tensor(kw[:, 1, :], w_win[od][:].indirect(pos[:]), k_ev[:], ALU.mult)
-            nc.vector.tensor_tensor(kc[:, 1, :], c_win[od][:].indirect(pos[:]), k_od[:], ALU.mult)
-            nc.vector.tensor_tensor(kw[:, 0, :], w_win[ev][:].indirect(pos[:]), k_neg[:], ALU.mult)
-            u_pair = u_bf[:, :, :, ev:ev + 2].rearrange("p t m j -> p m t j")
-            if pair == 0:
-                u_first = sb([P, 2, N], BF16, "u_first")
-                nc.vector.tensor_tensor(u_first[:], kc[:], kw[:], ALU.add)
-                nc.scalar.copy(u_pair, u_first[:].rearrange("p j (m t) -> p m t j", t=PACK))
-            else:
-                nc.vector.tensor_tensor(
-                    u_pair, kc[:].rearrange("p j (m t) -> p m t j", t=PACK),
-                    kw[:].rearrange("p j (m t) -> p m t j", t=PACK), ALU.add)
+        k_g2 = sb([P, N], F32, "k_g2")
+        gather(k_g2[:], k_win[2], tok)
+        x1 = sb([P, 2, N], F32, "x1")
+        nc.vector.tensor_tensor(x1[:], twice(k_g2[:]), rot[1][:, 1:3, :], ALU.mult)
+        k_g3 = sb([P, N], F32, "k_g3")
+        gather(k_g3[:], k_win[3], tok)
 
-        q_bf = sb([P, NQ, PACK], BF16, "q_bf", "w_win0")
+        q_bf = sb([P, NQ, PACK], BF16, "q_bf")
         nc.scalar.copy(q_bf[:], q_raw[:].rearrange("p j q -> p q j"))
-        q_codes, q_scales = quantize("q", q_bf[:], "kc1")
-        u_halves = [
-            quantize(f"u{half}", u_bf[:, 2 * half:2 * half + 2].rearrange("p t m j -> p (t m) j"))
-            for half in range(2)
-        ]
+        q_codes = sb([P, NQ], U32, "q_codes", "k_win3")
+        q_scales = sb([P, NQ], U8, "q_scales")
+        quantize(q_codes[:], q_scales[:], q_bf[:])
+
+        y1 = sb([P, 2, N], F32, "y1", "q_bf")
+        slot_halves = (slice(0, N // 2), slice(N // 2, N))
+        for s in slot_halves:
+            nc.vector.tensor_tensor(y1[:, :, s], twice(k_g3[:, s]), rot[1][:, 0:2, s], ALU.mult)
+        for s in slot_halves:
+            add_pair(u_pairs[:, 1, s, :], x1[:, :, s], y1[:, :, s])
+
+        u_bf = [sb([P, 2, P, PACK], BF16, f"u_bf{half}") for half in range(2)]
+        pair_words = u_pairs[:].rearrange("p a s j -> p a (s j)").bitcast(F32).rearrange("p a (m t) -> p m t a", t=PACK)
+        for half in range(2):
+            nc.vector.tensor_copy(
+                u_bf[half][:].rearrange("p t m j -> p (t m j)").bitcast(F32).rearrange("p (t m a) -> p m t a", t=2, a=2),
+                pair_words[:, :, 2 * half:2 * half + 2, :])
+        u_codes = [sb([P, 2 * P], U32, f"u_codes{half}") for half in range(2)]
+        u_scales = [sb([P, 2 * P], U8, f"u_scales{half}") for half in range(2)]
+        for half in range(2):
+            quantize(u_codes[half][:], u_scales[half][:], u_bf[half][:].rearrange("p t m j -> p (t m) j"))
+
+        v_bf = sb([P, DV, PACK], BF16, "v_bf")
+
+        def turn_values(b, v_g):
+            v_ps = psum.tile([P, 2, P], F32, name=f"v_ps{b}", tag=f"v_bank{b % 3}")
+            words = v_g[:].bitcast(F32).rearrange("p (m u) -> p u m", u=2)
+            for u in range(2):
+                nc.tensor.transpose(v_ps[:, u, :], words[:, u, :], ident[:])
+            dest = v_bf[:, b * P:(b + 1) * P, :].rearrange("p e t -> p (e t)").bitcast(F32)
+            nc.scalar.copy(dest.rearrange("p (e u) -> p e u", u=2), v_ps[:].rearrange("p u e -> p e u"))
 
         v0_win = sb([P, T], BF16, "v0_win")
         for tokens in token_halves:
             nc.scalar.activation(v0_win[:, tokens], v_win[0][:, tokens], ACT.Copy)
+        v_g0 = sb([P, N], BF16, "v_g0")
+        nc.scalar.activation(v_g0[:], v0_win[:].indirect(tok[:]), ACT.Copy)
+        turn_values(0, v_g0)
 
-        sig = sb([P, 2, PACK, P], F32, "sig", "v_win0")
-        for h in range(2):
+        sig = sb([P, PACK, NQ], F32, "sig")
+        for t in range(PACK):
+            half, cols = t // 2, slice(t % 2 * P, (t % 2 + 1) * P)
+            s_ps = psum.tile([P, NQ], F32, name=f"s_ps{t}")
+            nc.tensor.matmul_mx(
+                s_ps[:], lhsT=u_codes[half][:, cols].bitcast(FP8X4), lhsT_scale=u_scales[half][:, cols],
+                rhs=q_codes[:].bitcast(FP8X4), rhs_scale=q_scales[:], start=True, stop=True)
+            nc.scalar.activation(sig[:, t, :], s_ps[:], ACT.Sigmoid, bias=bias[:, t:t + 1])
+
+        for b in range(1, DV // P):
+            v_g = sb([P, N], BF16, f"v_g{b}")
+            gather(v_g[:], v_win[b], tok)
+            turn_values(b, v_g)
+
+        y_bf = sb([P, NQ, PACK], BF16, "y_bf", "v_win3")
+        nc.vector.tensor_tensor(
+            y_bf[:].rearrange("p (r i) t -> p r t i", i=RUN), sig[:].rearrange("p t (r i) -> p r t i", i=RUN),
+            us_sb[:].unsqueeze(1).unsqueeze(3).to_broadcast([P, NQ // RUN, PACK, RUN]), ALU.mult)
+        v_codes = sb([P, DV], U32, "v_codes", "sig")
+        v_scales = sb([P, DV], U8, "v_scales")
+        quantize(v_codes[:], v_scales[:], v_bf[:])
+        y_codes = sb([P, NQ], U32, "y_codes")
+        y_scales = sb([P, NQ], U8, "y_scales")
+        quantize(y_codes[:], y_scales[:], y_bf[:])
+
+        for piece in range(4):
+            h, e = piece % 2, piece // 2
             rows = slice(h * P, (h + 1) * P)
-            for half, (u_codes, u_scales) in enumerate(u_halves):
-                s_ps = psum.tile([P, 2, P], F32, name=f"s_ps{h}{half}")
-                for tt in range(2):
-                    cols = slice(tt * P, (tt + 1) * P)
-                    nc.tensor.matmul_mx(
-                        s_ps[:, tt, :], lhsT=u_codes[:, cols].bitcast(FP8X4), lhsT_scale=u_scales[:, cols],
-                        rhs=q_codes[:, rows].bitcast(FP8X4), rhs_scale=q_scales[:, rows], start=True, stop=True)
-                for tt in range(2):
-                    t = 2 * half + tt
-                    nc.scalar.activation(sig[:, h, t, :], s_ps[:, tt, :], ACT.Sigmoid, bias=bias[:, t:t + 1])
-
-        def turn_values(b, v_g):
-            v_ps = psum.tile([P, PACK, P], BF16, name=f"v_ps{b}", tag=f"v_bank{(0, 1, 2, 1)[b]}")
-            for t in range(PACK):
-                nc.tensor.transpose(v_ps[:, t, :], v_g[:, t, :], ident_b[:])
-            return v_ps
-
-        def gather_values(b, buffer_of=None):
-            v_g = sb([P, PACK, P], BF16, f"v_g{b}", buffer_of)
-            nc.vector.tensor_copy(v_g[:].rearrange("p t m -> p m t"), v_win[b][:].indirect(tok[:]))
-            return turn_values(b, v_g)
-
-        def interleave_values(dest, v_ps):
-            nc.scalar.copy(dest, v_ps[:].rearrange("p t e -> p e t"))
-
-        v_ps1 = gather_values(1, "kw1")
-        v_g0 = sb([P, PACK, P], BF16, "v_g0", "bias")
-        nc.scalar.activation(v_g0[:].rearrange("p t m -> p m t"), v0_win[:].indirect(tok[:]), ACT.Copy)
-        v_ps0 = turn_values(0, v_g0)
-
-        yv_bf = sb([P, NQ + 2 * P, PACK], BF16, "yv_bf", "v_win1")
-        for h in range(2):
-            nc.vector.tensor_tensor(
-                yv_bf[:, h * P:(h + 1) * P, :], sig[:, h].rearrange("p t r -> p r t"),
-                us_sb[:].unsqueeze(1).to_broadcast([P, P, PACK]), ALU.mult)
-        interleave_values(yv_bf[:, NQ + P:, :], v_ps1)
-        interleave_values(yv_bf[:, NQ:NQ + P, :], v_ps0)
-        v2_bf = sb([P, P, PACK], BF16, "v2_bf")
-        interleave_values(v2_bf[:], gather_values(2))
-        v3_bf = sb([P, P, PACK], BF16, "v3_bf")
-        interleave_values(v3_bf[:], gather_values(3))
-
-        yv_codes, yv_scales = quantize("yv", yv_bf[:], "v_win3")
-        v2_codes, v2_scales = quantize("v2", v2_bf[:], "v_win1")
-        v3_codes, v3_scales = quantize("v3", v3_bf[:])
-
-        out_rows = out[0].rearrange("(h p) e -> p h e", p=P)
-
-        def product(name, bank, codes, scales, e0, copy):
-            width = codes.shape[1]
-            o_ps = psum.tile([P, 2, width], F32, name=f"{name}_ps", tag=bank)
-            o_sb = sb([P, 2, width], F32, f"{name}_sb")
-            for h in range(2):
-                rows = slice(h * P, (h + 1) * P)
-                nc.tensor.matmul_mx(
-                    o_ps[:, h, :], lhsT=yv_codes[:, rows].bitcast(FP8X4), lhsT_scale=yv_scales[:, rows],
-                    rhs=codes.bitcast(FP8X4), rhs_scale=scales, start=True, stop=True)
-            copy(o_sb[:], o_ps[:])
-            nc.sync.dma_start(out_rows[:, :, e0:e0 + width], o_sb[:])
-
-        product("o01", "s_ps00", yv_codes[:, NQ:], yv_scales[:, NQ:], 0, nc.scalar.copy)
-        product("o2", "s_ps01", v2_codes[:], v2_scales[:], 2 * P, nc.vector.tensor_copy)
-        product("o3", "kb_ps", v3_codes[:], v3_scales[:], 3 * P, nc.vector.tensor_copy)
+            cols = slice(e * DV // 2, (e + 1) * DV // 2)
+            o_ps = psum.tile([P, DV // 2], F32, name=f"o_ps{piece}", tag=f"s_ps{piece}")
+            o_sb = sb([P, DV // 2], F32, f"o_sb{piece}")
+            nc.tensor.matmul_mx(
+                o_ps[:], lhsT=y_codes[:, rows].bitcast(FP8X4), lhsT_scale=y_scales[:, rows],
+                rhs=v_codes[:, cols].bitcast(FP8X4), rhs_scale=v_scales[:, cols], start=True, stop=True)
+            (nc.scalar.copy, nc.vector.tensor_copy)[h](o_sb[:], o_ps[:])
+            nc.sync.dma_start(out[0, rows, cols], o_sb[:])

@@ -55,9 +55,9 @@ def tile_attend_at_ropesig_f_topk_kernel(tc, qT, kT, cT, wT, vT, kb, us, offs, o
 
         nc.vector.memset(kb_win[:, token_halves[0]], 0.0)
         nc.gpsimd.memset(kb_win[:, token_halves[1]], 0.0)
+        nc.sync.dma_start(pos[:], offs2)
         for cols in position_halves:
             nc.sync.dma_start(c_win[0][:, cols], c_rows[:, 0, cols])
-        nc.sync.dma_start(pos[:], offs2)
         nc.sync.dma_start(tok[:], offs)
         for cols in position_halves:
             nc.sync.dma_start(w_win[0][:, cols], w_rows[:, 0, cols])
@@ -65,8 +65,8 @@ def tile_attend_at_ropesig_f_topk_kernel(tc, qT, kT, cT, wT, vT, kb, us, offs, o
         nc.sync.dma_start(k_win[0][:, :T // 4], k_rows[:, 0, :T // 4])
         nc.sync.dma_start(kb_win[0:1, :], kb[0:1, :])
         nc.sync.dma_start(k_win[0][:, T // 4:], k_rows[:, 0, T // 4:])
-        nc.sync.dma_start(k_win[1][:], k_rows[:, 1, :])
         nc.sync.dma_start(c_win[1][:], c_rows[:, 2, :])
+        nc.sync.dma_start(k_win[1][:], k_rows[:, 1, :])
         nc.sync.dma_start(w_win[1][:], w_rows[:, 2, :])
         nc.sync.dma_start(k_win[2][:], k_rows[:, 2, :])
         nc.sync.dma_start(q_raw[:], qT[0].rearrange("(p j) q -> p j q", j=PACK))
@@ -93,11 +93,6 @@ def tile_attend_at_ropesig_f_topk_kernel(tc, qT, kT, cT, wT, vT, kb, us, offs, o
         def twice(x):
             return x.unsqueeze(1).to_broadcast([P, 2, x.shape[1]])
 
-        def add_pair(dest, x, y):
-            nc.vector.tensor_tensor(
-                dest.rearrange("p (s i) j -> p s j i", i=RUN), x.rearrange("p j (s i) -> p s j i", i=RUN),
-                y.rearrange("p j (s i) -> p s j i", i=RUN), ALU.add)
-
         gather(rot[0][:, 1, :], c_win[0], pos)
         gather_w(0)
         bias = sb([P, PACK], F32, "bias")
@@ -109,45 +104,39 @@ def tile_attend_at_ropesig_f_topk_kernel(tc, qT, kT, cT, wT, vT, kb, us, offs, o
             nc.tensor.transpose(kb_ps[:, t, :], kb_by_t[:, t, :], ident[:])
         nc.scalar.copy(bias[:], kb_ps[:, :, 0])
 
-        u_pairs = sb([P, 2, N, 2], BF16, "u_pairs", "w_win1")
-        k_g0 = sb([P, N], F32, "k_g0", "kb_win")
-        gather(k_g0[:], k_win[0], tok)
-        x0 = sb([P, 2, N], F32, "x0")
-        nc.vector.tensor_tensor(x0[:], twice(k_g0[:]), rot[0][:, 1:3, :], ALU.mult)
-        k_g1 = sb([P, N], F32, "k_g1")
-        gather(k_g1[:], k_win[1], tok)
-        gather(rot[1][:, 1, :], c_win[1], pos)
-        y0 = sb([P, 2, N], F32, "y0", "c_win1")
-        nc.vector.tensor_tensor(y0[:], twice(k_g1[:]), rot[0][:, 0:2, :], ALU.mult)
-        gather_w(1)
-        add_pair(u_pairs[:, 0], x0[:], y0[:])
+        k_g = [sb([P, N], F32, f"k_g{j}", "kb_win" if j == 0 else None) for j in range(PACK)]
+        from_even = sb([P, PACK, N], F32, "from_even", "c_win1")
+        from_odd = sb([P, PACK, N], F32, "from_odd", "k_win2")
 
-        k_g2 = sb([P, N], F32, "k_g2")
-        gather(k_g2[:], k_win[2], tok)
-        x1 = sb([P, 2, N], F32, "x1")
-        nc.vector.tensor_tensor(x1[:], twice(k_g2[:]), rot[1][:, 1:3, :], ALU.mult)
-        k_g3 = sb([P, N], F32, "k_g3")
-        gather(k_g3[:], k_win[3], tok)
+        def products(j):
+            a, odd = divmod(j, 2)
+            dest = (from_even, from_odd)[odd]
+            nc.vector.tensor_tensor(dest[:, 2 * a:2 * a + 2, :], twice(k_g[j][:]), rot[a][:, 1 - odd:3 - odd, :], ALU.mult)
+
+        gather(k_g[0][:], k_win[0], tok)
+        gather(rot[1][:, 1, :], c_win[1], pos)
+        products(0)
+        gather(k_g[1][:], k_win[1], tok)
+        gather_w(1)
+        gather(k_g[2][:], k_win[2], tok)
+        products(1)
+        products(2)
+        gather(k_g[3][:], k_win[3], tok)
 
         q_bf = sb([P, NQ, PACK], BF16, "q_bf")
         nc.scalar.copy(q_bf[:], q_raw[:].rearrange("p j q -> p q j"))
         q_codes = sb([P, NQ], U32, "q_codes", "k_win3")
         q_scales = sb([P, NQ], U8, "q_scales")
         quantize(q_codes[:], q_scales[:], q_bf[:])
-
-        y1 = sb([P, 2, N], F32, "y1", "q_bf")
-        slot_halves = (slice(0, N // 2), slice(N // 2, N))
-        for s in slot_halves:
-            nc.vector.tensor_tensor(y1[:, :, s], twice(k_g3[:, s]), rot[1][:, 0:2, s], ALU.mult)
-        for s in slot_halves:
-            add_pair(u_pairs[:, 1, s, :], x1[:, :, s], y1[:, :, s])
+        products(3)
 
         u_bf = [sb([P, 2, P, PACK], BF16, f"u_bf{half}") for half in range(2)]
-        pair_words = u_pairs[:].rearrange("p a s j -> p a (s j)").bitcast(F32).rearrange("p a (m t) -> p m t a", t=PACK)
         for half in range(2):
-            nc.vector.tensor_copy(
-                u_bf[half][:].rearrange("p t m j -> p (t m j)").bitcast(F32).rearrange("p (t m a) -> p m t a", t=2, a=2),
-                pair_words[:, :, 2 * half:2 * half + 2, :])
+            ts = slice(2 * half, 2 * half + 2)
+            nc.vector.tensor_tensor(
+                u_bf[half][:].rearrange("p t m j -> p m j t"),
+                from_even[:].rearrange("p j (m t) -> p m j t", t=PACK)[:, :, :, ts],
+                from_odd[:].rearrange("p j (m t) -> p m j t", t=PACK)[:, :, :, ts], ALU.add)
         u_codes = [sb([P, 2 * P], U32, f"u_codes{half}") for half in range(2)]
         u_scales = [sb([P, 2 * P], U8, f"u_scales{half}") for half in range(2)]
         for half in range(2):
@@ -188,12 +177,13 @@ def tile_attend_at_ropesig_f_topk_kernel(tc, qT, kT, cT, wT, vT, kb, us, offs, o
         nc.vector.tensor_tensor(
             y_bf[:].rearrange("p (r i) t -> p r t i", i=RUN), sig[:].rearrange("p t (r i) -> p r t i", i=RUN),
             us_sb[:].unsqueeze(1).unsqueeze(3).to_broadcast([P, NQ // RUN, PACK, RUN]), ALU.mult)
-        v_codes = sb([P, DV], U32, "v_codes", "sig")
-        v_scales = sb([P, DV], U8, "v_scales")
-        quantize(v_codes[:], v_scales[:], v_bf[:])
+        v_codes = [sb([P, DV // 2], U32, f"v_codes{e}", ("sig", "v_win3")[e]) for e in range(2)]
+        v_scales = [sb([P, DV // 2], U8, f"v_scales{e}") for e in range(2)]
         y_codes = sb([P, NQ], U32, "y_codes")
         y_scales = sb([P, NQ], U8, "y_scales")
+        quantize(v_codes[0][:], v_scales[0][:], v_bf[:, :DV // 2, :])
         quantize(y_codes[:], y_scales[:], y_bf[:])
+        quantize(v_codes[1][:], v_scales[1][:], v_bf[:, DV // 2:, :])
 
         for piece in range(4):
             h, e = piece % 2, piece // 2
@@ -203,6 +193,6 @@ def tile_attend_at_ropesig_f_topk_kernel(tc, qT, kT, cT, wT, vT, kb, us, offs, o
             o_sb = sb([P, DV // 2], F32, f"o_sb{piece}")
             nc.tensor.matmul_mx(
                 o_ps[:], lhsT=y_codes[:, rows].bitcast(FP8X4), lhsT_scale=y_scales[:, rows],
-                rhs=v_codes[:, cols].bitcast(FP8X4), rhs_scale=v_scales[:, cols], start=True, stop=True)
+                rhs=v_codes[e][:].bitcast(FP8X4), rhs_scale=v_scales[e][:], start=True, stop=True)
             (nc.scalar.copy, nc.vector.tensor_copy)[h](o_sb[:], o_ps[:])
             nc.sync.dma_start(out[0, rows, cols], o_sb[:])

@@ -105,21 +105,21 @@ def tile_attend_at_ropesig_f_topk_kernel(tc, qT, kT, cT, wT, vT, kb, us, offs, o
         nc.scalar.copy(bias[:], kb_ps[:, :, 0])
 
         k_g = [sb([P, N], F32, f"k_g{j}", "kb_win" if j == 0 else None) for j in range(PACK)]
-        from_even = sb([P, PACK, N], F32, "from_even", "c_win1")
-        from_odd = sb([P, PACK, N], F32, "from_odd", "k_win2")
+        from_even = sb([P, PACK, N], F32, "from_even")
+        from_odd = sb([P, PACK, N], F32, "from_odd")
 
         def products(j):
             a, odd = divmod(j, 2)
             dest = (from_even, from_odd)[odd]
-            nc.vector.tensor_tensor(dest[:, 2 * a:2 * a + 2, :], twice(k_g[j][:]), rot[a][:, 1 - odd:3 - odd, :], ALU.mult)
+            (nc.gpsimd, nc.vector)[a].tensor_tensor(dest[:, 2 * a:2 * a + 2, :], twice(k_g[j][:]), rot[a][:, 1 - odd:3 - odd, :], ALU.mult)
 
         gather(k_g[0][:], k_win[0], tok)
-        gather(rot[1][:, 1, :], c_win[1], pos)
         products(0)
+        gather(rot[1][:, 1, :], c_win[1], pos)
         gather(k_g[1][:], k_win[1], tok)
+        products(1)
         gather_w(1)
         gather(k_g[2][:], k_win[2], tok)
-        products(1)
         products(2)
         gather(k_g[3][:], k_win[3], tok)
 

@@ -69,8 +69,8 @@ def tile_attend_at_ropesig_f_topk_kernel(tc, qT, kT, cT, wT, vT, kb, us, offs, o
         nc.sync.dma_start(k_win[1][:], k_rows[:, 1, :])
         nc.sync.dma_start(w_win[1][:], w_rows[:, 2, :])
         nc.sync.dma_start(k_win[2][:], k_rows[:, 2, :])
-        nc.sync.dma_start(q_raw[:], qT[0].rearrange("(p j) q -> p j q", j=PACK))
         nc.sync.dma_start(k_win[3][:], k_rows[:, 3, :])
+        nc.sync.dma_start(q_raw[:], qT[0].rearrange("(p j) q -> p j q", j=PACK))
         for tokens in token_halves:
             nc.sync.dma_start(v_win[0][:, tokens], vT[:P, tokens])
         for b in range(1, DV // P):
@@ -111,7 +111,7 @@ def tile_attend_at_ropesig_f_topk_kernel(tc, qT, kT, cT, wT, vT, kb, us, offs, o
         def products(j):
             a, odd = divmod(j, 2)
             dest = (from_even, from_odd)[odd]
-            (nc.gpsimd, nc.vector)[a].tensor_tensor(dest[:, 2 * a:2 * a + 2, :], twice(k_g[j][:]), rot[a][:, 1 - odd:3 - odd, :], ALU.mult)
+            (nc.vector if j == PACK - 1 else nc.gpsimd).tensor_tensor(dest[:, 2 * a:2 * a + 2, :], twice(k_g[j][:]), rot[a][:, 1 - odd:3 - odd, :], ALU.mult)
 
         gather(k_g[0][:], k_win[0], tok)
         products(0)
@@ -125,9 +125,6 @@ def tile_attend_at_ropesig_f_topk_kernel(tc, qT, kT, cT, wT, vT, kb, us, offs, o
 
         q_bf = sb([P, NQ, PACK], BF16, "q_bf")
         nc.scalar.copy(q_bf[:], q_raw[:].rearrange("p j q -> p q j"))
-        q_codes = sb([P, NQ], U32, "q_codes", "k_win3")
-        q_scales = sb([P, NQ], U8, "q_scales")
-        quantize(q_codes[:], q_scales[:], q_bf[:])
         products(3)
 
         u_bf = [sb([P, 2, P, PACK], BF16, f"u_bf{half}") for half in range(2)]
@@ -137,19 +134,23 @@ def tile_attend_at_ropesig_f_topk_kernel(tc, qT, kT, cT, wT, vT, kb, us, offs, o
                 u_bf[half][:].rearrange("p t m j -> p m j t"),
                 from_even[:].rearrange("p j (m t) -> p m j t", t=PACK)[:, :, :, ts],
                 from_odd[:].rearrange("p j (m t) -> p m j t", t=PACK)[:, :, :, ts], ALU.add)
+        q_codes = sb([P, NQ], U32, "q_codes", "from_odd")
+        q_scales = sb([P, NQ], U8, "q_scales")
+        quantize(q_codes[:], q_scales[:], q_bf[:])
         u_codes = [sb([P, 2 * P], U32, f"u_codes{half}") for half in range(2)]
         u_scales = [sb([P, 2 * P], U8, f"u_scales{half}") for half in range(2)]
         for half in range(2):
             quantize(u_codes[half][:], u_scales[half][:], u_bf[half][:].rearrange("p t m j -> p (t m) j"))
 
-        v_bf = sb([P, DV, PACK], BF16, "v_bf")
+        yv_bf = sb([P, NQ + 2 * P, PACK], BF16, "yv_bf", "v_win2")
+        v_bf = [yv_bf[:, NQ:NQ + P, :], yv_bf[:, NQ + P:, :], sb([P, P, PACK], BF16, "v2_bf")[:], sb([P, P, PACK], BF16, "v3_bf")[:]]
 
         def turn_values(b, v_g):
             v_ps = psum.tile([P, 2, P], F32, name=f"v_ps{b}", tag=f"v_bank{b % 3}")
             words = v_g[:].bitcast(F32).rearrange("p (m u) -> p u m", u=2)
             for u in range(2):
                 nc.tensor.transpose(v_ps[:, u, :], words[:, u, :], ident[:])
-            dest = v_bf[:, b * P:(b + 1) * P, :].rearrange("p e t -> p (e t)").bitcast(F32)
+            dest = v_bf[b].rearrange("p e t -> p (e t)").bitcast(F32)
             nc.scalar.copy(dest.rearrange("p (e u) -> p e u", u=2), v_ps[:].rearrange("p u e -> p e u"))
 
         v0_win = sb([P, T], BF16, "v0_win")
@@ -157,7 +158,6 @@ def tile_attend_at_ropesig_f_topk_kernel(tc, qT, kT, cT, wT, vT, kb, us, offs, o
             nc.scalar.activation(v0_win[:, tokens], v_win[0][:, tokens], ACT.Copy)
         v_g0 = sb([P, N], BF16, "v_g0")
         nc.scalar.activation(v_g0[:], v0_win[:].indirect(tok[:]), ACT.Copy)
-        turn_values(0, v_g0)
 
         sig = sb([P, PACK, NQ], F32, "sig")
         for t in range(PACK):
@@ -168,31 +168,45 @@ def tile_attend_at_ropesig_f_topk_kernel(tc, qT, kT, cT, wT, vT, kb, us, offs, o
                 rhs=q_codes[:].bitcast(FP8X4), rhs_scale=q_scales[:], start=True, stop=True)
             nc.scalar.activation(sig[:, t, :], s_ps[:], ACT.Sigmoid, bias=bias[:, t:t + 1])
 
-        for b in range(1, DV // P):
-            v_g = sb([P, N], BF16, f"v_g{b}")
+        def gather_values(b, buffer_of=None):
+            v_g = sb([P, N], BF16, f"v_g{b}", buffer_of)
             gather(v_g[:], v_win[b], tok)
-            turn_values(b, v_g)
+            return v_g
 
-        y_bf = sb([P, NQ, PACK], BF16, "y_bf", "v_win3")
+        def quantize_new(name, source, buffer_of=None):
+            codes = sb([P, source.shape[1]], U32, f"{name}_codes", buffer_of)
+            scales = sb([P, source.shape[1]], U8, f"{name}_scales")
+            quantize(codes[:], scales[:], source)
+            return codes, scales
+
+        v_g1 = gather_values(1)
+        v_g2 = gather_values(2)
+        turn_values(0, v_g0)
+        turn_values(1, v_g1)
+        turn_values(2, v_g2)
         nc.vector.tensor_tensor(
-            y_bf[:].rearrange("p (r i) t -> p r t i", i=RUN), sig[:].rearrange("p t (r i) -> p r t i", i=RUN),
+            yv_bf[:, :NQ, :].rearrange("p (r i) t -> p r t i", i=RUN), sig[:].rearrange("p t (r i) -> p r t i", i=RUN),
             us_sb[:].unsqueeze(1).unsqueeze(3).to_broadcast([P, NQ // RUN, PACK, RUN]), ALU.mult)
-        v_codes = [sb([P, DV // 2], U32, f"v_codes{e}", ("sig", "v_win3")[e]) for e in range(2)]
-        v_scales = [sb([P, DV // 2], U8, f"v_scales{e}") for e in range(2)]
-        y_codes = sb([P, NQ], U32, "y_codes")
-        y_scales = sb([P, NQ], U8, "y_scales")
-        quantize(v_codes[0][:], v_scales[0][:], v_bf[:, :DV // 2, :])
-        quantize(y_codes[:], y_scales[:], y_bf[:])
-        quantize(v_codes[1][:], v_scales[1][:], v_bf[:, DV // 2:, :])
+        turn_values(3, gather_values(3, "sig"))
+        yv_codes, yv_scales = quantize_new("yv", yv_bf[:], "v_win3")
+        v2_codes, v2_scales = quantize_new("v2", v_bf[2], "v_win2")
+        v3_codes, v3_scales = quantize_new("v3", v_bf[3])
 
-        for piece in range(4):
-            h, e = piece % 2, piece // 2
-            rows = slice(h * P, (h + 1) * P)
-            cols = slice(e * DV // 2, (e + 1) * DV // 2)
-            o_ps = psum.tile([P, DV // 2], F32, name=f"o_ps{piece}", tag=f"s_ps{piece}")
-            o_sb = sb([P, DV // 2], F32, f"o_sb{piece}")
-            nc.tensor.matmul_mx(
-                o_ps[:], lhsT=y_codes[:, rows].bitcast(FP8X4), lhsT_scale=y_scales[:, rows],
-                rhs=v_codes[e][:].bitcast(FP8X4), rhs_scale=v_scales[e][:], start=True, stop=True)
-            (nc.scalar.copy, nc.vector.tensor_copy)[h](o_sb[:], o_ps[:])
-            nc.sync.dma_start(out[0, rows, cols], o_sb[:])
+        out_rows = out[0].rearrange("(h p) e -> p h e", p=P)
+
+        def product(name, bank, codes, scales, e0, copy):
+            width = codes.shape[1]
+            cols = slice(e0, e0 + width)
+            o_ps = psum.tile([P, 2, width], F32, name=f"{name}_ps", tag=bank)
+            o_sb = sb([P, 2, width], F32, f"{name}_sb")
+            for h in range(2):
+                rows = slice(h * P, (h + 1) * P)
+                nc.tensor.matmul_mx(
+                    o_ps[:, h, :], lhsT=yv_codes[:, rows].bitcast(FP8X4), lhsT_scale=yv_scales[:, rows],
+                    rhs=codes.bitcast(FP8X4), rhs_scale=scales, start=True, stop=True)
+            copy(o_sb[:], o_ps[:])
+            nc.sync.dma_start(out_rows[:, :, cols], o_sb[:])
+
+        product("o01", "s_ps0", yv_codes[:, NQ:], yv_scales[:, NQ:], 0, nc.scalar.copy)
+        product("o2", "s_ps1", v2_codes[:], v2_scales[:], 2 * P, nc.vector.tensor_copy)
+        product("o3", "s_ps2", v3_codes[:], v3_scales[:], 3 * P, nc.vector.tensor_copy)

@@ -51,25 +51,22 @@ def tile_attend_at_ropesig_f_topk_kernel(tc, qT, kT, cT, wT, vT, kb, us, offs, o
         c_rows = cT.rearrange("(p j) n -> p j n", j=PACK)
         w_rows = wT.rearrange("(p j) n -> p j n", j=PACK)
         token_halves = (slice(0, T // 2), slice(T // 2, T))
-        position_halves = (slice(0, POSITIONS // 2), slice(POSITIONS // 2, POSITIONS))
 
         nc.vector.memset(kb_win[:, token_halves[0]], 0.0)
         nc.gpsimd.memset(kb_win[:, token_halves[1]], 0.0)
         nc.sync.dma_start(pos[:], offs2)
-        for cols in position_halves:
-            nc.sync.dma_start(c_win[0][:, cols], c_rows[:, 0, cols])
+        nc.sync.dma_start(c_win[0][:], c_rows[:, 0, :])
+        nc.sync.dma_start(w_win[0][:], w_rows[:, 0, :])
         nc.sync.dma_start(tok[:], offs)
-        for cols in position_halves:
-            nc.sync.dma_start(w_win[0][:, cols], w_rows[:, 0, cols])
         nc.sync.dma_start(us_sb[:], us[0].rearrange("(p t) o -> p (t o)", t=PACK))
-        nc.sync.dma_start(k_win[0][:, :T // 4], k_rows[:, 0, :T // 4])
-        nc.sync.dma_start(kb_win[0:1, :], kb[0:1, :])
-        nc.sync.dma_start(k_win[0][:, T // 4:], k_rows[:, 0, T // 4:])
+        for tokens in token_halves:
+            nc.sync.dma_start(k_win[0][:, tokens], k_rows[:, 0, tokens])
         nc.sync.dma_start(c_win[1][:], c_rows[:, 2, :])
+        nc.sync.dma_start(kb_win[0:1, :], kb[0:1, :])
         nc.sync.dma_start(k_win[1][:], k_rows[:, 1, :])
         nc.sync.dma_start(w_win[1][:], w_rows[:, 2, :])
-        nc.sync.dma_start(k_win[2][:], k_rows[:, 2, :])
-        nc.sync.dma_start(k_win[3][:], k_rows[:, 3, :])
+        for j in range(2, PACK):
+            nc.sync.dma_start(k_win[j][:], k_rows[:, j, :])
         nc.sync.dma_start(q_raw[:], qT[0].rearrange("(p j) q -> p j q", j=PACK))
         for tokens in token_halves:
             nc.sync.dma_start(v_win[0][:, tokens], vT[:P, tokens])
@@ -93,18 +90,18 @@ def tile_attend_at_ropesig_f_topk_kernel(tc, qT, kT, cT, wT, vT, kb, us, offs, o
         def twice(x):
             return x.unsqueeze(1).to_broadcast([P, 2, x.shape[1]])
 
-        gather(rot[0][:, 1, :], c_win[0], pos)
-        gather_w(0)
         bias = sb([P, PACK], F32, "bias")
-        kb_g = sb([P, N], F32, "kb_g")
-        gather(kb_g[:], kb_win, tok)
-        kb_ps = psum.tile([P, PACK, P], F32, name="kb_ps")
-        kb_by_t = kb_g[:].rearrange("p (m t) -> p t m", t=PACK)
-        for t in range(PACK):
-            nc.tensor.transpose(kb_ps[:, t, :], kb_by_t[:, t, :], ident[:])
-        nc.scalar.copy(bias[:], kb_ps[:, :, 0])
 
-        k_g = [sb([P, N], F32, f"k_g{j}", "kb_win" if j == 0 else None) for j in range(PACK)]
+        def gather_bias(buffer_of):
+            kb_g = sb([P, N], F32, "kb_g", buffer_of)
+            gather(kb_g[:], kb_win, tok)
+            kb_ps = psum.tile([P, PACK, P], F32, name="kb_ps")
+            kb_by_t = kb_g[:].rearrange("p (m t) -> p t m", t=PACK)
+            for t in range(PACK):
+                nc.tensor.transpose(kb_ps[:, t, :], kb_by_t[:, t, :], ident[:])
+            nc.scalar.copy(bias[:], kb_ps[:, :, 0])
+
+        k_g = [sb([P, N], F32, f"k_g{j}", "kb_win" if j == 1 else None) for j in range(PACK)]
         from_even = sb([P, PACK, N], F32, "from_even")
         from_odd = sb([P, PACK, N], F32, "from_odd")
 
@@ -113,30 +110,33 @@ def tile_attend_at_ropesig_f_topk_kernel(tc, qT, kT, cT, wT, vT, kb, us, offs, o
             dest = (from_even, from_odd)[odd]
             (nc.vector if j == PACK - 1 else nc.gpsimd).tensor_tensor(dest[:, 2 * a:2 * a + 2, :], twice(k_g[j][:]), rot[a][:, 1 - odd:3 - odd, :], ALU.mult)
 
-        gather(k_g[0][:], k_win[0], tok)
-        products(0)
+        def keys(j):
+            gather(k_g[j][:], k_win[j], tok)
+            products(j)
+
+        gather(rot[0][:, 1, :], c_win[0], pos)
+        gather_w(0)
+        keys(0)
         gather(rot[1][:, 1, :], c_win[1], pos)
-        gather(k_g[1][:], k_win[1], tok)
-        products(1)
+        gather_bias("c_win1")
+        keys(1)
         gather_w(1)
-        gather(k_g[2][:], k_win[2], tok)
-        products(2)
-        gather(k_g[3][:], k_win[3], tok)
+        keys(2)
+        keys(3)
 
         q_bf = sb([P, NQ, PACK], BF16, "q_bf")
         nc.scalar.copy(q_bf[:], q_raw[:].rearrange("p j q -> p q j"))
-        products(3)
 
-        u_bf = [sb([P, 2, P, PACK], BF16, f"u_bf{half}") for half in range(2)]
+        q_codes = sb([P, NQ], U32, "q_codes", "k_g3")
+        q_scales = sb([P, NQ], U8, "q_scales")
+        quantize(q_codes[:], q_scales[:], q_bf[:])
+        u_bf = [sb([P, 2, P, PACK], BF16, f"u_bf{half}", "q_bf" if half == 0 else None) for half in range(2)]
         for half in range(2):
             ts = slice(2 * half, 2 * half + 2)
             nc.vector.tensor_tensor(
                 u_bf[half][:].rearrange("p t m j -> p m j t"),
                 from_even[:].rearrange("p j (m t) -> p m j t", t=PACK)[:, :, :, ts],
                 from_odd[:].rearrange("p j (m t) -> p m j t", t=PACK)[:, :, :, ts], ALU.add)
-        q_codes = sb([P, NQ], U32, "q_codes", "from_odd")
-        q_scales = sb([P, NQ], U8, "q_scales")
-        quantize(q_codes[:], q_scales[:], q_bf[:])
         u_codes = [sb([P, 2 * P], U32, f"u_codes{half}") for half in range(2)]
         u_scales = [sb([P, 2 * P], U8, f"u_scales{half}") for half in range(2)]
         for half in range(2):
@@ -146,7 +146,7 @@ def tile_attend_at_ropesig_f_topk_kernel(tc, qT, kT, cT, wT, vT, kb, us, offs, o
         v_bf = [yv_bf[:, NQ:NQ + P, :], yv_bf[:, NQ + P:, :], sb([P, P, PACK], BF16, "v2_bf")[:], sb([P, P, PACK], BF16, "v3_bf")[:]]
 
         def turn_values(b, v_g):
-            v_ps = psum.tile([P, 2, P], F32, name=f"v_ps{b}", tag=f"v_bank{b % 3}")
+            v_ps = psum.tile([P, 2, P], F32, name=f"v_ps{b}", tag=f"v_bank{(0, 1, 2, 1)[b]}")
             words = v_g[:].bitcast(F32).rearrange("p (m u) -> p u m", u=2)
             for u in range(2):
                 nc.tensor.transpose(v_ps[:, u, :], words[:, u, :], ident[:])
@@ -156,10 +156,8 @@ def tile_attend_at_ropesig_f_topk_kernel(tc, qT, kT, cT, wT, vT, kb, us, offs, o
         v0_win = sb([P, T], BF16, "v0_win")
         for tokens in token_halves:
             nc.scalar.activation(v0_win[:, tokens], v_win[0][:, tokens], ACT.Copy)
-        v_g0 = sb([P, N], BF16, "v_g0")
-        nc.scalar.activation(v_g0[:], v0_win[:].indirect(tok[:]), ACT.Copy)
 
-        sig = sb([P, PACK, NQ], F32, "sig")
+        sig = sb([P, PACK, NQ], F32, "sig", "v_win0")
         for t in range(PACK):
             half, cols = t // 2, slice(t % 2 * P, (t % 2 + 1) * P)
             s_ps = psum.tile([P, NQ], F32, name=f"s_ps{t}")
@@ -179,15 +177,17 @@ def tile_attend_at_ropesig_f_topk_kernel(tc, qT, kT, cT, wT, vT, kb, us, offs, o
             quantize(codes[:], scales[:], source)
             return codes, scales
 
+        v_g0 = sb([P, N], BF16, "v_g0", "bias")
+        nc.scalar.activation(v_g0[:], v0_win[:].indirect(tok[:]), ACT.Copy)
         v_g1 = gather_values(1)
         v_g2 = gather_values(2)
-        turn_values(0, v_g0)
-        turn_values(1, v_g1)
-        turn_values(2, v_g2)
         nc.vector.tensor_tensor(
             yv_bf[:, :NQ, :].rearrange("p (r i) t -> p r t i", i=RUN), sig[:].rearrange("p t (r i) -> p r t i", i=RUN),
             us_sb[:].unsqueeze(1).unsqueeze(3).to_broadcast([P, NQ // RUN, PACK, RUN]), ALU.mult)
-        turn_values(3, gather_values(3, "sig"))
+        turn_values(1, v_g1)
+        turn_values(0, v_g0)
+        turn_values(2, v_g2)
+        turn_values(3, gather_values(3, "v_win0"))
         yv_codes, yv_scales = quantize_new("yv", yv_bf[:], "v_win3")
         v2_codes, v2_scales = quantize_new("v2", v_bf[2], "v_win2")
         v3_codes, v3_scales = quantize_new("v3", v_bf[3])

@@ -75,8 +75,6 @@ def tile_attend_at_ropesig_f_topk_kernel(tc, qT, kT, cT, wT, vT, kb, us, offs, o
 
         ident = sb([P, P], F32, "ident")
         make_identity(nc, ident[:])
-        warm = sb([P, 1], F32, "warm")
-        nc.scalar.activation(warm[:], ident[:, 0:1], ACT.Sigmoid)
 
         def gather(dest, window, offsets):
             nc.vector.tensor_copy(dest, window[:].indirect(offsets[:]))

@@ -54,8 +54,8 @@ def tile_attend_at_ropesig_f_topk_kernel(tc, qT, kT, cT, wT, vT, kb, us, offs, o
 
         nc.vector.memset(kb_win[:, token_halves[0]], 0.0)
         nc.gpsimd.memset(kb_win[:, token_halves[1]], 0.0)
-        nc.sync.dma_start(pos[:], offs2)
         nc.sync.dma_start(c_win[0][:], c_rows[:, 0, :])
+        nc.sync.dma_start(pos[:], offs2)
         nc.sync.dma_start(w_win[0][:], w_rows[:, 0, :])
         nc.sync.dma_start(tok[:], offs)
         nc.sync.dma_start(us_sb[:], us[0].rearrange("(p t) o -> p (t o)", t=PACK))
@@ -190,21 +190,20 @@ def tile_attend_at_ropesig_f_topk_kernel(tc, qT, kT, cT, wT, vT, kb, us, offs, o
         v2_codes, v2_scales = quantize_new("v2", v_bf[2], "v_win2")
         v3_codes, v3_scales = quantize_new("v3", v_bf[3])
 
-        out_rows = out[0].rearrange("(h p) e -> p h e", p=P)
-
-        def product(name, bank, codes, scales, e0, copy):
+        def product(name, bank, halves, codes, scales, e0, copy):
             width = codes.shape[1]
-            cols = slice(e0, e0 + width)
-            o_ps = psum.tile([P, 2, width], F32, name=f"{name}_ps", tag=bank)
-            o_sb = sb([P, 2, width], F32, f"{name}_sb")
-            for h in range(2):
+            o_ps = psum.tile([P, len(halves), width], F32, name=f"{name}_ps", tag=bank)
+            o_sb = sb([P, len(halves), width], F32, f"{name}_sb")
+            for i, h in enumerate(halves):
                 rows = slice(h * P, (h + 1) * P)
                 nc.tensor.matmul_mx(
-                    o_ps[:, h, :], lhsT=yv_codes[:, rows].bitcast(FP8X4), lhsT_scale=yv_scales[:, rows],
+                    o_ps[:, i, :], lhsT=yv_codes[:, rows].bitcast(FP8X4), lhsT_scale=yv_scales[:, rows],
                     rhs=codes.bitcast(FP8X4), rhs_scale=scales, start=True, stop=True)
             copy(o_sb[:], o_ps[:])
-            nc.sync.dma_start(out_rows[:, :, cols], o_sb[:])
+            nc.sync.dma_start(out_rows[:, halves[0]:halves[-1] + 1, e0:e0 + width], o_sb[:])
 
-        product("o01", "s_ps0", yv_codes[:, NQ:], yv_scales[:, NQ:], 0, nc.scalar.copy)
-        product("o2", "s_ps1", v2_codes[:], v2_scales[:], 2 * P, nc.vector.tensor_copy)
-        product("o3", "s_ps2", v3_codes[:], v3_scales[:], 3 * P, nc.vector.tensor_copy)
+        out_rows = out[0].rearrange("(h p) e -> p h e", p=P)
+        product("o01a", "s_ps0", (0,), yv_codes[:, NQ:], yv_scales[:, NQ:], 0, nc.scalar.copy)
+        product("o01b", "s_ps1", (1,), yv_codes[:, NQ:], yv_scales[:, NQ:], 0, nc.vector.tensor_copy)
+        product("o2", "s_ps2", (0, 1), v2_codes[:], v2_scales[:], 2 * P, nc.scalar.copy)
+        product("o3", "s_ps3", (0, 1), v3_codes[:], v3_scales[:], 3 * P, nc.vector.tensor_copy)

@@ -50,27 +50,24 @@ def tile_attend_at_ropesig_f_topk_kernel(tc, qT, kT, cT, wT, vT, kb, us, offs, o
         k_rows = kT.rearrange("(p j) n -> p j n", j=PACK)
         c_rows = cT.rearrange("(p j) n -> p j n", j=PACK)
         w_rows = wT.rearrange("(p j) n -> p j n", j=PACK)
-        token_halves = (slice(0, T // 2), slice(T // 2, T))
+        last = P - 1
 
-        nc.vector.memset(kb_win[:, token_halves[0]], 0.0)
-        nc.gpsimd.memset(kb_win[:, token_halves[1]], 0.0)
-        nc.sync.dma_start(c_win[0][:], c_rows[:, 0, :])
-        nc.sync.dma_start(pos[:], offs2)
-        nc.sync.dma_start(w_win[0][:], w_rows[:, 0, :])
+        nc.vector.memset(kb_win[:last, :T // 2], 0.0)
+        nc.gpsimd.memset(kb_win[:last, T // 2:], 0.0)
         nc.sync.dma_start(tok[:], offs)
-        nc.sync.dma_start(us_sb[:], us[0].rearrange("(p t) o -> p (t o)", t=PACK))
-        for tokens in token_halves:
-            nc.sync.dma_start(k_win[0][:, tokens], k_rows[:, 0, tokens])
-        nc.sync.dma_start(c_win[1][:], c_rows[:, 2, :])
-        nc.sync.dma_start(kb_win[0:1, :], kb[0:1, :])
+        nc.sync.dma_start(kb_win[last:, :], kb[0:1, :])
+        nc.sync.dma_start(k_win[0][:], k_rows[:, 0, :])
+        nc.sync.dma_start(pos[:], offs2)
+        nc.sync.dma_start(c_win[0][:], c_rows[:, 0, :])
+        nc.sync.dma_start(w_win[0][:], w_rows[:, 0, :])
         nc.sync.dma_start(k_win[1][:], k_rows[:, 1, :])
+        nc.sync.dma_start(us_sb[:], us[0].rearrange("(p t) o -> p (t o)", t=PACK))
+        nc.sync.dma_start(c_win[1][:], c_rows[:, 2, :])
         nc.sync.dma_start(w_win[1][:], w_rows[:, 2, :])
-        for j in range(2, PACK):
-            nc.sync.dma_start(k_win[j][:], k_rows[:, j, :])
+        nc.sync.dma_start(k_win[2][:], k_rows[:, 2, :])
+        nc.sync.dma_start(k_win[3][:], k_rows[:, 3, :])
         nc.sync.dma_start(q_raw[:], qT[0].rearrange("(p j) q -> p j q", j=PACK))
-        for tokens in token_halves:
-            nc.sync.dma_start(v_win[0][:, tokens], vT[:P, tokens])
-        for b in range(1, DV // P):
+        for b in range(DV // P):
             nc.sync.dma_start(v_win[b][:], vT[b * P:(b + 1) * P, :])
 
         ident = sb([P, P], F32, "ident")
@@ -79,95 +76,55 @@ def tile_attend_at_ropesig_f_topk_kernel(tc, qT, kT, cT, wT, vT, kb, us, offs, o
         def gather(dest, window, offsets):
             nc.vector.tensor_copy(dest, window[:].indirect(offsets[:]))
 
-        rot = [sb([P, 3, N], F32, f"rot{a}") for a in range(2)]
-
-        def gather_w(a):
-            gather(rot[a][:, 2, :], w_win[a], pos)
-            nc.scalar.activation(rot[a][:, 0, :], rot[a][:, 2, :], ACT.Copy, scale=-1.0)
-
-        def twice(x):
-            return x.unsqueeze(1).to_broadcast([P, 2, x.shape[1]])
-
         bias = sb([P, PACK], F32, "bias")
-
-        def gather_bias(buffer_of):
-            kb_g = sb([P, N], F32, "kb_g", buffer_of)
-            gather(kb_g[:], kb_win, tok)
-            kb_ps = psum.tile([P, PACK, P], F32, name="kb_ps")
-            kb_by_t = kb_g[:].rearrange("p (m t) -> p t m", t=PACK)
-            for t in range(PACK):
-                nc.tensor.transpose(kb_ps[:, t, :], kb_by_t[:, t, :], ident[:])
-            nc.scalar.copy(bias[:], kb_ps[:, :, 0])
-
-        k_g = [sb([P, N], F32, f"k_g{j}", "kb_win" if j == 1 else None) for j in range(PACK)]
-        from_even = sb([P, PACK, N], F32, "from_even")
-        from_odd = sb([P, PACK, N], F32, "from_odd")
-
-        def products(j):
-            a, odd = divmod(j, 2)
-            dest = (from_even, from_odd)[odd]
-            (nc.vector if j == PACK - 1 else nc.gpsimd).tensor_tensor(dest[:, 2 * a:2 * a + 2, :], twice(k_g[j][:]), rot[a][:, 1 - odd:3 - odd, :], ALU.mult)
-
-        def keys(j):
-            gather(k_g[j][:], k_win[j], tok)
-            products(j)
-
-        gather(rot[0][:, 1, :], c_win[0], pos)
-        gather_w(0)
-        keys(0)
-        gather(rot[1][:, 1, :], c_win[1], pos)
-        gather_bias("c_win1")
-        keys(1)
-        gather_w(1)
-        keys(2)
-        keys(3)
-
-        q_bf = sb([P, NQ, PACK], BF16, "q_bf")
-        nc.scalar.copy(q_bf[:], q_raw[:].rearrange("p j q -> p q j"))
-
-        q_codes = sb([P, NQ], U32, "q_codes", "k_g3")
-        q_scales = sb([P, NQ], U8, "q_scales")
-        quantize(q_codes[:], q_scales[:], q_bf[:])
-        u_bf = [sb([P, 2, P, PACK], BF16, f"u_bf{half}", "q_bf" if half == 0 else None) for half in range(2)]
-        for half in range(2):
-            ts = slice(2 * half, 2 * half + 2)
-            nc.vector.tensor_tensor(
-                u_bf[half][:].rearrange("p t m j -> p m j t"),
-                from_even[:].rearrange("p j (m t) -> p m j t", t=PACK)[:, :, :, ts],
-                from_odd[:].rearrange("p j (m t) -> p m j t", t=PACK)[:, :, :, ts], ALU.add)
-        u_codes = [sb([P, 2 * P], U32, f"u_codes{half}") for half in range(2)]
-        u_scales = [sb([P, 2 * P], U8, f"u_scales{half}") for half in range(2)]
-        for half in range(2):
-            quantize(u_codes[half][:], u_scales[half][:], u_bf[half][:].rearrange("p t m j -> p (t m) j"))
-
-        yv_bf = sb([P, NQ + 2 * P, PACK], BF16, "yv_bf", "v_win2")
-        v_bf = [yv_bf[:, NQ:NQ + P, :], yv_bf[:, NQ + P:, :], sb([P, P, PACK], BF16, "v2_bf")[:], sb([P, P, PACK], BF16, "v3_bf")[:]]
-
-        def turn_values(b, v_g):
-            v_ps = psum.tile([P, 2, P], F32, name=f"v_ps{b}", tag=f"v_bank{(0, 1, 2, 1)[b]}")
-            words = v_g[:].bitcast(F32).rearrange("p (m u) -> p u m", u=2)
-            for u in range(2):
-                nc.tensor.transpose(v_ps[:, u, :], words[:, u, :], ident[:])
-            dest = v_bf[b].rearrange("p e t -> p (e t)").bitcast(F32)
-            nc.scalar.copy(dest.rearrange("p (e u) -> p e u", u=2), v_ps[:].rearrange("p u e -> p e u"))
-
-        v0_win = sb([P, T], BF16, "v0_win")
-        for tokens in token_halves:
-            nc.scalar.activation(v0_win[:, tokens], v_win[0][:, tokens], ACT.Copy)
-
-        sig = sb([P, PACK, NQ], F32, "sig", "v_win0")
+        kb_g = sb([P, N], F32, "kb_g")
+        gather(kb_g[:], kb_win, tok)
+        kb_ps = psum.tile([P, PACK, P], F32, name="kb_ps")
+        kb_by_t = kb_g[:].rearrange("p (m t) -> p t m", t=PACK)
         for t in range(PACK):
-            half, cols = t // 2, slice(t % 2 * P, (t % 2 + 1) * P)
-            s_ps = psum.tile([P, NQ], F32, name=f"s_ps{t}")
-            nc.tensor.matmul_mx(
-                s_ps[:], lhsT=u_codes[half][:, cols].bitcast(FP8X4), lhsT_scale=u_scales[half][:, cols],
-                rhs=q_codes[:].bitcast(FP8X4), rhs_scale=q_scales[:], start=True, stop=True)
-            nc.scalar.activation(sig[:, t, :], s_ps[:], ACT.Sigmoid, bias=bias[:, t:t + 1])
+            nc.tensor.transpose(kb_ps[:, t, :], kb_by_t[:, t, :], ident[:])
+        nc.scalar.copy(bias[:], kb_ps[:, :, last])
 
-        def gather_values(b, buffer_of=None):
-            v_g = sb([P, N], BF16, f"v_g{b}", buffer_of)
-            gather(v_g[:], v_win[b], tok)
-            return v_g
+        k_g = [sb([P, N], F32, f"k_g{j}") for j in range(PACK)]
+        def twice(x):
+            return x.unsqueeze(1).to_broadcast([P, 2, N])
+
+        rot = sb([P, 3, N], F32, "rot")
+        from_k0 = sb([P, 2, N], F32, "from_k0")
+        from_k1 = sb([P, 2, N], F32, "from_k1")
+        u01 = sb([P, 2, N], F32, "u01")
+        gather(k_g[0][:], k_win[0], tok)
+        gather(rot[:, 1, :], c_win[0], pos)
+        nc.gpsimd.tensor_tensor(from_k0[:, 0, :], k_g[0][:], rot[:, 1, :], ALU.mult)
+        gather(rot[:, 2, :], w_win[0], pos)
+        nc.scalar.activation(rot[:, 0, :], rot[:, 2, :], ACT.Copy, scale=-1.0)
+        nc.gpsimd.tensor_tensor(from_k0[:, 1, :], k_g[0][:], rot[:, 2, :], ALU.mult)
+        gather(k_g[1][:], k_win[1], tok)
+        nc.gpsimd.tensor_tensor(from_k1[:], twice(k_g[1][:]), rot[:, 0:2, :], ALU.mult)
+        slot_halves = (slice(0, N // 2), slice(N // 2, N))
+        for slots in slot_halves:
+            nc.gpsimd.tensor_tensor(u01[:, :, slots], from_k0[:, :, slots], from_k1[:, :, slots], ALU.add)
+
+        cw = sb([P, 2, N], F32, "cw")
+        terms = sb([P, 4, N], F32, "terms")
+        gather(cw[:, 0, :], c_win[1], pos)
+        gather(cw[:, 1, :], w_win[1], pos)
+        nc.scalar.activation(terms[:, 0, :], cw[:, 1, :], ACT.Copy, scale=-1.0)
+        gather(k_g[2][:], k_win[2], tok)
+        qu_bf = sb([P, NQ + N, PACK], BF16, "qu_bf", "w_win1")
+        u_by_slot = qu_bf[:, NQ:, :].rearrange("p (t m) j -> p m j t", t=PACK)
+
+        def by_slot(planes):
+            return planes.rearrange("p j (m t) -> p m j t", t=PACK)
+
+        for i, slots in enumerate(slot_halves):
+            nc.scalar.copy(u_by_slot[:, i * P // 2:(i + 1) * P // 2, 0:2, :], by_slot(u01[:, :, slots]))
+        nc.vector.tensor_tensor(terms[:, 3, :], k_g[2][:], terms[:, 0, :], ALU.mult)
+        nc.gpsimd.tensor_tensor(terms[:, 0, :], k_g[2][:], cw[:, 0, :], ALU.mult)
+        gather(k_g[3][:], k_win[3], tok)
+        nc.vector.tensor_tensor(terms[:, 1:3, :], twice(k_g[3][:]), cw[:], ALU.mult)
+
+        nc.scalar.copy(qu_bf[:, :NQ, :], q_raw[:].rearrange("p j q -> p q j"))
 
         def quantize_new(name, source, buffer_of=None):
             codes = sb([P, source.shape[1]], U32, f"{name}_codes", buffer_of)
@@ -175,19 +132,49 @@ def tile_attend_at_ropesig_f_topk_kernel(tc, qT, kT, cT, wT, vT, kb, us, offs, o
             quantize(codes[:], scales[:], source)
             return codes, scales
 
-        v_g0 = sb([P, N], BF16, "v_g0", "bias")
-        nc.scalar.activation(v_g0[:], v0_win[:].indirect(tok[:]), ACT.Copy)
-        v_g1 = gather_values(1)
-        v_g2 = gather_values(2)
-        nc.vector.tensor_tensor(
-            yv_bf[:, :NQ, :].rearrange("p (r i) t -> p r t i", i=RUN), sig[:].rearrange("p t (r i) -> p r t i", i=RUN),
-            us_sb[:].unsqueeze(1).unsqueeze(3).to_broadcast([P, NQ // RUN, PACK, RUN]), ALU.mult)
-        turn_values(1, v_g1)
-        turn_values(0, v_g0)
-        turn_values(2, v_g2)
-        turn_values(3, gather_values(3, "v_win0"))
+        for half in range(2):
+            ts = slice(2 * half, 2 * half + 2)
+            nc.vector.tensor_tensor(
+                u_by_slot[:, :, 2:4, ts], by_slot(terms[:, 0:2, :])[:, :, :, ts], by_slot(terms[:, 2:4, :])[:, :, :, ts], ALU.subtract)
+        qu_codes = sb([P, NQ + N], U32, "qu_codes")
+        qu_scales = sb([P, NQ + N], U8, "qu_scales")
+        for cols in (slice(0, NQ + 2 * P), slice(NQ + 2 * P, NQ + N)):
+            quantize(qu_codes[:, cols], qu_scales[:, cols], qu_bf[:, cols, :])
+
+        yv_bf = sb([P, NQ + 2 * P, PACK], BF16, "yv_bf")
+        v_bf = [yv_bf[:, NQ:NQ + P, :], yv_bf[:, NQ + P:, :], sb([P, P, PACK], BF16, "v2_bf")[:], sb([P, P, PACK], BF16, "v3_bf")[:]]
+
+        sig = sb([P, PACK, NQ], F32, "sig")
+        y_planes = sb([P, PACK, NQ], BF16, "y_planes")
+        for t in range(PACK):
+            cols = slice(NQ + t * P, NQ + (t + 1) * P)
+            s_ps = psum.tile([P, NQ], F32, name=f"s_ps{t}")
+            nc.tensor.matmul_mx(
+                s_ps[:], lhsT=qu_codes[:, cols].bitcast(FP8X4), lhsT_scale=qu_scales[:, cols],
+                rhs=qu_codes[:, :NQ].bitcast(FP8X4), rhs_scale=qu_scales[:, :NQ], start=True, stop=True)
+            nc.scalar.activation(sig[:, t, :], s_ps[:], ACT.Sigmoid, bias=bias[:, t:t + 1])
+            if t < PACK - 1:
+                nc.gpsimd.tensor_scalar(y_planes[:, t, :], sig[:, t, :], us_sb[:, t:t + 1], 0.0, ALU.mult, ALU.add)
+            else:
+                nc.scalar.activation(y_planes[:, t, :], sig[:, t, :], ACT.Copy, scale=us_sb[:, t:t + 1])
+
+        def values(b):
+            v_g = sb([P, N], BF16, f"v_g{b}")
+            gather(v_g[:], v_win[b], tok)
+            v_ps = psum.tile([P, 2, P], F32, name=f"v_ps{b}", tag=f"v_bank{b % 3}")
+            words = v_g[:].bitcast(F32).rearrange("p (m u) -> p u m", u=2)
+            for u in range(2):
+                nc.tensor.transpose(v_ps[:, u, :], words[:, u, :], ident[:])
+            dest = v_bf[b].rearrange("p e t -> p (e t)").bitcast(F32)
+            nc.scalar.copy(dest.rearrange("p (e u) -> p e u", u=2), v_ps[:].rearrange("p u e -> p e u"))
+
+        values(0)
+        nc.scalar.copy(
+            yv_bf[:, :NQ, :].rearrange("p (r i) t -> p r t i", i=RUN), y_planes[:].rearrange("p t (r i) -> p r t i", i=RUN))
+        for b in range(1, DV // P):
+            values(b)
         yv_codes, yv_scales = quantize_new("yv", yv_bf[:], "v_win3")
-        v2_codes, v2_scales = quantize_new("v2", v_bf[2], "v_win2")
+        v2_codes, v2_scales = quantize_new("v2", v_bf[2], "yv_bf")
         v3_codes, v3_scales = quantize_new("v3", v_bf[3])
 
         def product(name, bank, halves, codes, scales, e0, copy):

@@ -63,8 +63,8 @@ def tile_attend_at_ropesig_f_topk_kernel(tc, qT, kT, cT, wT, vT, kb, us, offs, o
         nc.sync.dma_start(k_win[1][:], k_rows[:, 1, :])
         nc.sync.dma_start(us_sb[:], us[0].rearrange("(p t) o -> p (t o)", t=PACK))
         nc.sync.dma_start(c_win[1][:], c_rows[:, 2, :])
-        nc.sync.dma_start(w_win[1][:], w_rows[:, 2, :])
         nc.sync.dma_start(k_win[2][:], k_rows[:, 2, :])
+        nc.sync.dma_start(w_win[1][:], w_rows[:, 2, :])
         nc.sync.dma_start(k_win[3][:], k_rows[:, 3, :])
         nc.sync.dma_start(q_raw[:], qT[0].rearrange("(p j) q -> p j q", j=PACK))
         for b in range(DV // P):
@@ -85,7 +85,7 @@ def tile_attend_at_ropesig_f_topk_kernel(tc, qT, kT, cT, wT, vT, kb, us, offs, o
             nc.tensor.transpose(kb_ps[:, t, :], kb_by_t[:, t, :], ident[:])
         nc.scalar.copy(bias[:], kb_ps[:, :, last])
 
-        k_g = [sb([P, N], F32, f"k_g{j}") for j in range(PACK)]
+        k_g = [sb([P, N], F32, f"k_g{j}") for j in range(3)]
         def twice(x):
             return x.unsqueeze(1).to_broadcast([P, 2, N])
 
@@ -107,22 +107,28 @@ def tile_attend_at_ropesig_f_topk_kernel(tc, qT, kT, cT, wT, vT, kb, us, offs, o
 
         cw = sb([P, 2, N], F32, "cw")
         terms = sb([P, 4, N], F32, "terms")
+        minus_k2 = sb([P, N], F32, "minus_k2")
         gather(cw[:, 0, :], c_win[1], pos)
+        gather(terms[:, 3, :], k_win[2], tok)
+        nc.scalar.activation(minus_k2[:], terms[:, 3, :], ACT.Copy, scale=-1.0)
         gather(cw[:, 1, :], w_win[1], pos)
-        nc.scalar.activation(terms[:, 0, :], cw[:, 1, :], ACT.Copy, scale=-1.0)
-        gather(k_g[2][:], k_win[2], tok)
-        qu_bf = sb([P, NQ + N, PACK], BF16, "qu_bf", "w_win1")
+        qu_bf = sb([P, NQ + N, PACK], BF16, "qu_bf", "k_win2")
         u_by_slot = qu_bf[:, NQ:, :].rearrange("p (t m) j -> p m j t", t=PACK)
 
         def by_slot(planes):
             return planes.rearrange("p j (m t) -> p m j t", t=PACK)
 
-        for i, slots in enumerate(slot_halves):
-            nc.scalar.copy(u_by_slot[:, i * P // 2:(i + 1) * P // 2, 0:2, :], by_slot(u01[:, :, slots]))
-        nc.vector.tensor_tensor(terms[:, 3, :], k_g[2][:], terms[:, 0, :], ALU.mult)
-        nc.gpsimd.tensor_tensor(terms[:, 0, :], k_g[2][:], cw[:, 0, :], ALU.mult)
-        gather(k_g[3][:], k_win[3], tok)
-        nc.vector.tensor_tensor(terms[:, 1:3, :], twice(k_g[3][:]), cw[:], ALU.mult)
+        m_halves = (slice(0, P // 2), slice(P // 2, P))
+        for slots, ms in zip(slot_halves, m_halves):
+            nc.scalar.copy(u_by_slot[:, ms, 0:2, :], by_slot(u01[:, :, slots]))
+        nc.vector.tensor_tensor(terms[:, 0, :], terms[:, 3, :], cw[:, 0, :], ALU.mult)
+        nc.gpsimd.tensor_tensor(terms[:, 3, :], minus_k2[:], cw[:, 1, :], ALU.mult)
+        k3 = k_g[2]
+        for slots in slot_halves:
+            nc.vector.tensor_copy(k3[:, slots], k_win[3][:].indirect(tok[:, slots.start // 16:slots.stop // 16]))
+        for slots in slot_halves:
+            nc.vector.tensor_tensor(
+                terms[:, 1:3, slots], k3[:, slots].unsqueeze(1).to_broadcast([P, 2, N // 2]), cw[:, :, slots], ALU.mult)
 
         nc.scalar.copy(qu_bf[:, :NQ, :], q_raw[:].rearrange("p j q -> p q j"))
 
@@ -132,13 +138,11 @@ def tile_attend_at_ropesig_f_topk_kernel(tc, qT, kT, cT, wT, vT, kb, us, offs, o
             quantize(codes[:], scales[:], source)
             return codes, scales
 
-        for half in range(2):
-            ts = slice(2 * half, 2 * half + 2)
-            nc.vector.tensor_tensor(
-                u_by_slot[:, :, 2:4, ts], by_slot(terms[:, 0:2, :])[:, :, :, ts], by_slot(terms[:, 2:4, :])[:, :, :, ts], ALU.subtract)
+        for slots, ms in zip(slot_halves, m_halves):
+            nc.vector.tensor_tensor(u_by_slot[:, ms, 2:4, :], by_slot(terms[:, 0:2, slots]), by_slot(terms[:, 2:4, slots]), ALU.subtract)
         qu_codes = sb([P, NQ + N], U32, "qu_codes")
         qu_scales = sb([P, NQ + N], U8, "qu_scales")
-        for cols in (slice(0, NQ + 2 * P), slice(NQ + 2 * P, NQ + N)):
+        for cols in (slice(0, NQ), slice(NQ, NQ + 2 * P), slice(NQ + 2 * P, NQ + N)):
             quantize(qu_codes[:, cols], qu_scales[:, cols], qu_bf[:, cols, :])
 
         yv_bf = sb([P, NQ + 2 * P, PACK], BF16, "yv_bf")

@@ -177,24 +177,34 @@ def tile_attend_at_ropesig_f_topk_kernel(tc, qT, kT, cT, wT, vT, kb, us, offs, o
             yv_bf[:, :NQ, :].rearrange("p (r i) t -> p r t i", i=RUN), y_planes[:].rearrange("p t (r i) -> p r t i", i=RUN))
         for b in range(1, DV // P):
             values(b)
-        yv_codes, yv_scales = quantize_new("yv", yv_bf[:], "v_win3")
+        yv_codes = sb([P, 2 * NQ], U32, "yv_codes", "v_win3")
+        yv_scales = sb([P, 2 * NQ], U8, "yv_scales")
+        for cols in (slice(0, P), slice(NQ, 2 * NQ), slice(P, NQ)):
+            quantize(yv_codes[:, cols], yv_scales[:, cols], yv_bf[:, cols, :])
         v2_codes, v2_scales = quantize_new("v2", v_bf[2], "yv_bf")
         v3_codes, v3_scales = quantize_new("v3", v_bf[3])
 
-        def product(name, bank, halves, codes, scales, e0, copy):
-            width = codes.shape[1]
-            o_ps = psum.tile([P, len(halves), width], F32, name=f"{name}_ps", tag=bank)
-            o_sb = sb([P, len(halves), width], F32, f"{name}_sb")
-            for i, h in enumerate(halves):
-                rows = slice(h * P, (h + 1) * P)
-                nc.tensor.matmul_mx(
-                    o_ps[:, i, :], lhsT=yv_codes[:, rows].bitcast(FP8X4), lhsT_scale=yv_scales[:, rows],
-                    rhs=codes.bitcast(FP8X4), rhs_scale=scales, start=True, stop=True)
-            copy(o_sb[:], o_ps[:])
-            nc.sync.dma_start(out_rows[:, halves[0]:halves[-1] + 1, e0:e0 + width], o_sb[:])
+        def product(o_ps, h, codes, scales):
+            rows = slice(h * P, (h + 1) * P)
+            nc.tensor.matmul_mx(
+                o_ps, lhsT=yv_codes[:, rows].bitcast(FP8X4), lhsT_scale=yv_scales[:, rows],
+                rhs=codes.bitcast(FP8X4), rhs_scale=scales, start=True, stop=True)
 
         out_rows = out[0].rearrange("(h p) e -> p h e", p=P)
-        product("o01a", "s_ps0", (0,), yv_codes[:, NQ:], yv_scales[:, NQ:], 0, nc.scalar.copy)
-        product("o01b", "s_ps1", (1,), yv_codes[:, NQ:], yv_scales[:, NQ:], 0, nc.vector.tensor_copy)
-        product("o2", "s_ps2", (0, 1), v2_codes[:], v2_scales[:], 2 * P, nc.scalar.copy)
-        product("o3", "s_ps3", (0, 1), v3_codes[:], v3_scales[:], 3 * P, nc.vector.tensor_copy)
+        engines = (nc.scalar.copy, nc.vector.tensor_copy)
+        for h, copy in enumerate(engines):
+            o_ps = psum.tile([P, 2 * P], F32, name=f"o01_ps{h}", tag=f"s_ps{h}")
+            o_sb = sb([P, 2 * P], F32, f"o01_sb{h}")
+            product(o_ps[:], h, yv_codes[:, NQ:], yv_scales[:, NQ:])
+            copy(o_sb[:], o_ps[:])
+            nc.sync.dma_start(out_rows[:, h, :2 * P], o_sb[:])
+        o23_sb = sb([P, 2, 2 * P], F32, "o23_sb")
+        o2_ps = psum.tile([P, 2, P], F32, name="o2_ps", tag="s_ps2")
+        for h in range(2):
+            product(o2_ps[:, h, :], h, v2_codes[:], v2_scales[:])
+        nc.scalar.copy(o23_sb[:, :, :P], o2_ps[:])
+        for h, (copy, bank) in enumerate(zip(engines, ("s_ps3", "v_bank1"))):
+            o3_ps = psum.tile([P, P], F32, name=f"o3_ps{h}", tag=bank)
+            product(o3_ps[:], h, v3_codes[:], v3_scales[:])
+            copy(o23_sb[:, h, P:], o3_ps[:])
+            nc.sync.dma_start(out_rows[:, h, 2 * P:], o23_sb[:, h, :])

@@ -61,12 +61,12 @@ def tile_attend_at_ropesig_f_topk_kernel(tc, qT, kT, cT, wT, vT, kb, us, offs, o
         nc.sync.dma_start(c_win[0][:], c_rows[:, 0, :])
         nc.sync.dma_start(w_win[0][:], w_rows[:, 0, :])
         nc.sync.dma_start(k_win[1][:], k_rows[:, 1, :])
-        nc.sync.dma_start(us_sb[:], us[0].rearrange("(p t) o -> p (t o)", t=PACK))
         nc.sync.dma_start(c_win[1][:], c_rows[:, 2, :])
         nc.sync.dma_start(k_win[2][:], k_rows[:, 2, :])
         nc.sync.dma_start(w_win[1][:], w_rows[:, 2, :])
         nc.sync.dma_start(k_win[3][:], k_rows[:, 3, :])
         nc.sync.dma_start(q_raw[:], qT[0].rearrange("(p j) q -> p j q", j=PACK))
+        nc.sync.dma_start(us_sb[:], us[0].rearrange("(p t) o -> p (t o)", t=PACK))
         for b in range(DV // P):
             nc.sync.dma_start(v_win[b][:], vT[b * P:(b + 1) * P, :])
 
@@ -130,7 +130,8 @@ def tile_attend_at_ropesig_f_topk_kernel(tc, qT, kT, cT, wT, vT, kb, us, offs, o
             nc.vector.tensor_tensor(
                 terms[:, 1:3, slots], k3[:, slots].unsqueeze(1).to_broadcast([P, 2, N // 2]), cw[:, :, slots], ALU.mult)
 
-        nc.scalar.copy(qu_bf[:, :NQ, :], q_raw[:].rearrange("p j q -> p q j"))
+        nc.scalar.copy(
+            qu_bf[:, :NQ, :].rearrange("p (r i) j -> p r j i", i=RUN), q_raw[:].rearrange("p j (r i) -> p r j i", i=RUN))
 
         def quantize_new(name, source, buffer_of=None):
             codes = sb([P, source.shape[1]], U32, f"{name}_codes", buffer_of)
@@ -192,7 +193,7 @@ def tile_attend_at_ropesig_f_topk_kernel(tc, qT, kT, cT, wT, vT, kb, us, offs, o
 
         out_rows = out[0].rearrange("(h p) e -> p h e", p=P)
         engines = (nc.scalar.copy, nc.vector.tensor_copy)
-        for h, copy in enumerate(engines):
+        for h, copy in enumerate((nc.scalar.copy, nc.scalar.copy)):
             o_ps = psum.tile([P, 2 * P], F32, name=f"o01_ps{h}", tag=f"s_ps{h}")
             o_sb = sb([P, 2 * P], F32, f"o01_sb{h}")
             product(o_ps[:], h, yv_codes[:, NQ:], yv_scales[:, NQ:])
@@ -202,7 +203,7 @@ def tile_attend_at_ropesig_f_topk_kernel(tc, qT, kT, cT, wT, vT, kb, us, offs, o
         o2_ps = psum.tile([P, 2, P], F32, name="o2_ps", tag="s_ps2")
         for h in range(2):
             product(o2_ps[:, h, :], h, v2_codes[:], v2_scales[:])
-        nc.scalar.copy(o23_sb[:, :, :P], o2_ps[:])
+        nc.vector.tensor_copy(o23_sb[:, :, :P], o2_ps[:])
         for h, (copy, bank) in enumerate(zip(engines, ("s_ps3", "v_bank1"))):
             o3_ps = psum.tile([P, P], F32, name=f"o3_ps{h}", tag=bank)
             product(o3_ps[:], h, v3_codes[:], v3_scales[:])

@@ -121,7 +121,7 @@ def tile_attend_at_ropesig_f_topk_kernel(tc, qT, kT, cT, wT, vT, kb, us, offs, o
         m_halves = (slice(0, P // 2), slice(P // 2, P))
         for slots, ms in zip(slot_halves, m_halves):
             nc.scalar.copy(u_by_slot[:, ms, 0:2, :], by_slot(u01[:, :, slots]))
-        nc.vector.tensor_tensor(terms[:, 0, :], terms[:, 3, :], cw[:, 0, :], ALU.mult)
+        nc.gpsimd.tensor_tensor(terms[:, 0, :], terms[:, 3, :], cw[:, 0, :], ALU.mult)
         nc.gpsimd.tensor_tensor(terms[:, 3, :], minus_k2[:], cw[:, 1, :], ALU.mult)
         k3 = k_g[2]
         for slots in slot_halves:
@@ -146,8 +146,8 @@ def tile_attend_at_ropesig_f_topk_kernel(tc, qT, kT, cT, wT, vT, kb, us, offs, o
         for cols in (slice(0, NQ), slice(NQ, NQ + 2 * P), slice(NQ + 2 * P, NQ + N)):
             quantize(qu_codes[:, cols], qu_scales[:, cols], qu_bf[:, cols, :])
 
-        yv_bf = sb([P, NQ + 2 * P, PACK], BF16, "yv_bf")
-        v_bf = [yv_bf[:, NQ:NQ + P, :], yv_bf[:, NQ + P:, :], sb([P, P, PACK], BF16, "v2_bf")[:], sb([P, P, PACK], BF16, "v3_bf")[:]]
+        v01_bf = sb([P, 2 * P, PACK], BF16, "v01_bf")
+        v_bf = [v01_bf[:, :P, :], v01_bf[:, P:, :], sb([P, P, PACK], BF16, "v2_bf")[:], sb([P, P, PACK], BF16, "v3_bf")[:]]
 
         sig = sb([P, PACK, NQ], F32, "sig")
         y_planes = sb([P, PACK, NQ], BF16, "y_planes")
@@ -174,15 +174,21 @@ def tile_attend_at_ropesig_f_topk_kernel(tc, qT, kT, cT, wT, vT, kb, us, offs, o
             nc.scalar.copy(dest.rearrange("p (e u) -> p e u", u=2), v_ps[:].rearrange("p u e -> p e u"))
 
         values(0)
-        nc.scalar.copy(
-            yv_bf[:, :NQ, :].rearrange("p (r i) t -> p r t i", i=RUN), y_planes[:].rearrange("p t (r i) -> p r t i", i=RUN))
-        for b in range(1, DV // P):
-            values(b)
-        yv_codes = sb([P, 2 * NQ], U32, "yv_codes", "v_win3")
-        yv_scales = sb([P, 2 * NQ], U8, "yv_scales")
-        for cols in (slice(0, P), slice(NQ, 2 * NQ), slice(P, NQ)):
-            quantize(yv_codes[:, cols], yv_scales[:, cols], yv_bf[:, cols, :])
-        v2_codes, v2_scales = quantize_new("v2", v_bf[2], "yv_bf")
+        values(1)
+        y_bf = sb([P, NQ, PACK], BF16, "y_bf", "v_g1")
+        q_halves = (slice(0, P), slice(P, NQ))
+        for rows in q_halves:
+            nc.scalar.copy(
+                y_bf[:, rows, :].rearrange("p (r i) t -> p r t i", i=RUN),
+                y_planes[:, :, rows].rearrange("p t (r i) -> p r t i", i=RUN))
+        values(2)
+        v01_codes, v01_scales = quantize_new("v01", v01_bf[:], "v_win2")
+        values(3)
+        yv_codes = sb([P, NQ], U32, "y_codes", "v_win3")
+        yv_scales = sb([P, NQ], U8, "y_scales")
+        for rows in q_halves:
+            quantize(yv_codes[:, rows], yv_scales[:, rows], y_bf[:, rows, :])
+        v2_codes, v2_scales = quantize_new("v2", v_bf[2], "v_g1")
         v3_codes, v3_scales = quantize_new("v3", v_bf[3])
 
         def product(o_ps, h, codes, scales):
@@ -196,7 +202,7 @@ def tile_attend_at_ropesig_f_topk_kernel(tc, qT, kT, cT, wT, vT, kb, us, offs, o
         for h, copy in enumerate((nc.scalar.copy, nc.scalar.copy)):
             o_ps = psum.tile([P, 2 * P], F32, name=f"o01_ps{h}", tag=f"s_ps{h}")
             o_sb = sb([P, 2 * P], F32, f"o01_sb{h}")
-            product(o_ps[:], h, yv_codes[:, NQ:], yv_scales[:, NQ:])
+            product(o_ps[:], h, v01_codes[:], v01_scales[:])
             copy(o_sb[:], o_ps[:])
             nc.sync.dma_start(out_rows[:, h, :2 * P], o_sb[:])
         o23_sb = sb([P, 2, 2 * P], F32, "o23_sb")

@@ -86,13 +86,9 @@ def tile_attend_at_ropesig_f_topk_kernel(tc, qT, kT, cT, wT, vT, kb, us, offs, o
         nc.scalar.copy(bias[:], kb_ps[:, :, last])
 
         k_g = [sb([P, N], F32, f"k_g{j}") for j in range(3)]
-        def twice(x):
-            return x.unsqueeze(1).to_broadcast([P, 2, N])
-
         rot = sb([P, 3, N], F32, "rot")
         from_k0 = sb([P, 2, N], F32, "from_k0")
         from_k1 = sb([P, 2, N], F32, "from_k1")
-        u01 = sb([P, 2, N], F32, "u01")
         gather(k_g[0][:], k_win[0], tok)
         gather(rot[:, 1, :], c_win[0], pos)
         nc.gpsimd.tensor_tensor(from_k0[:, 0, :], k_g[0][:], rot[:, 1, :], ALU.mult)
@@ -100,35 +96,50 @@ def tile_attend_at_ropesig_f_topk_kernel(tc, qT, kT, cT, wT, vT, kb, us, offs, o
         nc.scalar.activation(rot[:, 0, :], rot[:, 2, :], ACT.Copy, scale=-1.0)
         nc.gpsimd.tensor_tensor(from_k0[:, 1, :], k_g[0][:], rot[:, 2, :], ALU.mult)
         gather(k_g[1][:], k_win[1], tok)
-        nc.gpsimd.tensor_tensor(from_k1[:], twice(k_g[1][:]), rot[:, 0:2, :], ALU.mult)
         slot_halves = (slice(0, N // 2), slice(N // 2, N))
         for slots in slot_halves:
-            nc.gpsimd.tensor_tensor(u01[:, :, slots], from_k0[:, :, slots], from_k1[:, :, slots], ALU.add)
+            nc.gpsimd.tensor_tensor(
+                from_k1[:, :, slots], k_g[1][:, slots].unsqueeze(1).to_broadcast([P, 2, N // 2]), rot[:, 0:2, slots], ALU.mult)
 
-        cw = sb([P, 2, N], F32, "cw")
+        cw = sb([P, 3, N], F32, "cw")
         terms = sb([P, 4, N], F32, "terms")
-        minus_k2 = sb([P, N], F32, "minus_k2")
+        k2 = sb([P, N], F32, "k2")
         gather(cw[:, 0, :], c_win[1], pos)
-        gather(terms[:, 3, :], k_win[2], tok)
-        nc.scalar.activation(minus_k2[:], terms[:, 3, :], ACT.Copy, scale=-1.0)
+        nc.scalar.activation(cw[:, 2, :], cw[:, 0, :], ACT.Copy, scale=-1.0)
+        gather(k2[:], k_win[2], tok)
+        nc.gpsimd.tensor_tensor(terms[:, 0, :], k2[:], cw[:, 0, :], ALU.mult)
         gather(cw[:, 1, :], w_win[1], pos)
-        qu_bf = sb([P, NQ + N, PACK], BF16, "qu_bf", "k_win2")
+        nc.gpsimd.tensor_tensor(terms[:, 1, :], k2[:], cw[:, 1, :], ALU.mult)
+        qu_bf = sb([P, NQ + N, PACK], BF16, "qu_bf")
         u_by_slot = qu_bf[:, NQ:, :].rearrange("p (t m) j -> p m j t", t=PACK)
 
         def by_slot(planes):
             return planes.rearrange("p j (m t) -> p m j t", t=PACK)
 
         m_halves = (slice(0, P // 2), slice(P // 2, P))
-        for slots, ms in zip(slot_halves, m_halves):
-            nc.scalar.copy(u_by_slot[:, ms, 0:2, :], by_slot(u01[:, :, slots]))
-        nc.gpsimd.tensor_tensor(terms[:, 0, :], terms[:, 3, :], cw[:, 0, :], ALU.mult)
-        nc.gpsimd.tensor_tensor(terms[:, 3, :], minus_k2[:], cw[:, 1, :], ALU.mult)
+        u_words = qu_bf[:, NQ:, :].rearrange("p c j -> p (c j)").bitcast(F32).rearrange("p (t m a) -> p m t a", t=PACK, a=2)
+        for half, ms in enumerate(m_halves):
+            sum_ps = psum.tile([P, 2, 2, P], F32, name=f"sum_ps{half}", tag=f"s_ps{half}")
+            for c in range(2):
+                slots = slice((2 * half + c) * P, (2 * half + c + 1) * P)
+                for j in range(2):
+                    for term, first in ((from_k0, True), (from_k1, False)):
+                        nc.tensor.matmul(
+                            sum_ps[:, c, j, :], lhsT=term[:, j, slots], rhs=ident[:], start=first, stop=not first,
+                            is_transpose=True)
+            pairs = sb([P, 2, P, 2], BF16, f"pairs{half}")
+            nc.scalar.copy(pairs[:], sum_ps[:].rearrange("s c j p -> s c p j"))
+            pair_words = pairs[:].rearrange("s c p j -> s (c p j)").bitcast(F32)
+            back_ps = psum.tile([P, 2 * P], F32, name=f"back_ps{half}", tag=f"v_bank{half}")
+            for c in range(2):
+                nc.tensor.transpose(back_ps[:, c * P:(c + 1) * P], pair_words[:, c * P:(c + 1) * P], ident[:])
+            nc.scalar.copy(u_words[:, ms, :, 0], back_ps[:].rearrange("p (m t) -> p m t", t=PACK))
         k3 = k_g[2]
         for slots in slot_halves:
             nc.vector.tensor_copy(k3[:, slots], k_win[3][:].indirect(tok[:, slots.start // 16:slots.stop // 16]))
         for slots in slot_halves:
             nc.vector.tensor_tensor(
-                terms[:, 1:3, slots], k3[:, slots].unsqueeze(1).to_broadcast([P, 2, N // 2]), cw[:, :, slots], ALU.mult)
+                terms[:, 2:4, slots], k3[:, slots].unsqueeze(1).to_broadcast([P, 2, N // 2]), cw[:, 1:3, slots], ALU.mult)
 
         nc.scalar.copy(
             qu_bf[:, :NQ, :].rearrange("p (r i) j -> p r j i", i=RUN), q_raw[:].rearrange("p j (r i) -> p r j i", i=RUN))
@@ -158,10 +169,7 @@ def tile_attend_at_ropesig_f_topk_kernel(tc, qT, kT, cT, wT, vT, kb, us, offs, o
                 s_ps[:], lhsT=qu_codes[:, cols].bitcast(FP8X4), lhsT_scale=qu_scales[:, cols],
                 rhs=qu_codes[:, :NQ].bitcast(FP8X4), rhs_scale=qu_scales[:, :NQ], start=True, stop=True)
             nc.scalar.activation(sig[:, t, :], s_ps[:], ACT.Sigmoid, bias=bias[:, t:t + 1])
-            if t < PACK - 1:
-                nc.gpsimd.tensor_scalar(y_planes[:, t, :], sig[:, t, :], us_sb[:, t:t + 1], 0.0, ALU.mult, ALU.add)
-            else:
-                nc.scalar.activation(y_planes[:, t, :], sig[:, t, :], ACT.Copy, scale=us_sb[:, t:t + 1])
+            nc.gpsimd.tensor_scalar(y_planes[:, t, :], sig[:, t, :], us_sb[:, t:t + 1], 0.0, ALU.mult, ALU.add)
 
         def values(b):
             v_g = sb([P, N], BF16, f"v_g{b}")

@@ -21,6 +21,9 @@ D = 512
 NQ = 256
 DV = 512
 RUN = 4
+VECTOR_SHARE = 320
+K_SHARE = 128
+LAST_K_SHARE = 192
 
 FLOPS = 2 * N * NQ * D + 2 * N * NQ * DV
 BYTES = 4 * (D * NQ + D * T + D * POSITIONS + DV * T + T + N + NQ * DV) + 2 * 2 * P * (N // 16)
@@ -38,188 +41,179 @@ def tile_attend_at_ropesig_f_topk_kernel(tc, qT, kT, cT, wT, vT, kb, us, offs, o
         def quantize(codes, scales, source):
             nc.vector.quantize_mx(codes.bitcast(FP8X4), scales, source.rearrange("p c j -> p (c j)"))
 
-        tok = sb([P, N // 16], U16, "tok")
-        pos = sb([P, N // 16], U16, "pos")
-        us_sb = sb([P, PACK], F32, "us_sb")
-        kb_win = sb([P, T], F32, "kb_win")
-        q_raw = sb([P, PACK, NQ], F32, "q_raw")
-        k_win = [sb([P, T], F32, f"k_win{j}") for j in range(PACK)]
-        c_win = [sb([P, POSITIONS], F32, f"c_win{a}") for a in range(2)]
-        w_win = [sb([P, POSITIONS], F32, f"w_win{a}") for a in range(2)]
-        v_win = [sb([P, T], F32, f"v_win{b}") for b in range(DV // P)]
-        k_rows = kT.rearrange("(p j) n -> p j n", j=PACK)
-        c_rows = cT.rearrange("(p j) n -> p j n", j=PACK)
-        w_rows = wT.rearrange("(p j) n -> p j n", j=PACK)
-        last = P - 1
-
-        nc.vector.memset(kb_win[:last, :T // 2], 0.0)
-        nc.gpsimd.memset(kb_win[:last, T // 2:], 0.0)
-        nc.sync.dma_start(tok[:], offs)
-        nc.sync.dma_start(kb_win[last:, :], kb[0:1, :])
-        nc.sync.dma_start(k_win[0][:], k_rows[:, 0, :])
-        nc.sync.dma_start(pos[:], offs2)
-        nc.sync.dma_start(c_win[0][:], c_rows[:, 0, :])
-        nc.sync.dma_start(w_win[0][:], w_rows[:, 0, :])
-        nc.sync.dma_start(k_win[1][:], k_rows[:, 1, :])
-        nc.sync.dma_start(c_win[1][:], c_rows[:, 2, :])
-        nc.sync.dma_start(k_win[2][:], k_rows[:, 2, :])
-        nc.sync.dma_start(w_win[1][:], w_rows[:, 2, :])
-        nc.sync.dma_start(k_win[3][:], k_rows[:, 3, :])
-        nc.sync.dma_start(q_raw[:], qT[0].rearrange("(p j) q -> p j q", j=PACK))
-        nc.sync.dma_start(us_sb[:], us[0].rearrange("(p t) o -> p (t o)", t=PACK))
-        for b in range(DV // P):
-            nc.sync.dma_start(v_win[b][:], vT[b * P:(b + 1) * P, :])
-
-        ident = sb([P, P], F32, "ident")
-        make_identity(nc, ident[:])
-
-        def gather(dest, window, offsets):
-            nc.vector.tensor_copy(dest, window[:].indirect(offsets[:]))
-
-        bias = sb([P, PACK], F32, "bias")
-        kb_g = sb([P, N], F32, "kb_g")
-        gather(kb_g[:], kb_win, tok)
-        kb_ps = psum.tile([P, PACK, P], F32, name="kb_ps")
-        kb_by_t = kb_g[:].rearrange("p (m t) -> p t m", t=PACK)
-        for t in range(PACK):
-            nc.tensor.transpose(kb_ps[:, t, :], kb_by_t[:, t, :], ident[:])
-        nc.scalar.copy(bias[:], kb_ps[:, :, last])
-
-        k_g = [sb([P, N], F32, f"k_g{j}") for j in range(3)]
-        rot = sb([P, 3, N], F32, "rot")
-        from_k0 = sb([P, 2, N], F32, "from_k0")
-        from_k1 = sb([P, 2, N], F32, "from_k1")
-        gather(k_g[0][:], k_win[0], tok)
-        gather(rot[:, 1, :], c_win[0], pos)
-        nc.gpsimd.tensor_tensor(from_k0[:, 0, :], k_g[0][:], rot[:, 1, :], ALU.mult)
-        gather(rot[:, 2, :], w_win[0], pos)
-        nc.scalar.activation(rot[:, 0, :], rot[:, 2, :], ACT.Copy, scale=-1.0)
-        nc.gpsimd.tensor_tensor(from_k0[:, 1, :], k_g[0][:], rot[:, 2, :], ALU.mult)
-        gather(k_g[1][:], k_win[1], tok)
-        slot_halves = (slice(0, N // 2), slice(N // 2, N))
-        for slots in slot_halves:
-            nc.gpsimd.tensor_tensor(
-                from_k1[:, :, slots], k_g[1][:, slots].unsqueeze(1).to_broadcast([P, 2, N // 2]), rot[:, 0:2, slots], ALU.mult)
-
-        cw = sb([P, 3, N], F32, "cw")
-        terms = sb([P, 4, N], F32, "terms")
-        k2 = sb([P, N], F32, "k2")
-        gather(cw[:, 0, :], c_win[1], pos)
-        nc.scalar.activation(cw[:, 2, :], cw[:, 0, :], ACT.Copy, scale=-1.0)
-        gather(k2[:], k_win[2], tok)
-        nc.gpsimd.tensor_tensor(terms[:, 0, :], k2[:], cw[:, 0, :], ALU.mult)
-        gather(cw[:, 1, :], w_win[1], pos)
-        nc.gpsimd.tensor_tensor(terms[:, 1, :], k2[:], cw[:, 1, :], ALU.mult)
-        qu_bf = sb([P, NQ + N, PACK], BF16, "qu_bf")
-        u_by_slot = qu_bf[:, NQ:, :].rearrange("p (t m) j -> p m j t", t=PACK)
-
-        def by_slot(planes):
-            return planes.rearrange("p j (m t) -> p m j t", t=PACK)
-
-        m_halves = (slice(0, P // 2), slice(P // 2, P))
-        u_words = qu_bf[:, NQ:, :].rearrange("p c j -> p (c j)").bitcast(F32).rearrange("p (t m a) -> p m t a", t=PACK, a=2)
-        for half, ms in enumerate(m_halves):
-            sum_ps = psum.tile([P, 2, 2, P], F32, name=f"sum_ps{half}", tag=f"s_ps{half}")
-            for c in range(2):
-                slots = slice((2 * half + c) * P, (2 * half + c + 1) * P)
-                for j in range(2):
-                    for term, first in ((from_k0, True), (from_k1, False)):
-                        nc.tensor.matmul(
-                            sum_ps[:, c, j, :], lhsT=term[:, j, slots], rhs=ident[:], start=first, stop=not first,
-                            is_transpose=True)
-            pairs = sb([P, 2, P, 2], BF16, f"pairs{half}")
-            nc.scalar.copy(pairs[:], sum_ps[:].rearrange("s c j p -> s c p j"))
-            pair_words = pairs[:].rearrange("s c p j -> s (c p j)").bitcast(F32)
-            back_ps = psum.tile([P, 2 * P], F32, name=f"back_ps{half}", tag=f"v_bank{half}")
-            for c in range(2):
-                nc.tensor.transpose(back_ps[:, c * P:(c + 1) * P], pair_words[:, c * P:(c + 1) * P], ident[:])
-            nc.scalar.copy(u_words[:, ms, :, 0], back_ps[:].rearrange("p (m t) -> p m t", t=PACK))
-        k3 = k_g[2]
-        for slots in slot_halves:
-            nc.vector.tensor_copy(k3[:, slots], k_win[3][:].indirect(tok[:, slots.start // 16:slots.stop // 16]))
-        for slots in slot_halves:
-            nc.vector.tensor_tensor(
-                terms[:, 2:4, slots], k3[:, slots].unsqueeze(1).to_broadcast([P, 2, N // 2]), cw[:, 1:3, slots], ALU.mult)
-
-        nc.scalar.copy(
-            qu_bf[:, :NQ, :].rearrange("p (r i) j -> p r j i", i=RUN), q_raw[:].rearrange("p j (r i) -> p r j i", i=RUN))
-
         def quantize_new(name, source, buffer_of=None):
             codes = sb([P, source.shape[1]], U32, f"{name}_codes", buffer_of)
             scales = sb([P, source.shape[1]], U8, f"{name}_scales")
             quantize(codes[:], scales[:], source)
             return codes, scales
 
-        for slots, ms in zip(slot_halves, m_halves):
-            nc.vector.tensor_tensor(u_by_slot[:, ms, 2:4, :], by_slot(terms[:, 0:2, slots]), by_slot(terms[:, 2:4, slots]), ALU.subtract)
-        qu_codes = sb([P, NQ + N], U32, "qu_codes")
-        qu_scales = sb([P, NQ + N], U8, "qu_scales")
-        for cols in (slice(0, NQ), slice(NQ, NQ + 2 * P), slice(NQ + 2 * P, NQ + N)):
-            quantize(qu_codes[:, cols], qu_scales[:, cols], qu_bf[:, cols, :])
+        def entries(offsets, slots):
+            return offsets[:, slots.start // 16:slots.stop // 16]
 
-        v01_bf = sb([P, 2 * P, PACK], BF16, "v01_bf")
-        v_bf = [v01_bf[:, :P, :], v01_bf[:, P:, :], sb([P, P, PACK], BF16, "v2_bf")[:], sb([P, P, PACK], BF16, "v3_bf")[:]]
+        def gather_vector(dest, window, offsets):
+            nc.vector.tensor_copy(dest, window.indirect(offsets))
 
-        sig = sb([P, PACK, NQ], F32, "sig")
-        y_planes = sb([P, PACK, NQ], BF16, "y_planes")
+        def gather_scalar(dest, window, offsets):
+            nc.scalar.activation(dest, window.indirect(offsets), ACT.Copy)
+
+        tok = sb([P, N // 16], U16, "tok")
+        pos = sb([P, N // 16], U16, "pos")
+        us_sb = sb([P, PACK], F32, "us_sb")[:]
+        kb_win = sb([P, T], F32, "kb_win")
+        q_raw = sb([P, PACK, NQ], F32, "q_raw")
+        k_win = [sb([P, T], F32, f"k_win{j}") for j in range(PACK)]
+        c_win = sb([P, 2, POSITIONS], F32, "c_win")
+        w_win = sb([P, 2, POSITIONS], F32, "w_win")
+        v_win = [sb([P, T], F32, f"v_win{b}") for b in range(DV // P)]
+        k_rows = kT.rearrange("(p j) n -> p j n", j=PACK)
+        c_rows = cT.rearrange("(p j) n -> p j n", j=PACK)
+        w_rows = wT.rearrange("(p j) n -> p j n", j=PACK)
+        last = P - 1
+
+        warm = sb([P, 2], F32, "warm")
+        nc.vector.memset(warm[:, 0:1], 0.0)
+        nc.scalar.activation(warm[:, 1:2], warm[:, 0:1], ACT.Sigmoid)
+        nc.vector.memset(kb_win[:last, :T // 2], 0.0)
+        nc.gpsimd.memset(kb_win[:last, T // 2:], 0.0)
+        nc.sync.dma_start(tok[:], offs)
+        nc.sync.dma_start(kb_win[last:, :], kb[0:1, :])
+        nc.sync.dma_start(c_win[:], c_rows[:, 1:3, :])
+        nc.sync.dma_start(pos[:], offs2)
+        nc.sync.dma_start(w_win[:], w_rows[:, 1:3, :])
+        for j in range(PACK):
+            nc.sync.dma_start(k_win[j][:], k_rows[:, j, :])
+        nc.sync.dma_start(q_raw[:], qT[0].rearrange("(p j) q -> p j q", j=PACK))
+        nc.sync.dma_start(us_sb, us[0].rearrange("(p t) o -> p (t o)", t=PACK))
+        for b in range(DV // P):
+            nc.sync.dma_start(v_win[b][:], vT[b * P:(b + 1) * P, :])
+
+        ident = sb([P, P], F32, "ident")
+        make_identity(nc, ident[:])
+
+
+        kb_g = sb([P, N], F32, "kb_g")
+        gather_vector(kb_g[:], kb_win[:], tok[:])
+        kb_ps = psum.tile([P, PACK, P], F32, name="kb_ps")
+        kb_by_t = kb_g[:].rearrange("p (m t) -> p t m", t=PACK)
         for t in range(PACK):
-            cols = slice(NQ + t * P, NQ + (t + 1) * P)
-            s_ps = psum.tile([P, NQ], F32, name=f"s_ps{t}")
-            nc.tensor.matmul_mx(
-                s_ps[:], lhsT=qu_codes[:, cols].bitcast(FP8X4), lhsT_scale=qu_scales[:, cols],
-                rhs=qu_codes[:, :NQ].bitcast(FP8X4), rhs_scale=qu_scales[:, :NQ], start=True, stop=True)
-            nc.scalar.activation(sig[:, t, :], s_ps[:], ACT.Sigmoid, bias=bias[:, t:t + 1])
-            nc.gpsimd.tensor_scalar(y_planes[:, t, :], sig[:, t, :], us_sb[:, t:t + 1], 0.0, ALU.mult, ALU.add)
+            nc.tensor.transpose(kb_ps[:, t, :], kb_by_t[:, t, :], ident[:])
 
-        def values(b):
-            v_g = sb([P, N], BF16, f"v_g{b}")
-            gather(v_g[:], v_win[b], tok)
-            v_ps = psum.tile([P, 2, P], F32, name=f"v_ps{b}", tag=f"v_bank{b % 3}")
-            words = v_g[:].bitcast(F32).rearrange("p (m u) -> p u m", u=2)
+        slot_halves = (slice(0, N // 2), slice(N // 2, N))
+        u_bf = sb([P, N, PACK], BF16, "u_bf")
+        u_by_slot = u_bf[:].rearrange("p (t m) j -> p m j t", t=PACK)
+
+        def by_slot(planes):
+            return planes.rearrange("p j (m t) -> p m j t", t=PACK)
+
+        def shared(vector_slots):
+            return ((slice(0, vector_slots), gather_vector), (slice(vector_slots, N), gather_scalar))
+
+        cw = [sb([P, 2, N], F32, f"cw{a}") for a in range(2)]
+        for which, window in enumerate((c_win, w_win)):
+            gather_scalar(cw[0][:, which, :], window[:, 0, :], pos[:])
+            gather_vector(cw[1][:, which, :], window[:, 1, :], pos[:])
+        terms = sb([P, 2, PACK, N], F32, "terms")
+        for j in range(PACK):
+            a = j // 2
+            parts = []
+            for i, (slots, gather) in enumerate(shared(LAST_K_SHARE if j == PACK - 1 else K_SHARE)):
+                width = slots.stop - slots.start
+                k_g = sb([P, width], F32, f"k_g{j}{i}", "k_vector" if i == 0 else None)
+                gather(k_g[:], k_win[j][:], entries(tok, slots))
+                parts.append((slots, width, k_g))
+            for slots, width, k_g in parts:
+                if j % 2:
+                    both = terms[:].rearrange("p s j n -> p (s j) n")[:, j:PACK + j:PACK - 1, slots]
+                    nc.vector.tensor_tensor(both, k_g[:].unsqueeze(1).to_broadcast([P, 2, width]), cw[a][:, :, slots], ALU.mult)
+                else:
+                    nc.vector.tensor_tensor(terms[:, 0, j, slots], k_g[:], cw[a][:, 0, slots], ALU.mult)
+                    nc.vector.scalar_tensor_tensor(
+                        terms[:, 1, j + 1, slots], k_g[:], -1.0, cw[a][:, 1, slots], ALU.mult, ALU.mult)
+
+        q_bf = sb([P, NQ, PACK], BF16, "q_bf")
+        nc.scalar.copy(
+            q_bf[:].rearrange("p (r i) j -> p r j i", i=RUN), q_raw[:].rearrange("p j (r i) -> p r j i", i=RUN))
+        v2_words = sb([P, N // 2], F32, "v2_words", "q_raw")
+        bias = v2_words[:, :PACK]
+        nc.scalar.copy(bias, kb_ps[:, :, last])
+        u_codes = sb([P, N], U32, "u_codes")
+        u_scales = sb([P, N], U8, "u_scales")
+        for half, cols in enumerate(slot_halves):
+            ts = slice(2 * half, 2 * half + 2)
+            nc.vector.tensor_tensor(
+                u_by_slot[:, :, :, ts], by_slot(terms[:, 0])[:, :, :, ts], by_slot(terms[:, 1])[:, :, :, ts], ALU.subtract)
+            if half == 0:
+                q_codes, q_scales = quantize_new("q", q_bf[:], "k_g31")
+            quantize(u_codes[:, cols], u_scales[:, cols], u_bf[:, cols, :])
+
+        v01_bf = sb([P, 2 * P, PACK], BF16, "v01_bf")[:]
+        v_bf = [v01_bf[:, :P, :], v01_bf[:, P:, :], None, sb([P, P, PACK], BF16, "v3_bf")[:]]
+
+        def values(b, shares, bank, v_g):
+            for slots, gather in shares:
+                gather(v_g[:, slots], v_win[b][:], entries(tok, slots))
+            v_ps = psum.tile([P, 2, P], F32, name=f"v_ps{b}", tag=bank)
+            words = v_g.bitcast(F32).rearrange("p (m u) -> p u m", u=2)
             for u in range(2):
                 nc.tensor.transpose(v_ps[:, u, :], words[:, u, :], ident[:])
             dest = v_bf[b].rearrange("p e t -> p (e t)").bitcast(F32)
             nc.scalar.copy(dest.rearrange("p (e u) -> p e u", u=2), v_ps[:].rearrange("p u e -> p e u"))
 
-        values(0)
-        values(1)
-        y_bf = sb([P, NQ, PACK], BF16, "y_bf", "v_g1")
-        q_halves = (slice(0, P), slice(P, NQ))
-        for rows in q_halves:
-            nc.scalar.copy(
-                y_bf[:, rows, :].rearrange("p (r i) t -> p r t i", i=RUN),
-                y_planes[:, :, rows].rearrange("p t (r i) -> p r t i", i=RUN))
-        values(2)
-        v01_codes, v01_scales = quantize_new("v01", v01_bf[:], "v_win2")
-        values(3)
-        yv_codes = sb([P, NQ], U32, "y_codes", "v_win3")
-        yv_scales = sb([P, NQ], U8, "y_scales")
-        for rows in q_halves:
-            quantize(yv_codes[:, rows], yv_scales[:, rows], y_bf[:, rows, :])
-        v2_codes, v2_scales = quantize_new("v2", v_bf[2], "v_g1")
-        v3_codes, v3_scales = quantize_new("v3", v_bf[3])
+        everything = slice(0, N)
+        v_g0 = sb([P, N], BF16, "v_g0")
+        gather_scalar(v_g0[:], v_win[0][:], tok[:])
+
+        sig = sb([P, PACK, NQ], F32, "sig", "v_win0")
+        for t in range(PACK):
+            cols = slice(t * P, (t + 1) * P)
+            s_ps = psum.tile([P, NQ], F32, name=f"s_ps{t}")
+            nc.tensor.matmul_mx(
+                s_ps[:], lhsT=u_codes[:, cols].bitcast(FP8X4), lhsT_scale=u_scales[:, cols],
+                rhs=q_codes[:].bitcast(FP8X4), rhs_scale=q_scales[:], start=True, stop=True)
+            nc.scalar.activation(sig[:, t, :], s_ps[:], ACT.Sigmoid, bias=bias[:, t:t + 1])
+
+        values(0, [], "s_ps0", v_g0[:])
+        values(1, [(everything, gather_vector)], "s_ps1", sb([P, N], BF16, "v_g1", "u_bf")[:])
+        y_bf = sb([P, NQ, PACK], BF16, "y_bf", "v_win1")
+        nc.vector.tensor_tensor(
+            y_bf[:].rearrange("p (r i) t -> p r t i", i=2), sig[:].rearrange("p t (r i) -> p r t i", i=2),
+            us_sb.unsqueeze(1).unsqueeze(3).to_broadcast([P, NQ // 2, PACK, 2]), ALU.mult)
+        gather_scalar(v2_words[:].bitcast(BF16), v_win[2][:], tok[:])
+        y_codes, y_scales = quantize_new("y", y_bf[:])
+        v01_codes, v01_scales = quantize_new("v01", v01_bf, "v_win1")
 
         def product(o_ps, h, codes, scales):
             rows = slice(h * P, (h + 1) * P)
             nc.tensor.matmul_mx(
-                o_ps, lhsT=yv_codes[:, rows].bitcast(FP8X4), lhsT_scale=yv_scales[:, rows],
+                o_ps, lhsT=y_codes[:, rows].bitcast(FP8X4), lhsT_scale=y_scales[:, rows],
                 rhs=codes.bitcast(FP8X4), rhs_scale=scales, start=True, stop=True)
 
         out_rows = out[0].rearrange("(h p) e -> p h e", p=P)
-        engines = (nc.scalar.copy, nc.vector.tensor_copy)
-        for h, copy in enumerate((nc.scalar.copy, nc.scalar.copy)):
-            o_ps = psum.tile([P, 2 * P], F32, name=f"o01_ps{h}", tag=f"s_ps{h}")
-            o_sb = sb([P, 2 * P], F32, f"o01_sb{h}")
-            product(o_ps[:], h, v01_codes[:], v01_scales[:])
-            copy(o_sb[:], o_ps[:])
-            nc.sync.dma_start(out_rows[:, h, :2 * P], o_sb[:])
-        o23_sb = sb([P, 2, 2 * P], F32, "o23_sb")
+        engines = (nc.vector.tensor_copy, nc.scalar.copy)
+        o01_ps = psum.tile([P, 2, 2 * P], F32, name="o01_ps", tag="s_ps0")
+        for h in range(2):
+            product(o01_ps[:, h, :], h, v01_codes[:], v01_scales[:])
+        v_g3 = sb([P, N], BF16, "v_g3", "v01_bf")
+        for slots, gather in shared(VECTOR_SHARE):
+            gather(v_g3[:, slots], v_win[3][:], entries(tok, slots))
+        late = sb([P, 6 * P], F32, "late", "v_win3")
+        o01_sb = late[:, :4 * P].rearrange("p (h e) -> p h e", h=2)
+        v_bf[2] = late[:, 4 * P:].bitcast(BF16).rearrange("p (e t) -> p e t", t=PACK)
+        values(2, [], "v_bank2", v2_words[:].bitcast(BF16))
+        values(3, [], "v_bank3", v_g3[:])
+        nc.vector.tensor_copy(o01_sb, o01_ps[:])
+        nc.sync.dma_start(out_rows[:, :, :2 * P], o01_sb)
+        v2_codes, v2_scales = quantize_new("v2", v_bf[2])
         o2_ps = psum.tile([P, 2, P], F32, name="o2_ps", tag="s_ps2")
+        o2_sb = sb([P, 2, P], F32, "o2_sb")
         for h in range(2):
             product(o2_ps[:, h, :], h, v2_codes[:], v2_scales[:])
-        nc.vector.tensor_copy(o23_sb[:, :, :P], o2_ps[:])
-        for h, (copy, bank) in enumerate(zip(engines, ("s_ps3", "v_bank1"))):
+        nc.scalar.copy(o2_sb[:], o2_ps[:])
+        nc.sync.dma_start(out_rows[:, :, 2 * P:3 * P], o2_sb[:])
+        v3_codes, v3_scales = quantize_new("v3", v_bf[3])
+        for h, (copy, bank) in enumerate(zip(engines, ("s_ps3", "kb_ps"))):
             o3_ps = psum.tile([P, P], F32, name=f"o3_ps{h}", tag=bank)
+            o3_sb = sb([P, P], F32, f"o3_sb{h}")
             product(o3_ps[:], h, v3_codes[:], v3_scales[:])
-            copy(o23_sb[:, h, P:], o3_ps[:])
-            nc.sync.dma_start(out_rows[:, h, 2 * P:], o23_sb[:, h, :])
+            copy(o3_sb[:], o3_ps[:])
+            nc.sync.dma_start(out_rows[:, h, 3 * P:], o3_sb[:])

@@ -63,7 +63,7 @@ def tile_attend_at_ropesig_f_topk_kernel(tc, qT, kT, cT, wT, vT, kb, us, offs, o
         q_raw = sb([P, PACK, NQ], F32, "q_raw")
         k_win = [sb([P, T], F32, f"k_win{j}") for j in range(PACK)]
         c_win = sb([P, 2, POSITIONS], F32, "c_win")
-        w_win = sb([P, 2, POSITIONS], F32, "w_win")
+        w_win = [sb([P, POSITIONS], F32, f"w_win{a}") for a in range(2)]
         v_win = [sb([P, T], F32, f"v_win{b}") for b in range(DV // P)]
         k_rows = kT.rearrange("(p j) n -> p j n", j=PACK)
         c_rows = cT.rearrange("(p j) n -> p j n", j=PACK)
@@ -75,15 +75,16 @@ def tile_attend_at_ropesig_f_topk_kernel(tc, qT, kT, cT, wT, vT, kb, us, offs, o
         nc.scalar.activation(warm[:, 1:2], warm[:, 0:1], ACT.Sigmoid)
         nc.vector.memset(kb_win[:last, :T // 2], 0.0)
         nc.gpsimd.memset(kb_win[:last, T // 2:], 0.0)
-        nc.sync.dma_start(tok[:], offs)
-        nc.sync.dma_start(kb_win[last:, :], kb[0:1, :])
+        nc.scalar.dma_start(kb_win[last:, :], kb[0:1, :])
+        nc.scalar.dma_start(us_sb, us[0].rearrange("(p t) o -> p (t o)", t=PACK))
         nc.sync.dma_start(c_win[:], c_rows[:, 1:3, :])
         nc.sync.dma_start(pos[:], offs2)
-        nc.sync.dma_start(w_win[:], w_rows[:, 1:3, :])
+        nc.sync.dma_start(tok[:], offs)
         for j in range(PACK):
+            if j % 2 == 0:
+                nc.sync.dma_start(w_win[j // 2][:], w_rows[:, j, :])
             nc.sync.dma_start(k_win[j][:], k_rows[:, j, :])
         nc.sync.dma_start(q_raw[:], qT[0].rearrange("(p j) q -> p j q", j=PACK))
-        nc.sync.dma_start(us_sb, us[0].rearrange("(p t) o -> p (t o)", t=PACK))
         for b in range(DV // P):
             nc.sync.dma_start(v_win[b][:], vT[b * P:(b + 1) * P, :])
 
@@ -100,7 +101,6 @@ def tile_attend_at_ropesig_f_topk_kernel(tc, qT, kT, cT, wT, vT, kb, us, offs, o
 
         slot_halves = (slice(0, N // 2), slice(N // 2, N))
         u_bf = sb([P, N, PACK], BF16, "u_bf")
-        u_by_slot = u_bf[:].rearrange("p (t m) j -> p m j t", t=PACK)
 
         def by_slot(planes):
             return planes.rearrange("p j (m t) -> p m j t", t=PACK)
@@ -109,26 +109,37 @@ def tile_attend_at_ropesig_f_topk_kernel(tc, qT, kT, cT, wT, vT, kb, us, offs, o
             return ((slice(0, vector_slots), gather_vector), (slice(vector_slots, N), gather_scalar))
 
         cw = [sb([P, 2, N], F32, f"cw{a}") for a in range(2)]
-        for which, window in enumerate((c_win, w_win)):
-            gather_scalar(cw[0][:, which, :], window[:, 0, :], pos[:])
-            gather_vector(cw[1][:, which, :], window[:, 1, :], pos[:])
-        terms = sb([P, 2, PACK, N], F32, "terms")
+        gather_scalar(cw[0][:, 0, :], c_win[:, 0, :], pos[:])
+        gather_vector(cw[1][:, 0, :], c_win[:, 1, :], pos[:])
+        pairs = sb([P, 2, N, 2], BF16, "pairs")
+
+        def pair_sum(a, ts):
+            nc.vector.tensor_tensor(
+                pairs[:, a].rearrange("p (t m) e -> p m e t", t=PACK)[:, :, :, ts],
+                by_slot(terms[:, 0])[:, :, :, ts], by_slot(terms[:, 1])[:, :, :, ts], ALU.subtract)
+
         for j in range(PACK):
+            if j % 2 == 0:
+                terms = sb([P, 2, 2, N], F32, f"terms{j // 2}")
             a = j // 2
+            if j % 2 == 0:
+                gather_scalar(cw[a][:, 1, :], w_win[a][:], pos[:])
             parts = []
             for i, (slots, gather) in enumerate(shared(LAST_K_SHARE if j == PACK - 1 else K_SHARE)):
                 width = slots.stop - slots.start
-                k_g = sb([P, width], F32, f"k_g{j}{i}", "k_vector" if i == 0 else None)
+                k_g = sb([P, width], F32, f"k_g{j}{i}", ("terms0" if j > 1 else "k_vector") if i == 0 else None)
                 gather(k_g[:], k_win[j][:], entries(tok, slots))
                 parts.append((slots, width, k_g))
             for slots, width, k_g in parts:
                 if j % 2:
-                    both = terms[:].rearrange("p s j n -> p (s j) n")[:, j:PACK + j:PACK - 1, slots]
+                    both = terms[:].rearrange("p s j n -> p (s j) n")[:, 1:3, slots]
                     nc.vector.tensor_tensor(both, k_g[:].unsqueeze(1).to_broadcast([P, 2, width]), cw[a][:, :, slots], ALU.mult)
                 else:
-                    nc.vector.tensor_tensor(terms[:, 0, j, slots], k_g[:], cw[a][:, 0, slots], ALU.mult)
+                    nc.vector.tensor_tensor(terms[:, 0, 0, slots], k_g[:], cw[a][:, 0, slots], ALU.mult)
                     nc.vector.scalar_tensor_tensor(
-                        terms[:, 1, j + 1, slots], k_g[:], -1.0, cw[a][:, 1, slots], ALU.mult, ALU.mult)
+                        terms[:, 1, 1, slots], k_g[:], -1.0, cw[a][:, 1, slots], ALU.mult, ALU.mult)
+            if j == 1:
+                pair_sum(0, slice(0, PACK))
 
         q_bf = sb([P, NQ, PACK], BF16, "q_bf")
         nc.scalar.copy(
@@ -138,12 +149,14 @@ def tile_attend_at_ropesig_f_topk_kernel(tc, qT, kT, cT, wT, vT, kb, us, offs, o
         nc.scalar.copy(bias, kb_ps[:, :, last])
         u_codes = sb([P, N], U32, "u_codes")
         u_scales = sb([P, N], U8, "u_scales")
-        for half, cols in enumerate(slot_halves):
-            ts = slice(2 * half, 2 * half + 2)
-            nc.vector.tensor_tensor(
-                u_by_slot[:, :, :, ts], by_slot(terms[:, 0])[:, :, :, ts], by_slot(terms[:, 1])[:, :, :, ts], ALU.subtract)
-            if half == 0:
-                q_codes, q_scales = quantize_new("q", q_bf[:], "k_g31")
+        for half in range(2):
+            pair_sum(1, slice(2 * half, 2 * half + 2))
+        q_codes, q_scales = quantize_new("q", q_bf[:], "terms1")
+        pair_words = pairs[:].rearrange("p a c e -> p a (c e)").bitcast(F32).rearrange("p a c -> p c a")
+        u_words = u_bf[:].rearrange("p c j -> p (c j)").bitcast(F32).rearrange("p (c a) -> p c a", a=2)
+        for cols in slot_halves:
+            nc.vector.tensor_copy(u_words[:, cols, :], pair_words[:, cols, :])
+        for cols in slot_halves:
             quantize(u_codes[:, cols], u_scales[:, cols], u_bf[:, cols, :])
 
         v01_bf = sb([P, 2 * P, PACK], BF16, "v01_bf")[:]

@@ -21,9 +21,10 @@ D = 512
 NQ = 256
 DV = 512
 RUN = 4
-VECTOR_SHARE = 320
-K_SHARE = 128
-LAST_K_SHARE = 192
+V2_SHARE = 192
+V1_SHARE = 384
+VECTOR_SHARE = 256
+K_SHARE = 192
 
 FLOPS = 2 * N * NQ * D + 2 * N * NQ * DV
 BYTES = 4 * (D * NQ + D * T + D * POSITIONS + DV * T + T + N + NQ * DV) + 2 * 2 * P * (N // 16)
@@ -76,7 +77,6 @@ def tile_attend_at_ropesig_f_topk_kernel(tc, qT, kT, cT, wT, vT, kb, us, offs, o
         nc.vector.memset(kb_win[:last, :T // 2], 0.0)
         nc.gpsimd.memset(kb_win[:last, T // 2:], 0.0)
         nc.scalar.dma_start(kb_win[last:, :], kb[0:1, :])
-        nc.scalar.dma_start(us_sb, us[0].rearrange("(p t) o -> p (t o)", t=PACK))
         nc.sync.dma_start(c_win[:], c_rows[:, 1:3, :])
         nc.sync.dma_start(pos[:], offs2)
         nc.sync.dma_start(tok[:], offs)
@@ -87,6 +87,8 @@ def tile_attend_at_ropesig_f_topk_kernel(tc, qT, kT, cT, wT, vT, kb, us, offs, o
         nc.sync.dma_start(q_raw[:], qT[0].rearrange("(p j) q -> p j q", j=PACK))
         for b in range(DV // P):
             nc.sync.dma_start(v_win[b][:], vT[b * P:(b + 1) * P, :])
+            if b == 1:
+                nc.sync.dma_start(us_sb, us[0].rearrange("(p t) o -> p (t o)", t=PACK))
 
         ident = sb([P, P], F32, "ident")
         make_identity(nc, ident[:])
@@ -100,7 +102,7 @@ def tile_attend_at_ropesig_f_topk_kernel(tc, qT, kT, cT, wT, vT, kb, us, offs, o
             nc.tensor.transpose(kb_ps[:, t, :], kb_by_t[:, t, :], ident[:])
 
         slot_halves = (slice(0, N // 2), slice(N // 2, N))
-        u_bf = sb([P, N, PACK], BF16, "u_bf")
+        u_bf = [sb([P, N // 2, PACK], BF16, f"u_bf{half}") for half in range(2)]
 
         def by_slot(planes):
             return planes.rearrange("p j (m t) -> p m j t", t=PACK)
@@ -111,12 +113,13 @@ def tile_attend_at_ropesig_f_topk_kernel(tc, qT, kT, cT, wT, vT, kb, us, offs, o
         cw = [sb([P, 2, N], F32, f"cw{a}") for a in range(2)]
         gather_scalar(cw[0][:, 0, :], c_win[:, 0, :], pos[:])
         gather_vector(cw[1][:, 0, :], c_win[:, 1, :], pos[:])
-        pairs = sb([P, 2, N, 2], BF16, "pairs")
+        pairs = [sb([P, 2, N // 2, 2], BF16, f"pairs{half}") for half in range(2)]
 
-        def pair_sum(a, ts):
+        def pair_sum(a, half, ms=slice(0, P)):
+            ts = slice(2 * half, 2 * half + 2)
             nc.vector.tensor_tensor(
-                pairs[:, a].rearrange("p (t m) e -> p m e t", t=PACK)[:, :, :, ts],
-                by_slot(terms[:, 0])[:, :, :, ts], by_slot(terms[:, 1])[:, :, :, ts], ALU.subtract)
+                pairs[half][:, a].rearrange("p (s m) e -> p m e s", s=2)[:, ms],
+                by_slot(terms[:, 0])[:, ms, :, ts], by_slot(terms[:, 1])[:, ms, :, ts], ALU.subtract)
 
         for j in range(PACK):
             if j % 2 == 0:
@@ -125,9 +128,12 @@ def tile_attend_at_ropesig_f_topk_kernel(tc, qT, kT, cT, wT, vT, kb, us, offs, o
             if j % 2 == 0:
                 gather_scalar(cw[a][:, 1, :], w_win[a][:], pos[:])
             parts = []
-            for i, (slots, gather) in enumerate(shared(LAST_K_SHARE if j == PACK - 1 else K_SHARE)):
+            cuts = shared(K_SHARE)
+            if j == PACK - 1:
+                cuts = ((slice(0, P), gather_scalar), (slice(P, P + K_SHARE), gather_vector), (slice(P + K_SHARE, N), gather_scalar))
+            for i, (slots, gather) in enumerate(cuts):
                 width = slots.stop - slots.start
-                k_g = sb([P, width], F32, f"k_g{j}{i}", ("terms0" if j > 1 else "k_vector") if i == 0 else None)
+                k_g = sb([P, width], F32, f"k_g{j}{i}", ("terms0" if j > 1 else "k_vector") if gather is gather_vector else None)
                 gather(k_g[:], k_win[j][:], entries(tok, slots))
                 parts.append((slots, width, k_g))
             for slots, width, k_g in parts:
@@ -139,7 +145,8 @@ def tile_attend_at_ropesig_f_topk_kernel(tc, qT, kT, cT, wT, vT, kb, us, offs, o
                     nc.vector.scalar_tensor_tensor(
                         terms[:, 1, 1, slots], k_g[:], -1.0, cw[a][:, 1, slots], ALU.mult, ALU.mult)
             if j == 1:
-                pair_sum(0, slice(0, PACK))
+                for half in range(2):
+                    pair_sum(0, half)
 
         q_bf = sb([P, NQ, PACK], BF16, "q_bf")
         nc.scalar.copy(
@@ -149,15 +156,18 @@ def tile_attend_at_ropesig_f_topk_kernel(tc, qT, kT, cT, wT, vT, kb, us, offs, o
         nc.scalar.copy(bias, kb_ps[:, :, last])
         u_codes = sb([P, N], U32, "u_codes")
         u_scales = sb([P, N], U8, "u_scales")
-        for half in range(2):
-            pair_sum(1, slice(2 * half, 2 * half + 2))
-        q_codes, q_scales = quantize_new("q", q_bf[:], "terms1")
-        pair_words = pairs[:].rearrange("p a c e -> p a (c e)").bitcast(F32).rearrange("p a c -> p c a")
-        u_words = u_bf[:].rearrange("p c j -> p (c j)").bitcast(F32).rearrange("p (c a) -> p c a", a=2)
-        for cols in slot_halves:
-            nc.vector.tensor_copy(u_words[:, cols, :], pair_words[:, cols, :])
-        for cols in slot_halves:
-            quantize(u_codes[:, cols], u_scales[:, cols], u_bf[:, cols, :])
+        ready = (P + K_SHARE) // PACK
+        pair_sum(1, 0, slice(0, ready))
+        pair_sum(1, 0, slice(ready, P))
+        pair_sum(1, 1)
+        q_codes, q_scales = quantize_new("q", q_bf[:], "k_g32")
+        for half, copy in enumerate((nc.scalar.copy, nc.vector.tensor_copy)):
+            pair_words = pairs[half][:].rearrange("p a c e -> p a (c e)").bitcast(F32).rearrange("p a c -> p c a")
+            copy(u_bf[half][:].rearrange("p c j -> p (c j)").bitcast(F32).rearrange("p (c a) -> p c a", a=2), pair_words)
+        for t in range(2):
+            cols = slice(t * P, (t + 1) * P)
+            quantize(u_codes[:, cols], u_scales[:, cols], u_bf[0][:, cols, :])
+        quantize(u_codes[:, 2 * P:], u_scales[:, 2 * P:], u_bf[1][:])
 
         v01_bf = sb([P, 2 * P, PACK], BF16, "v01_bf")[:]
         v_bf = [v01_bf[:, :P, :], v01_bf[:, P:, :], None, sb([P, P, PACK], BF16, "v3_bf")[:]]
@@ -173,7 +183,7 @@ def tile_attend_at_ropesig_f_topk_kernel(tc, qT, kT, cT, wT, vT, kb, us, offs, o
             nc.scalar.copy(dest.rearrange("p (e u) -> p e u", u=2), v_ps[:].rearrange("p u e -> p e u"))
 
         everything = slice(0, N)
-        v_g0 = sb([P, N], BF16, "v_g0")
+        v_g0 = sb([P, N], BF16, "v_g0", "pairs0")
         gather_scalar(v_g0[:], v_win[0][:], tok[:])
 
         sig = sb([P, PACK, NQ], F32, "sig", "v_win0")
@@ -186,14 +196,17 @@ def tile_attend_at_ropesig_f_topk_kernel(tc, qT, kT, cT, wT, vT, kb, us, offs, o
             nc.scalar.activation(sig[:, t, :], s_ps[:], ACT.Sigmoid, bias=bias[:, t:t + 1])
 
         values(0, [], "s_ps0", v_g0[:])
-        values(1, [(everything, gather_vector)], "s_ps1", sb([P, N], BF16, "v_g1", "u_bf")[:])
-        y_bf = sb([P, NQ, PACK], BF16, "y_bf", "v_win1")
+        values(1, shared(V1_SHARE), "s_ps1", sb([P, N], BF16, "v_g1", "u_bf1")[:])
+        y_bf = sb([P, NQ, PACK], BF16, "y_bf")
         nc.vector.tensor_tensor(
             y_bf[:].rearrange("p (r i) t -> p r t i", i=2), sig[:].rearrange("p t (r i) -> p r t i", i=2),
             us_sb.unsqueeze(1).unsqueeze(3).to_broadcast([P, NQ // 2, PACK, 2]), ALU.mult)
-        gather_scalar(v2_words[:].bitcast(BF16), v_win[2][:], tok[:])
+        v_g2 = v2_words[:].bitcast(BF16)
+        gather_scalar(v_g2[:, :N - V2_SHARE], v_win[2][:], entries(tok, slice(0, N - V2_SHARE)))
         y_codes, y_scales = quantize_new("y", y_bf[:])
-        v01_codes, v01_scales = quantize_new("v01", v01_bf, "v_win1")
+        v01_codes, v01_scales = quantize_new("v01", v01_bf, "y_bf")
+
+        gather_vector(v_g2[:, N - V2_SHARE:], v_win[2][:], entries(tok, slice(N - V2_SHARE, N)))
 
         def product(o_ps, h, codes, scales):
             rows = slice(h * P, (h + 1) * P)
@@ -206,7 +219,7 @@ def tile_attend_at_ropesig_f_topk_kernel(tc, qT, kT, cT, wT, vT, kb, us, offs, o
         o01_ps = psum.tile([P, 2, 2 * P], F32, name="o01_ps", tag="s_ps0")
         for h in range(2):
             product(o01_ps[:, h, :], h, v01_codes[:], v01_scales[:])
-        v_g3 = sb([P, N], BF16, "v_g3", "v01_bf")
+        v_g3 = sb([P, N], BF16, "v_g3", "v_win2")
         for slots, gather in shared(VECTOR_SHARE):
             gather(v_g3[:, slots], v_win[3][:], entries(tok, slots))
         late = sb([P, 6 * P], F32, "late", "v_win3")

@@ -102,7 +102,7 @@ def tile_attend_at_ropesig_f_topk_kernel(tc, qT, kT, cT, wT, vT, kb, us, offs, o
             nc.tensor.transpose(kb_ps[:, t, :], kb_by_t[:, t, :], ident[:])
 
         slot_halves = (slice(0, N // 2), slice(N // 2, N))
-        u_bf = [sb([P, N // 2, PACK], BF16, f"u_bf{half}") for half in range(2)]
+        u_first = sb([P, N // 2, PACK], BF16, "u_first")
 
         def by_slot(planes):
             return planes.rearrange("p j (m t) -> p m j t", t=PACK)
@@ -151,8 +151,10 @@ def tile_attend_at_ropesig_f_topk_kernel(tc, qT, kT, cT, wT, vT, kb, us, offs, o
         q_bf = sb([P, NQ, PACK], BF16, "q_bf")
         nc.scalar.copy(
             q_bf[:].rearrange("p (r i) j -> p r j i", i=RUN), q_raw[:].rearrange("p j (r i) -> p r j i", i=RUN))
-        v2_words = sb([P, N // 2], F32, "v2_words", "q_raw")
-        bias = v2_words[:, :PACK]
+        stage = sb([P, N + (N - V1_SHARE) // 2], F32, "stage", "q_raw")
+        u_bf = [u_first[:], stage[:, :N].bitcast(BF16).rearrange("p (c j) -> p c j", j=PACK)]
+        bias = stage[:, N:N + PACK]
+        v_g12 = stage[:, N - V1_SHARE // 2:].bitcast(BF16)
         nc.scalar.copy(bias, kb_ps[:, :, last])
         u_codes = sb([P, N], U32, "u_codes")
         u_scales = sb([P, N], U8, "u_scales")
@@ -163,11 +165,11 @@ def tile_attend_at_ropesig_f_topk_kernel(tc, qT, kT, cT, wT, vT, kb, us, offs, o
         q_codes, q_scales = quantize_new("q", q_bf[:], "k_g32")
         for half, copy in enumerate((nc.scalar.copy, nc.vector.tensor_copy)):
             pair_words = pairs[half][:].rearrange("p a c e -> p a (c e)").bitcast(F32).rearrange("p a c -> p c a")
-            copy(u_bf[half][:].rearrange("p c j -> p (c j)").bitcast(F32).rearrange("p (c a) -> p c a", a=2), pair_words)
+            copy(u_bf[half].rearrange("p c j -> p (c j)").bitcast(F32).rearrange("p (c a) -> p c a", a=2), pair_words)
         for t in range(2):
             cols = slice(t * P, (t + 1) * P)
             quantize(u_codes[:, cols], u_scales[:, cols], u_bf[0][:, cols, :])
-        quantize(u_codes[:, 2 * P:], u_scales[:, 2 * P:], u_bf[1][:])
+        quantize(u_codes[:, 2 * P:], u_scales[:, 2 * P:], u_bf[1])
 
         v01_bf = sb([P, 2 * P, PACK], BF16, "v01_bf")[:]
         v_bf = [v01_bf[:, :P, :], v01_bf[:, P:, :], None, sb([P, P, PACK], BF16, "v3_bf")[:]]
@@ -196,12 +198,12 @@ def tile_attend_at_ropesig_f_topk_kernel(tc, qT, kT, cT, wT, vT, kb, us, offs, o
             nc.scalar.activation(sig[:, t, :], s_ps[:], ACT.Sigmoid, bias=bias[:, t:t + 1])
 
         values(0, [], "s_ps0", v_g0[:])
-        values(1, shared(V1_SHARE), "s_ps1", sb([P, N], BF16, "v_g1", "u_bf1")[:])
+        values(1, shared(V1_SHARE), "s_ps1", v_g12)
         y_bf = sb([P, NQ, PACK], BF16, "y_bf")
         nc.vector.tensor_tensor(
             y_bf[:].rearrange("p (r i) t -> p r t i", i=2), sig[:].rearrange("p t (r i) -> p r t i", i=2),
             us_sb.unsqueeze(1).unsqueeze(3).to_broadcast([P, NQ // 2, PACK, 2]), ALU.mult)
-        v_g2 = v2_words[:].bitcast(BF16)
+        v_g2 = v_g12
         gather_scalar(v_g2[:, :N - V2_SHARE], v_win[2][:], entries(tok, slice(0, N - V2_SHARE)))
         y_codes, y_scales = quantize_new("y", y_bf[:])
         v01_codes, v01_scales = quantize_new("v01", v01_bf, "y_bf")
@@ -216,20 +218,22 @@ def tile_attend_at_ropesig_f_topk_kernel(tc, qT, kT, cT, wT, vT, kb, us, offs, o
 
         out_rows = out[0].rearrange("(h p) e -> p h e", p=P)
         engines = (nc.vector.tensor_copy, nc.scalar.copy)
-        o01_ps = psum.tile([P, 2, 2 * P], F32, name="o01_ps", tag="s_ps0")
+        o01_ps = [psum.tile([P, 2 * P], F32, name=f"o01_ps{h}", tag=f"s_ps{h}") for h in range(2)]
         for h in range(2):
-            product(o01_ps[:, h, :], h, v01_codes[:], v01_scales[:])
+            product(o01_ps[h][:], h, v01_codes[:], v01_scales[:])
         v_g3 = sb([P, N], BF16, "v_g3", "v_win2")
         for slots, gather in shared(VECTOR_SHARE):
             gather(v_g3[:, slots], v_win[3][:], entries(tok, slots))
-        late = sb([P, 6 * P], F32, "late", "v_win3")
-        o01_sb = late[:, :4 * P].rearrange("p (h e) -> p h e", h=2)
-        v_bf[2] = late[:, 4 * P:].bitcast(BF16).rearrange("p (e t) -> p e t", t=PACK)
-        values(2, [], "v_bank2", v2_words[:].bitcast(BF16))
+        late = sb([P, 4 * P], F32, "late", "v_win3")
+        o01_sb = late[:].rearrange("p (h e) -> p h e", h=2)
+        v_bf[2] = late[:, 2 * P:].bitcast(BF16).rearrange("p (e t) -> p e t", t=PACK)
+        values(2, [], "v_bank2", v_g12)
         values(3, [], "v_bank3", v_g3[:])
-        nc.vector.tensor_copy(o01_sb, o01_ps[:])
-        nc.sync.dma_start(out_rows[:, :, :2 * P], o01_sb)
-        v2_codes, v2_scales = quantize_new("v2", v_bf[2])
+        for h in range(2):
+            nc.vector.tensor_copy(o01_sb[:, h, :], o01_ps[h][:])
+            nc.sync.dma_start(out_rows[:, h, :2 * P], o01_sb[:, h, :])
+            if h == 0:
+                v2_codes, v2_scales = quantize_new("v2", v_bf[2])
         o2_ps = psum.tile([P, 2, P], F32, name="o2_ps", tag="s_ps2")
         o2_sb = sb([P, 2, P], F32, "o2_sb")
         for h in range(2):

@@ -20,14 +20,17 @@ POSITIONS = 1024
 D = 512
 NQ = 256
 DV = 512
-RUN = 4
-V2_SHARE = 192
-V1_SHARE = 384
-VECTOR_SHARE = 256
+PER_COLUMN = 16
+Q_RUN = 4
+Y_RUN = 2
+
 K_SHARE = 192
+V1_SHARE = 384
+V2_SHARE = 192
+V3_SHARE = 256
 
 FLOPS = 2 * N * NQ * D + 2 * N * NQ * DV
-BYTES = 4 * (D * NQ + D * T + D * POSITIONS + DV * T + T + N + NQ * DV) + 2 * 2 * P * (N // 16)
+BYTES = 4 * (D * NQ + D * T + D * POSITIONS + DV * T + T + N + NQ * DV) + 2 * 2 * P * (N // PER_COLUMN)
 
 
 def tile_attend_at_ropesig_f_topk_kernel(tc, qT, kT, cT, wT, vT, kb, us, offs, offs2, out):
@@ -49,7 +52,7 @@ def tile_attend_at_ropesig_f_topk_kernel(tc, qT, kT, cT, wT, vT, kb, us, offs, o
             return codes, scales
 
         def entries(offsets, slots):
-            return offsets[:, slots.start // 16:slots.stop // 16]
+            return offsets[:, slots.start // PER_COLUMN:slots.stop // PER_COLUMN]
 
         def gather_vector(dest, window, offsets):
             nc.vector.tensor_copy(dest, window.indirect(offsets))
@@ -57,8 +60,17 @@ def tile_attend_at_ropesig_f_topk_kernel(tc, qT, kT, cT, wT, vT, kb, us, offs, o
         def gather_scalar(dest, window, offsets):
             nc.scalar.activation(dest, window.indirect(offsets), ACT.Copy)
 
-        tok = sb([P, N // 16], U16, "tok")
-        pos = sb([P, N // 16], U16, "pos")
+        def shared(vector_slots):
+            return ((slice(0, vector_slots), gather_vector), (slice(vector_slots, N), gather_scalar))
+
+        def by_slot(planes):
+            return planes.rearrange("p j (m t) -> p m j t", t=PACK)
+
+        def as_words(tile_bf16):
+            return tile_bf16.rearrange("p c j -> p (c j)").bitcast(F32).rearrange("p (c a) -> p c a", a=2)
+
+        tok = sb([P, N // PER_COLUMN], U16, "tok")
+        pos = sb([P, N // PER_COLUMN], U16, "pos")
         us_sb = sb([P, PACK], F32, "us_sb")[:]
         kb_win = sb([P, T], F32, "kb_win")
         q_raw = sb([P, PACK, NQ], F32, "q_raw")
@@ -74,9 +86,11 @@ def tile_attend_at_ropesig_f_topk_kernel(tc, qT, kT, cT, wT, vT, kb, us, offs, o
         warm = sb([P, 2], F32, "warm")
         nc.vector.memset(warm[:, 0:1], 0.0)
         nc.scalar.activation(warm[:, 1:2], warm[:, 0:1], ACT.Sigmoid)
+
         nc.vector.memset(kb_win[:last, :T // 2], 0.0)
         nc.gpsimd.memset(kb_win[:last, T // 2:], 0.0)
         nc.scalar.dma_start(kb_win[last:, :], kb[0:1, :])
+
         nc.sync.dma_start(c_win[:], c_rows[:, 1:3, :])
         nc.sync.dma_start(pos[:], offs2)
         nc.sync.dma_start(tok[:], offs)
@@ -93,7 +107,6 @@ def tile_attend_at_ropesig_f_topk_kernel(tc, qT, kT, cT, wT, vT, kb, us, offs, o
         ident = sb([P, P], F32, "ident")
         make_identity(nc, ident[:])
 
-
         kb_g = sb([P, N], F32, "kb_g")
         gather_vector(kb_g[:], kb_win[:], tok[:])
         kb_ps = psum.tile([P, PACK, P], F32, name="kb_ps")
@@ -101,90 +114,89 @@ def tile_attend_at_ropesig_f_topk_kernel(tc, qT, kT, cT, wT, vT, kb, us, offs, o
         for t in range(PACK):
             nc.tensor.transpose(kb_ps[:, t, :], kb_by_t[:, t, :], ident[:])
 
-        slot_halves = (slice(0, N // 2), slice(N // 2, N))
         u_first = sb([P, N // 2, PACK], BF16, "u_first")
-
-        def by_slot(planes):
-            return planes.rearrange("p j (m t) -> p m j t", t=PACK)
-
-        def shared(vector_slots):
-            return ((slice(0, vector_slots), gather_vector), (slice(vector_slots, N), gather_scalar))
 
         cw = [sb([P, 2, N], F32, f"cw{a}") for a in range(2)]
         gather_scalar(cw[0][:, 0, :], c_win[:, 0, :], pos[:])
         gather_vector(cw[1][:, 0, :], c_win[:, 1, :], pos[:])
+
         pairs = [sb([P, 2, N // 2, 2], BF16, f"pairs{half}") for half in range(2)]
 
-        def pair_sum(a, half, ms=slice(0, P)):
+        def pair_sum(a, terms, half, ms=slice(0, P)):
             ts = slice(2 * half, 2 * half + 2)
             nc.vector.tensor_tensor(
                 pairs[half][:, a].rearrange("p (s m) e -> p m e s", s=2)[:, ms],
                 by_slot(terms[:, 0])[:, ms, :, ts], by_slot(terms[:, 1])[:, ms, :, ts], ALU.subtract)
 
-        for j in range(PACK):
-            if j % 2 == 0:
-                terms = sb([P, 2, 2, N], F32, f"terms{j // 2}")
-            a = j // 2
-            if j % 2 == 0:
-                gather_scalar(cw[a][:, 1, :], w_win[a][:], pos[:])
-            parts = []
-            cuts = shared(K_SHARE)
-            if j == PACK - 1:
-                cuts = ((slice(0, P), gather_scalar), (slice(P, P + K_SHARE), gather_vector), (slice(P + K_SHARE, N), gather_scalar))
-            for i, (slots, gather) in enumerate(cuts):
-                width = slots.stop - slots.start
-                k_g = sb([P, width], F32, f"k_g{j}{i}", ("terms0" if j > 1 else "k_vector") if gather is gather_vector else None)
-                gather(k_g[:], k_win[j][:], entries(tok, slots))
-                parts.append((slots, width, k_g))
-            for slots, width, k_g in parts:
-                if j % 2:
-                    both = terms[:].rearrange("p s j n -> p (s j) n")[:, 1:3, slots]
-                    nc.vector.tensor_tensor(both, k_g[:].unsqueeze(1).to_broadcast([P, 2, width]), cw[a][:, :, slots], ALU.mult)
-                else:
-                    nc.vector.tensor_tensor(terms[:, 0, 0, slots], k_g[:], cw[a][:, 0, slots], ALU.mult)
-                    nc.vector.scalar_tensor_tensor(
-                        terms[:, 1, 1, slots], k_g[:], -1.0, cw[a][:, 1, slots], ALU.mult, ALU.mult)
-            if j == 1:
+        last_plane_cuts = (
+            (slice(0, P), gather_scalar), (slice(P, P + K_SHARE), gather_vector), (slice(P + K_SHARE, N), gather_scalar))
+        for a in range(2):
+            terms = sb([P, 2, 2, N], F32, f"terms{a}")
+            gather_scalar(cw[a][:, 1, :], w_win[a][:], pos[:])
+            for odd in range(2):
+                j = 2 * a + odd
+                parts = []
+                for i, (slots, gather) in enumerate(last_plane_cuts if j == PACK - 1 else shared(K_SHARE)):
+                    width = slots.stop - slots.start
+                    vector_buffer = "terms0" if a else "k_vector"
+                    k_g = sb([P, width], F32, f"k_g{j}{i}", vector_buffer if gather is gather_vector else None)
+                    gather(k_g[:], k_win[j][:], entries(tok, slots))
+                    parts.append((slots, width, k_g))
+                for slots, width, k_g in parts:
+                    if odd:
+                        both = terms[:].rearrange("p s j n -> p (s j) n")[:, 1:3, slots]
+                        nc.vector.tensor_tensor(
+                            both, k_g[:].unsqueeze(1).to_broadcast([P, 2, width]), cw[a][:, :, slots], ALU.mult)
+                    else:
+                        nc.vector.tensor_tensor(terms[:, 0, 0, slots], k_g[:], cw[a][:, 0, slots], ALU.mult)
+                        nc.vector.scalar_tensor_tensor(
+                            terms[:, 1, 1, slots], k_g[:], -1.0, cw[a][:, 1, slots], ALU.mult, ALU.mult)
+            if a == 0:
                 for half in range(2):
-                    pair_sum(0, half)
+                    pair_sum(0, terms, half)
 
         q_bf = sb([P, NQ, PACK], BF16, "q_bf")
         nc.scalar.copy(
-            q_bf[:].rearrange("p (r i) j -> p r j i", i=RUN), q_raw[:].rearrange("p j (r i) -> p r j i", i=RUN))
+            q_bf[:].rearrange("p (r i) j -> p r j i", i=Q_RUN), q_raw[:].rearrange("p j (r i) -> p r j i", i=Q_RUN))
+
         stage = sb([P, N + (N - V1_SHARE) // 2], F32, "stage", "q_raw")
         u_bf = [u_first[:], stage[:, :N].bitcast(BF16).rearrange("p (c j) -> p c j", j=PACK)]
         bias = stage[:, N:N + PACK]
         v_g12 = stage[:, N - V1_SHARE // 2:].bitcast(BF16)
         nc.scalar.copy(bias, kb_ps[:, :, last])
+
         u_codes = sb([P, N], U32, "u_codes")
         u_scales = sb([P, N], U8, "u_scales")
-        ready = (P + K_SHARE) // PACK
-        pair_sum(1, 0, slice(0, ready))
-        pair_sum(1, 0, slice(ready, P))
-        pair_sum(1, 1)
-        q_codes, q_scales = quantize_new("q", q_bf[:], "k_g32")
+        older = (P + K_SHARE) // PACK
+        pair_sum(1, terms, 0, slice(0, older))
+        pair_sum(1, terms, 0, slice(older, P))
+        pair_sum(1, terms, 1)
+        q_codes, q_scales = quantize_new("q", q_bf[:], f"k_g{PACK - 1}2")
+
         for half, copy in enumerate((nc.scalar.copy, nc.vector.tensor_copy)):
             pair_words = pairs[half][:].rearrange("p a c e -> p a (c e)").bitcast(F32).rearrange("p a c -> p c a")
-            copy(u_bf[half].rearrange("p c j -> p (c j)").bitcast(F32).rearrange("p (c a) -> p c a", a=2), pair_words)
+            copy(as_words(u_bf[half]), pair_words)
         for t in range(2):
             cols = slice(t * P, (t + 1) * P)
             quantize(u_codes[:, cols], u_scales[:, cols], u_bf[0][:, cols, :])
         quantize(u_codes[:, 2 * P:], u_scales[:, 2 * P:], u_bf[1])
 
         v01_bf = sb([P, 2 * P, PACK], BF16, "v01_bf")[:]
-        v_bf = [v01_bf[:, :P, :], v01_bf[:, P:, :], None, sb([P, P, PACK], BF16, "v3_bf")[:]]
+        v3_bf = sb([P, P, PACK], BF16, "v3_bf")[:]
 
-        def values(b, shares, bank, v_g):
+        def gather_values(b, shares, v_g):
             for slots, gather in shares:
                 gather(v_g[:, slots], v_win[b][:], entries(tok, slots))
+
+        def turn_values(b, v_g, bank, v_bf, pieces=1):
             v_ps = psum.tile([P, 2, P], F32, name=f"v_ps{b}", tag=bank)
             words = v_g.bitcast(F32).rearrange("p (m u) -> p u m", u=2)
             for u in range(2):
                 nc.tensor.transpose(v_ps[:, u, :], words[:, u, :], ident[:])
-            dest = v_bf[b].rearrange("p e t -> p (e t)").bitcast(F32)
-            nc.scalar.copy(dest.rearrange("p (e u) -> p e u", u=2), v_ps[:].rearrange("p u e -> p e u"))
+            for i in range(pieces):
+                es = slice(i * P // pieces, (i + 1) * P // pieces)
+                nc.scalar.copy(as_words(v_bf[:, es, :]), v_ps[:, :, es].rearrange("p u e -> p e u"))
 
-        everything = slice(0, N)
         v_g0 = sb([P, N], BF16, "v_g0", "pairs0")
         gather_scalar(v_g0[:], v_win[0][:], tok[:])
 
@@ -197,18 +209,18 @@ def tile_attend_at_ropesig_f_topk_kernel(tc, qT, kT, cT, wT, vT, kb, us, offs, o
                 rhs=q_codes[:].bitcast(FP8X4), rhs_scale=q_scales[:], start=True, stop=True)
             nc.scalar.activation(sig[:, t, :], s_ps[:], ACT.Sigmoid, bias=bias[:, t:t + 1])
 
-        values(0, [], "s_ps0", v_g0[:])
-        values(1, shared(V1_SHARE), "s_ps1", v_g12)
+        turn_values(0, v_g0[:], "s_ps0", v01_bf[:, :P, :])
+        gather_values(1, shared(V1_SHARE), v_g12)
+        turn_values(1, v_g12, "s_ps1", v01_bf[:, P:, :])
+
         y_bf = sb([P, NQ, PACK], BF16, "y_bf")
         nc.vector.tensor_tensor(
-            y_bf[:].rearrange("p (r i) t -> p r t i", i=2), sig[:].rearrange("p t (r i) -> p r t i", i=2),
-            us_sb.unsqueeze(1).unsqueeze(3).to_broadcast([P, NQ // 2, PACK, 2]), ALU.mult)
-        v_g2 = v_g12
-        gather_scalar(v_g2[:, :N - V2_SHARE], v_win[2][:], entries(tok, slice(0, N - V2_SHARE)))
+            y_bf[:].rearrange("p (r i) t -> p r t i", i=Y_RUN), sig[:].rearrange("p t (r i) -> p r t i", i=Y_RUN),
+            us_sb.unsqueeze(1).unsqueeze(3).to_broadcast([P, NQ // Y_RUN, PACK, Y_RUN]), ALU.mult)
+        gather_values(2, [(slice(0, N - V2_SHARE), gather_scalar)], v_g12)
         y_codes, y_scales = quantize_new("y", y_bf[:])
         v01_codes, v01_scales = quantize_new("v01", v01_bf, "y_bf")
-
-        gather_vector(v_g2[:, N - V2_SHARE:], v_win[2][:], entries(tok, slice(N - V2_SHARE, N)))
+        gather_values(2, [(slice(N - V2_SHARE, N), gather_vector)], v_g12)
 
         def product(o_ps, h, codes, scales):
             rows = slice(h * P, (h + 1) * P)
@@ -217,31 +229,37 @@ def tile_attend_at_ropesig_f_topk_kernel(tc, qT, kT, cT, wT, vT, kb, us, offs, o
                 rhs=codes.bitcast(FP8X4), rhs_scale=scales, start=True, stop=True)
 
         out_rows = out[0].rearrange("(h p) e -> p h e", p=P)
-        engines = (nc.vector.tensor_copy, nc.scalar.copy)
         o01_ps = [psum.tile([P, 2 * P], F32, name=f"o01_ps{h}", tag=f"s_ps{h}") for h in range(2)]
         for h in range(2):
             product(o01_ps[h][:], h, v01_codes[:], v01_scales[:])
+
         v_g3 = sb([P, N], BF16, "v_g3", "v_win2")
-        for slots, gather in shared(VECTOR_SHARE):
-            gather(v_g3[:, slots], v_win[3][:], entries(tok, slots))
-        late = sb([P, 4 * P], F32, "late", "v_win3")
+        gather_values(3, shared(V3_SHARE), v_g3)
+        late = sb([P, 2 * 2 * P], F32, "late", "v_win3")
         o01_sb = late[:].rearrange("p (h e) -> p h e", h=2)
-        v_bf[2] = late[:, 2 * P:].bitcast(BF16).rearrange("p (e t) -> p e t", t=PACK)
-        values(2, [], "v_bank2", v_g12)
-        values(3, [], "v_bank3", v_g3[:])
+        v2_bf = late[:, 2 * P:].bitcast(BF16).rearrange("p (e t) -> p e t", t=PACK)
+        turn_values(2, v_g12, "v_bank2", v2_bf, pieces=2)
+        turn_values(3, v_g3[:], "v_bank3", v3_bf, pieces=2)
         for h in range(2):
             nc.vector.tensor_copy(o01_sb[:, h, :], o01_ps[h][:])
             nc.sync.dma_start(out_rows[:, h, :2 * P], o01_sb[:, h, :])
             if h == 0:
-                v2_codes, v2_scales = quantize_new("v2", v_bf[2])
+                v2_codes = sb([P, P], U32, "v2_codes")
+                v2_scales = sb([P, P], U8, "v2_scales")
+                for es in (slice(0, P // 2), slice(P // 2, P)):
+                    quantize(v2_codes[:, es], v2_scales[:, es], v2_bf[:, es, :])
         o2_ps = psum.tile([P, 2, P], F32, name="o2_ps", tag="s_ps2")
         o2_sb = sb([P, 2, P], F32, "o2_sb")
         for h in range(2):
             product(o2_ps[:, h, :], h, v2_codes[:], v2_scales[:])
         nc.scalar.copy(o2_sb[:], o2_ps[:])
         nc.sync.dma_start(out_rows[:, :, 2 * P:3 * P], o2_sb[:])
-        v3_codes, v3_scales = quantize_new("v3", v_bf[3])
-        for h, (copy, bank) in enumerate(zip(engines, ("s_ps3", "kb_ps"))):
+
+        v3_codes = sb([P, P], U32, "v3_codes")
+        v3_scales = sb([P, P], U8, "v3_scales")
+        for es in (slice(0, P // 2), slice(P // 2, P)):
+            quantize(v3_codes[:, es], v3_scales[:, es], v3_bf[:, es, :])
+        for h, (copy, bank) in enumerate(((nc.vector.tensor_copy, "s_ps3"), (nc.scalar.copy, "kb_ps"))):
             o3_ps = psum.tile([P, P], F32, name=f"o3_ps{h}", tag=bank)
             o3_sb = sb([P, P], F32, f"o3_sb{h}")
             product(o3_ps[:], h, v3_codes[:], v3_scales[:])

@@ -87,9 +87,12 @@ def tile_attend_at_ropesig_f_topk_kernel(tc, qT, kT, cT, wT, vT, kb, us, offs, o
         nc.vector.memset(warm[:, 0:1], 0.0)
         nc.scalar.activation(warm[:, 1:2], warm[:, 0:1], ACT.Sigmoid)
 
+        mid = P // 2 - 1
         nc.vector.memset(kb_win[:last, :T // 2], 0.0)
-        nc.gpsimd.memset(kb_win[:last, T // 2:], 0.0)
-        nc.scalar.dma_start(kb_win[last:, :], kb[0:1, :])
+        nc.gpsimd.memset(kb_win[:mid, T // 2:], 0.0)
+        nc.gpsimd.memset(kb_win[mid + 1:, T // 2:], 0.0)
+        nc.scalar.dma_start(kb_win[last:, :T // 2], kb[0:1, :T // 2])
+        nc.scalar.dma_start(kb_win[mid:mid + 1, T // 2:], kb[0:1, T // 2:])
 
         nc.sync.dma_start(c_win[:], c_rows[:, 1:3, :])
         nc.sync.dma_start(pos[:], offs2)
@@ -113,6 +116,9 @@ def tile_attend_at_ropesig_f_topk_kernel(tc, qT, kT, cT, wT, vT, kb, us, offs, o
         kb_by_t = kb_g[:].rearrange("p (m t) -> p t m", t=PACK)
         for t in range(PACK):
             nc.tensor.transpose(kb_ps[:, t, :], kb_by_t[:, t, :], ident[:])
+
+        bias_sum = sb([P, PACK], F32, "bias_sum")
+        nc.vector.tensor_reduce(bias_sum[:], kb_ps[:, :, mid::P // 2], mybir.AxisListType.X, ALU.add)
 
         u_first = sb([P, N // 2, PACK], BF16, "u_first")
 
@@ -163,7 +169,7 @@ def tile_attend_at_ropesig_f_topk_kernel(tc, qT, kT, cT, wT, vT, kb, us, offs, o
         u_bf = [u_first[:], stage[:, :N].bitcast(BF16).rearrange("p (c j) -> p c j", j=PACK)]
         bias = stage[:, N:N + PACK]
         v_g12 = stage[:, N - V1_SHARE // 2:].bitcast(BF16)
-        nc.scalar.copy(bias, kb_ps[:, :, last])
+        nc.scalar.copy(bias, bias_sum[:])
 
         u_codes = sb([P, N], U32, "u_codes")
         u_scales = sb([P, N], U8, "u_scales")

@@ -21,6 +21,7 @@ D = 512
 NQ = 256
 DV = 512
 PER_COLUMN = 16
+LINE = 256
 Q_RUN = 4
 Y_RUN = 2
 
@@ -40,7 +41,7 @@ def tile_attend_at_ropesig_f_topk_kernel(tc, qT, kT, cT, wT, vT, kb, us, offs, o
         psum = ctx.enter_context(tc.psum_pool(name="psum", bufs=1))
 
         def sb(shape, dtype, name, buffer_of=None):
-            return keep.tile(shape, dtype, name=name, tag=buffer_of or name, align_bytes=64)
+            return keep.tile(shape, dtype, name=name, tag=buffer_of or name, align_bytes=LINE)
 
         def quantize(codes, scales, source):
             nc.vector.quantize_mx(codes.bitcast(FP8X4), scales, source.rearrange("p c j -> p (c j)"))

@@ -26,8 +26,7 @@ Q_RUN = 4
 Y_RUN = 2
 
 K_SHARE = 192
-V1_SHARE = 384
-V2_SHARE = 192
+V2_SHARE = 128
 V3_SHARE = 256
 
 FLOPS = 2 * N * NQ * D + 2 * N * NQ * DV
@@ -118,8 +117,8 @@ def tile_attend_at_ropesig_f_topk_kernel(tc, qT, kT, cT, wT, vT, kb, us, offs, o
         for t in range(PACK):
             nc.tensor.transpose(kb_ps[:, t, :], kb_by_t[:, t, :], ident[:])
 
-        bias_sum = sb([P, PACK], F32, "bias_sum")
-        nc.vector.tensor_reduce(bias_sum[:], kb_ps[:, :, mid::P // 2], mybir.AxisListType.X, ALU.add)
+        bias = sb([P, PACK], F32, "bias")
+        nc.vector.tensor_reduce(bias[:], kb_ps[:, :, mid::P // 2], mybir.AxisListType.X, ALU.add)
 
         u_first = sb([P, N // 2, PACK], BF16, "u_first")
 
@@ -166,27 +165,24 @@ def tile_attend_at_ropesig_f_topk_kernel(tc, qT, kT, cT, wT, vT, kb, us, offs, o
         nc.scalar.copy(
             q_bf[:].rearrange("p (r i) j -> p r j i", i=Q_RUN), q_raw[:].rearrange("p j (r i) -> p r j i", i=Q_RUN))
 
-        stage = sb([P, N + (N - V1_SHARE) // 2], F32, "stage", "q_raw")
-        u_bf = [u_first[:], stage[:, :N].bitcast(BF16).rearrange("p (c j) -> p c j", j=PACK)]
-        bias = stage[:, N:N + PACK]
-        v_g12 = stage[:, N - V1_SHARE // 2:].bitcast(BF16)
-        nc.scalar.copy(bias, bias_sum[:])
+        def merge(half, u_half, copy):
+            pair_words = pairs[half][:].rearrange("p a c e -> p a (c e)").bitcast(F32).rearrange("p a c -> p c a")
+            copy(as_words(u_half), pair_words)
 
         u_codes = sb([P, N], U32, "u_codes")
         u_scales = sb([P, N], U8, "u_scales")
         older = (P + K_SHARE) // PACK
         pair_sum(1, terms, 0, slice(0, older))
         pair_sum(1, terms, 0, slice(older, P))
+        merge(0, u_first[:], nc.scalar.copy)
         pair_sum(1, terms, 1)
         q_codes, q_scales = quantize_new("q", q_bf[:], f"k_g{PACK - 1}2")
-
-        for half, copy in enumerate((nc.scalar.copy, nc.vector.tensor_copy)):
-            pair_words = pairs[half][:].rearrange("p a c e -> p a (c e)").bitcast(F32).rearrange("p a c -> p c a")
-            copy(as_words(u_bf[half]), pair_words)
         for t in range(2):
             cols = slice(t * P, (t + 1) * P)
-            quantize(u_codes[:, cols], u_scales[:, cols], u_bf[0][:, cols, :])
-        quantize(u_codes[:, 2 * P:], u_scales[:, 2 * P:], u_bf[1])
+            quantize(u_codes[:, cols], u_scales[:, cols], u_first[:, cols, :])
+        u_second = sb([P, N // 2, PACK], BF16, "u_second", "q_bf")
+        merge(1, u_second[:], nc.vector.tensor_copy)
+        quantize(u_codes[:, 2 * P:], u_scales[:, 2 * P:], u_second[:])
 
         v01_bf = sb([P, 2 * P, PACK], BF16, "v01_bf")[:]
         v3_bf = sb([P, P, PACK], BF16, "v3_bf")[:]
@@ -217,16 +213,23 @@ def tile_attend_at_ropesig_f_topk_kernel(tc, qT, kT, cT, wT, vT, kb, us, offs, o
             nc.scalar.activation(sig[:, t, :], s_ps[:], ACT.Sigmoid, bias=bias[:, t:t + 1])
 
         turn_values(0, v_g0[:], "s_ps0", v01_bf[:, :P, :])
-        gather_values(1, shared(V1_SHARE), v_g12)
+        v_g12 = sb([P, N], BF16, "v_g12", "q_bf")[:]
+        gather_values(1, [(slice(0, N), gather_vector)], v_g12)
         turn_values(1, v_g12, "s_ps1", v01_bf[:, P:, :])
 
         y_bf = sb([P, NQ, PACK], BF16, "y_bf")
-        nc.vector.tensor_tensor(
-            y_bf[:].rearrange("p (r i) t -> p r t i", i=Y_RUN), sig[:].rearrange("p t (r i) -> p r t i", i=Y_RUN),
-            us_sb.unsqueeze(1).unsqueeze(3).to_broadcast([P, NQ // Y_RUN, PACK, Y_RUN]), ALU.mult)
+        halves = (slice(0, P), slice(P, NQ))
+        for qs in halves:
+            nc.vector.tensor_tensor(
+                y_bf[:, qs].rearrange("p (r i) t -> p r t i", i=Y_RUN),
+                sig[:, :, qs].rearrange("p t (r i) -> p r t i", i=Y_RUN),
+                us_sb.unsqueeze(1).unsqueeze(3).to_broadcast([P, P // Y_RUN, PACK, Y_RUN]), ALU.mult)
         gather_values(2, [(slice(0, N - V2_SHARE), gather_scalar)], v_g12)
-        y_codes, y_scales = quantize_new("y", y_bf[:])
-        v01_codes, v01_scales = quantize_new("v01", v01_bf, "y_bf")
+        y_codes = sb([P, NQ], U32, "y_codes")
+        y_scales = sb([P, NQ], U8, "y_scales")
+        for qs in halves:
+            quantize(y_codes[:, qs], y_scales[:, qs], y_bf[:, qs, :])
+        v01_codes, v01_scales = quantize_new("v01", v01_bf)
         gather_values(2, [(slice(N - V2_SHARE, N), gather_vector)], v_g12)
 
         def product(o_ps, h, codes, scales):

@@ -76,7 +76,7 @@ def tile_attend_at_ropesig_f_topk_kernel(tc, qT, kT, cT, wT, vT, kb, us, offs, o
         q_raw = sb([P, PACK, NQ], F32, "q_raw")
         k_win = [sb([P, T], F32, f"k_win{j}") for j in range(PACK)]
         c_win = sb([P, 2, POSITIONS], F32, "c_win")
-        w_win = [sb([P, POSITIONS], F32, f"w_win{a}") for a in range(2)]
+        w_win = sb([P, 2, POSITIONS], F32, "w_win")
         v_win = [sb([P, T], F32, f"v_win{b}") for b in range(DV // P)]
         k_rows = kT.rearrange("(p j) n -> p j n", j=PACK)
         c_rows = cT.rearrange("(p j) n -> p j n", j=PACK)
@@ -91,15 +91,14 @@ def tile_attend_at_ropesig_f_topk_kernel(tc, qT, kT, cT, wT, vT, kb, us, offs, o
         nc.vector.memset(kb_win[:last, :T // 2], 0.0)
         nc.gpsimd.memset(kb_win[:mid, T // 2:], 0.0)
         nc.gpsimd.memset(kb_win[mid + 1:, T // 2:], 0.0)
-        nc.scalar.dma_start(kb_win[last:, :T // 2], kb[0:1, :T // 2])
-        nc.scalar.dma_start(kb_win[mid:mid + 1, T // 2:], kb[0:1, T // 2:])
 
-        nc.sync.dma_start(c_win[:], c_rows[:, 1:3, :])
+        nc.scalar.dma_start(c_win[:], c_rows[:, 1:3, :])
         nc.sync.dma_start(pos[:], offs2)
         nc.sync.dma_start(tok[:], offs)
+        nc.sync.dma_start(kb_win[last:, :T // 2], kb[0:1, :T // 2])
+        nc.sync.dma_start(kb_win[mid:mid + 1, T // 2:], kb[0:1, T // 2:])
+        nc.sync.dma_start(w_win[:], w_rows[:, 1:3, :])
         for j in range(PACK):
-            if j % 2 == 0:
-                nc.sync.dma_start(w_win[j // 2][:], w_rows[:, j, :])
             nc.sync.dma_start(k_win[j][:], k_rows[:, j, :])
         nc.sync.dma_start(q_raw[:], qT[0].rearrange("(p j) q -> p j q", j=PACK))
         for b in range(DV // P):
@@ -125,6 +124,8 @@ def tile_attend_at_ropesig_f_topk_kernel(tc, qT, kT, cT, wT, vT, kb, us, offs, o
         cw = [sb([P, 2, N], F32, f"cw{a}") for a in range(2)]
         gather_scalar(cw[0][:, 0, :], c_win[:, 0, :], pos[:])
         gather_vector(cw[1][:, 0, :], c_win[:, 1, :], pos[:])
+        gather_scalar(cw[0][:, 1, :], w_win[:, 0, :], pos[:])
+        gather_vector(cw[1][:, 1, :], w_win[:, 1, :], pos[:])
 
         pairs = [sb([P, 2, N // 2, 2], BF16, f"pairs{half}") for half in range(2)]
 
@@ -136,15 +137,16 @@ def tile_attend_at_ropesig_f_topk_kernel(tc, qT, kT, cT, wT, vT, kb, us, offs, o
 
         last_plane_cuts = (
             (slice(0, P), gather_scalar), (slice(P, P + K_SHARE), gather_vector), (slice(P + K_SHARE, N), gather_scalar))
+        scalar_alone = ((slice(0, N // 2), gather_scalar), (slice(N // 2, N), gather_scalar))
+        cuts = (shared(K_SHARE), shared(K_SHARE), scalar_alone, last_plane_cuts)
         for a in range(2):
             terms = sb([P, 2, 2, N], F32, f"terms{a}")
-            gather_scalar(cw[a][:, 1, :], w_win[a][:], pos[:])
             for odd in range(2):
                 j = 2 * a + odd
                 parts = []
-                for i, (slots, gather) in enumerate(last_plane_cuts if j == PACK - 1 else shared(K_SHARE)):
+                for i, (slots, gather) in enumerate(cuts[j]):
                     width = slots.stop - slots.start
-                    vector_buffer = "terms0" if a else "k_vector"
+                    vector_buffer = "k_g20" if a else "k_vector"
                     k_g = sb([P, width], F32, f"k_g{j}{i}", vector_buffer if gather is gather_vector else None)
                     gather(k_g[:], k_win[j][:], entries(tok, slots))
                     parts.append((slots, width, k_g))

@@ -26,7 +26,7 @@ Q_RUN = 4
 Y_RUN = 2
 
 K_SHARE = 192
-V2_SHARE = 128
+V2_SHARE = 160
 V3_SHARE = 256
 
 FLOPS = 2 * N * NQ * D + 2 * N * NQ * DV
@@ -121,11 +121,12 @@ def tile_attend_at_ropesig_f_topk_kernel(tc, qT, kT, cT, wT, vT, kb, us, offs, o
 
         u_first = sb([P, N // 2, PACK], BF16, "u_first")
 
-        cw = [sb([P, 2, N], F32, f"cw{a}") for a in range(2)]
-        gather_scalar(cw[0][:, 0, :], c_win[:, 0, :], pos[:])
-        gather_vector(cw[1][:, 0, :], c_win[:, 1, :], pos[:])
-        gather_scalar(cw[0][:, 1, :], w_win[:, 0, :], pos[:])
-        gather_vector(cw[1][:, 1, :], w_win[:, 1, :], pos[:])
+        cw = [sb([P, 3, N], F32, f"cw{a}") for a in range(2)]
+        for s, window in enumerate((c_win, w_win)):
+            gather_scalar(cw[0][:, s, :], window[:, 0, :], pos[:])
+            gather_vector(cw[1][:, s, :], window[:, 1, :], pos[:])
+        for a in range(2):
+            nc.scalar.mul(cw[a][:, 2, :], cw[a][:, 0, :], -1.0)
 
         pairs = [sb([P, 2, N // 2, 2], BF16, f"pairs{half}") for half in range(2)]
 
@@ -135,30 +136,25 @@ def tile_attend_at_ropesig_f_topk_kernel(tc, qT, kT, cT, wT, vT, kb, us, offs, o
                 pairs[half][:, a].rearrange("p (s m) e -> p m e s", s=2)[:, ms],
                 by_slot(terms[:, 0])[:, ms, :, ts], by_slot(terms[:, 1])[:, ms, :, ts], ALU.subtract)
 
+        scalar_halves = ((slice(0, N // 2), gather_scalar), (slice(N // 2, N), gather_scalar))
         last_plane_cuts = (
             (slice(0, P), gather_scalar), (slice(P, P + K_SHARE), gather_vector), (slice(P + K_SHARE, N), gather_scalar))
-        scalar_alone = ((slice(0, N // 2), gather_scalar), (slice(N // 2, N), gather_scalar))
-        cuts = (shared(K_SHARE), shared(K_SHARE), scalar_alone, last_plane_cuts)
+        cuts = (shared(K_SHARE), shared(K_SHARE), scalar_halves, last_plane_cuts)
         for a in range(2):
             terms = sb([P, 2, 2, N], F32, f"terms{a}")
             for odd in range(2):
                 j = 2 * a + odd
+                factors = cw[a][:, odd:odd + 2, :]
                 parts = []
                 for i, (slots, gather) in enumerate(cuts[j]):
                     width = slots.stop - slots.start
-                    vector_buffer = "k_g20" if a else "k_vector"
-                    k_g = sb([P, width], F32, f"k_g{j}{i}", vector_buffer if gather is gather_vector else None)
+                    k_g = sb([P, width], F32, f"k_g{j}{i}", ("k_g20" if a else "k_vector") if gather is gather_vector else None)
                     gather(k_g[:], k_win[j][:], entries(tok, slots))
                     parts.append((slots, width, k_g))
                 for slots, width, k_g in parts:
-                    if odd:
-                        both = terms[:].rearrange("p s j n -> p (s j) n")[:, 1:3, slots]
-                        nc.vector.tensor_tensor(
-                            both, k_g[:].unsqueeze(1).to_broadcast([P, 2, width]), cw[a][:, :, slots], ALU.mult)
-                    else:
-                        nc.vector.tensor_tensor(terms[:, 0, 0, slots], k_g[:], cw[a][:, 0, slots], ALU.mult)
-                        nc.vector.scalar_tensor_tensor(
-                            terms[:, 1, 1, slots], k_g[:], -1.0, cw[a][:, 1, slots], ALU.mult, ALU.mult)
+                    nc.vector.tensor_tensor(
+                        terms[:, odd, :, slots], k_g[:].unsqueeze(1).to_broadcast([P, 2, width]), factors[:, :, slots],
+                        ALU.mult)
             if a == 0:
                 for half in range(2):
                     pair_sum(0, terms, half)
@@ -167,24 +163,26 @@ def tile_attend_at_ropesig_f_topk_kernel(tc, qT, kT, cT, wT, vT, kb, us, offs, o
         nc.scalar.copy(
             q_bf[:].rearrange("p (r i) j -> p r j i", i=Q_RUN), q_raw[:].rearrange("p j (r i) -> p r j i", i=Q_RUN))
 
-        def merge(half, u_half, copy):
+        def merge(half, u_half, copy, cols=slice(0, 2 * P)):
             pair_words = pairs[half][:].rearrange("p a c e -> p a (c e)").bitcast(F32).rearrange("p a c -> p c a")
-            copy(as_words(u_half), pair_words)
+            copy(as_words(u_half)[:, cols], pair_words[:, cols])
 
         u_codes = sb([P, N], U32, "u_codes")
         u_scales = sb([P, N], U8, "u_scales")
         older = (P + K_SHARE) // PACK
         pair_sum(1, terms, 0, slice(0, older))
         pair_sum(1, terms, 0, slice(older, P))
-        merge(0, u_first[:], nc.scalar.copy)
+        merge(0, u_first[:], nc.scalar.copy, slice(0, P))
         pair_sum(1, terms, 1)
+        merge(0, u_first[:], nc.vector.tensor_copy, slice(P, 2 * P))
         q_codes, q_scales = quantize_new("q", q_bf[:], f"k_g{PACK - 1}2")
-        for t in range(2):
+        u_second = sb([P, N // 2, PACK], BF16, "u_second", "q_raw")
+        for t in range(PACK):
             cols = slice(t * P, (t + 1) * P)
-            quantize(u_codes[:, cols], u_scales[:, cols], u_first[:, cols, :])
-        u_second = sb([P, N // 2, PACK], BF16, "u_second", "q_bf")
-        merge(1, u_second[:], nc.vector.tensor_copy)
-        quantize(u_codes[:, 2 * P:], u_scales[:, 2 * P:], u_second[:])
+            u_half = u_second if t // 2 else u_first
+            quantize(u_codes[:, cols], u_scales[:, cols], u_half[:, t % 2 * P:(t % 2 + 1) * P, :])
+            if t == 0:
+                merge(1, u_second[:], nc.vector.tensor_copy)
 
         v01_bf = sb([P, 2 * P, PACK], BF16, "v01_bf")[:]
         v3_bf = sb([P, P, PACK], BF16, "v3_bf")[:]
@@ -202,7 +200,7 @@ def tile_attend_at_ropesig_f_topk_kernel(tc, qT, kT, cT, wT, vT, kb, us, offs, o
                 es = slice(i * P // pieces, (i + 1) * P // pieces)
                 nc.scalar.copy(as_words(v_bf[:, es, :]), v_ps[:, :, es].rearrange("p u e -> p e u"))
 
-        v_g0 = sb([P, N], BF16, "v_g0", "pairs0")
+        v_g0 = sb([P, N], BF16, "v_g0")
         gather_scalar(v_g0[:], v_win[0][:], tok[:])
 
         sig = sb([P, PACK, NQ], F32, "sig", "v_win0")
@@ -215,7 +213,7 @@ def tile_attend_at_ropesig_f_topk_kernel(tc, qT, kT, cT, wT, vT, kb, us, offs, o
             nc.scalar.activation(sig[:, t, :], s_ps[:], ACT.Sigmoid, bias=bias[:, t:t + 1])
 
         turn_values(0, v_g0[:], "s_ps0", v01_bf[:, :P, :])
-        v_g12 = sb([P, N], BF16, "v_g12", "q_bf")[:]
+        v_g12 = sb([P, N], BF16, "v_g12", "q_raw")[:]
         gather_values(1, [(slice(0, N), gather_vector)], v_g12)
         turn_values(1, v_g12, "s_ps1", v01_bf[:, P:, :])
 
@@ -271,7 +269,7 @@ def tile_attend_at_ropesig_f_topk_kernel(tc, qT, kT, cT, wT, vT, kb, us, offs, o
         v3_scales = sb([P, P], U8, "v3_scales")
         for es in (slice(0, P // 2), slice(P // 2, P)):
             quantize(v3_codes[:, es], v3_scales[:, es], v3_bf[:, es, :])
-        for h, (copy, bank) in enumerate(((nc.vector.tensor_copy, "s_ps3"), (nc.scalar.copy, "kb_ps"))):
+        for h, copy, bank in ((1, nc.vector.tensor_copy, "s_ps3"), (0, nc.scalar.copy, "kb_ps")):
             o3_ps = psum.tile([P, P], F32, name=f"o3_ps{h}", tag=bank)
             o3_sb = sb([P, P], F32, f"o3_sb{h}")
             product(o3_ps[:], h, v3_codes[:], v3_scales[:])

@@ -26,7 +26,7 @@ Q_RUN = 4
 Y_RUN = 2
 
 K_SHARE = 192
-V2_SHARE = 160
+V2_SHARE = 128
 V3_SHARE = 256
 
 FLOPS = 2 * N * NQ * D + 2 * N * NQ * DV
@@ -243,7 +243,7 @@ def tile_attend_at_ropesig_f_topk_kernel(tc, qT, kT, cT, wT, vT, kb, us, offs, o
         for h in range(2):
             product(o01_ps[h][:], h, v01_codes[:], v01_scales[:])
 
-        v_g3 = sb([P, N], BF16, "v_g3", "v_win2")
+        v_g3 = sb([P, N], BF16, "v_g3")
         gather_values(3, shared(V3_SHARE), v_g3)
         late = sb([P, 2 * 2 * P], F32, "late", "v_win3")
         o01_sb = late[:].rearrange("p (h e) -> p h e", h=2)

from contextlib import ExitStack

import concourse.mybir as mybir
from concourse.masks import make_identity

F32 = mybir.dt.float32
BF16 = mybir.dt.bfloat16
U32 = mybir.dt.uint32
U16 = mybir.dt.uint16
U8 = mybir.dt.uint8
FP8X4 = mybir.dt.float8_e4m3fn_x4
ACT = mybir.ActivationFunctionType
ALU = mybir.AluOpType

P = 128
PACK = 4
N = 512
T = 2048
POSITIONS = 1024
D = 512
NQ = 256
DV = 512
PER_COLUMN = 16
LINE = 256
Q_RUN = 4
Y_RUN = 2

K_SHARE = 192
V2_SHARE = 128
V3_SHARE = 256

FLOPS = 2 * N * NQ * D + 2 * N * NQ * DV
BYTES = 4 * (D * NQ + D * T + D * POSITIONS + DV * T + T + N + NQ * DV) + 2 * 2 * P * (N // PER_COLUMN)


def tile_attend_at_ropesig_f_topk_kernel(tc, qT, kT, cT, wT, vT, kb, us, offs, offs2, out):
    nc = tc.nc
    with ExitStack() as ctx:
        keep = ctx.enter_context(tc.tile_pool(name="keep", bufs=1))
        psum = ctx.enter_context(tc.psum_pool(name="psum", bufs=1))

        def sb(shape, dtype, name, buffer_of=None):
            return keep.tile(shape, dtype, name=name, tag=buffer_of or name, align_bytes=LINE)

        def quantize(codes, scales, source):
            nc.vector.quantize_mx(codes.bitcast(FP8X4), scales, source.rearrange("p c j -> p (c j)"))

        def quantize_new(name, source, buffer_of=None):
            codes = sb([P, source.shape[1]], U32, f"{name}_codes", buffer_of)
            scales = sb([P, source.shape[1]], U8, f"{name}_scales")
            quantize(codes[:], scales[:], source)
            return codes, scales

        def entries(offsets, slots):
            return offsets[:, slots.start // PER_COLUMN:slots.stop // PER_COLUMN]

        def gather_vector(dest, window, offsets):
            nc.vector.tensor_copy(dest, window.indirect(offsets))

        def gather_scalar(dest, window, offsets):
            nc.scalar.activation(dest, window.indirect(offsets), ACT.Copy)

        def shared(vector_slots):
            return ((slice(0, vector_slots), gather_vector), (slice(vector_slots, N), gather_scalar))

        def by_slot(planes):
            return planes.rearrange("p j (m t) -> p m j t", t=PACK)

        def as_words(tile_bf16):
            return tile_bf16.rearrange("p c j -> p (c j)").bitcast(F32).rearrange("p (c a) -> p c a", a=2)

        tok = sb([P, N // PER_COLUMN], U16, "tok")
        pos = sb([P, N // PER_COLUMN], U16, "pos")
        us_sb = sb([P, PACK], F32, "us_sb")[:]
        kb_win = sb([P, T], F32, "kb_win")
        q_raw = sb([P, PACK, NQ], F32, "q_raw")
        k_win = [sb([P, T], F32, f"k_win{j}") for j in range(PACK)]
        c_win = sb([P, 2, POSITIONS], F32, "c_win")
        w_win = sb([P, 2, POSITIONS], F32, "w_win")
        v_win = [sb([P, T], F32, f"v_win{b}") for b in range(DV // P)]
        k_rows = kT.rearrange("(p j) n -> p j n", j=PACK)
        c_rows = cT.rearrange("(p j) n -> p j n", j=PACK)
        w_rows = wT.rearrange("(p j) n -> p j n", j=PACK)
        last = P - 1

        warm = sb([P, 2], F32, "warm")
        nc.vector.memset(warm[:, 0:1], 0.0)
        nc.scalar.activation(warm[:, 1:2], warm[:, 0:1], ACT.Sigmoid)

        mid = P // 2 - 1
        nc.vector.memset(kb_win[:last, :T // 2], 0.0)
        nc.gpsimd.memset(kb_win[:mid, T // 2:], 0.0)
        nc.gpsimd.memset(kb_win[mid + 1:, T // 2:], 0.0)

        nc.scalar.dma_start(c_win[:], c_rows[:, 1:3, :])
        nc.sync.dma_start(pos[:], offs2)
        nc.sync.dma_start(tok[:], offs)
        nc.sync.dma_start(kb_win[last:, :T // 2], kb[0:1, :T // 2])
        nc.sync.dma_start(kb_win[mid:mid + 1, T // 2:], kb[0:1, T // 2:])
        nc.sync.dma_start(w_win[:], w_rows[:, 1:3, :])
        for j in range(PACK):
            nc.sync.dma_start(k_win[j][:], k_rows[:, j, :])
        nc.sync.dma_start(q_raw[:], qT[0].rearrange("(p j) q -> p j q", j=PACK))
        for b in range(DV // P):
            nc.sync.dma_start(v_win[b][:], vT[b * P:(b + 1) * P, :])
            if b == 1:
                nc.sync.dma_start(us_sb, us[0].rearrange("(p t) o -> p (t o)", t=PACK))

        ident = sb([P, P], F32, "ident")
        make_identity(nc, ident[:])

        kb_g = sb([P, N], F32, "kb_g")
        gather_vector(kb_g[:], kb_win[:], tok[:])
        kb_ps = psum.tile([P, PACK, P], F32, name="kb_ps")
        kb_by_t = kb_g[:].rearrange("p (m t) -> p t m", t=PACK)
        for t in range(PACK):
            nc.tensor.transpose(kb_ps[:, t, :], kb_by_t[:, t, :], ident[:])

        bias = sb([P, PACK], F32, "bias")
        nc.vector.tensor_reduce(bias[:], kb_ps[:, :, mid::P // 2], mybir.AxisListType.X, ALU.add)

        u_first = sb([P, N // 2, PACK], BF16, "u_first")

        cw = [sb([P, 3, N], F32, f"cw{a}") for a in range(2)]
        for s, window in enumerate((c_win, w_win)):
            gather_scalar(cw[0][:, s, :], window[:, 0, :], pos[:])
            gather_vector(cw[1][:, s, :], window[:, 1, :], pos[:])
        for a in range(2):
            nc.scalar.mul(cw[a][:, 2, :], cw[a][:, 0, :], -1.0)

        pairs = [sb([P, 2, N // 2, 2], BF16, f"pairs{half}") for half in range(2)]

        def pair_sum(a, terms, half, ms=slice(0, P)):
            ts = slice(2 * half, 2 * half + 2)
            nc.vector.tensor_tensor(
                pairs[half][:, a].rearrange("p (s m) e -> p m e s", s=2)[:, ms],
                by_slot(terms[:, 0])[:, ms, :, ts], by_slot(terms[:, 1])[:, ms, :, ts], ALU.subtract)

        scalar_halves = ((slice(0, N // 2), gather_scalar), (slice(N // 2, N), gather_scalar))
        last_plane_cuts = (
            (slice(0, P), gather_scalar), (slice(P, P + K_SHARE), gather_vector), (slice(P + K_SHARE, N), gather_scalar))
        cuts = (shared(K_SHARE), shared(K_SHARE), scalar_halves, last_plane_cuts)
        for a in range(2):
            terms = sb([P, 2, 2, N], F32, f"terms{a}")
            for odd in range(2):
                j = 2 * a + odd
                factors = cw[a][:, odd:odd + 2, :]
                parts = []
                for i, (slots, gather) in enumerate(cuts[j]):
                    width = slots.stop - slots.start
                    k_g = sb([P, width], F32, f"k_g{j}{i}", ("k_g20" if a else "k_vector") if gather is gather_vector else None)
                    gather(k_g[:], k_win[j][:], entries(tok, slots))
                    parts.append((slots, width, k_g))
                for slots, width, k_g in parts:
                    nc.vector.tensor_tensor(
                        terms[:, odd, :, slots], k_g[:].unsqueeze(1).to_broadcast([P, 2, width]), factors[:, :, slots],
                        ALU.mult)
            if a == 0:
                for half in range(2):
                    pair_sum(0, terms, half)

        q_bf = sb([P, NQ, PACK], BF16, "q_bf")
        nc.scalar.copy(
            q_bf[:].rearrange("p (r i) j -> p r j i", i=Q_RUN), q_raw[:].rearrange("p j (r i) -> p r j i", i=Q_RUN))

        def merge(half, u_half, copy, cols=slice(0, 2 * P)):
            pair_words = pairs[half][:].rearrange("p a c e -> p a (c e)").bitcast(F32).rearrange("p a c -> p c a")
            copy(as_words(u_half)[:, cols], pair_words[:, cols])

        u_codes = sb([P, N], U32, "u_codes")
        u_scales = sb([P, N], U8, "u_scales")
        older = (P + K_SHARE) // PACK
        pair_sum(1, terms, 0, slice(0, older))
        pair_sum(1, terms, 0, slice(older, P))
        merge(0, u_first[:], nc.scalar.copy, slice(0, P))
        pair_sum(1, terms, 1)
        merge(0, u_first[:], nc.vector.tensor_copy, slice(P, 2 * P))
        q_codes, q_scales = quantize_new("q", q_bf[:], f"k_g{PACK - 1}2")
        u_second = sb([P, N // 2, PACK], BF16, "u_second", "q_raw")
        for t in range(PACK):
            cols = slice(t * P, (t + 1) * P)
            u_half = u_second if t // 2 else u_first
            quantize(u_codes[:, cols], u_scales[:, cols], u_half[:, t % 2 * P:(t % 2 + 1) * P, :])
            if t == 0:
                merge(1, u_second[:], nc.vector.tensor_copy)

        v01_bf = sb([P, 2 * P, PACK], BF16, "v01_bf")[:]
        v3_bf = sb([P, P, PACK], BF16, "v3_bf")[:]

        def gather_values(b, shares, v_g):
            for slots, gather in shares:
                gather(v_g[:, slots], v_win[b][:], entries(tok, slots))

        def turn_values(b, v_g, bank, v_bf, pieces=1):
            v_ps = psum.tile([P, 2, P], F32, name=f"v_ps{b}", tag=bank)
            words = v_g.bitcast(F32).rearrange("p (m u) -> p u m", u=2)
            for u in range(2):
                nc.tensor.transpose(v_ps[:, u, :], words[:, u, :], ident[:])
            for i in range(pieces):
                es = slice(i * P // pieces, (i + 1) * P // pieces)
                nc.scalar.copy(as_words(v_bf[:, es, :]), v_ps[:, :, es].rearrange("p u e -> p e u"))

        v_g0 = sb([P, N], BF16, "v_g0")
        gather_scalar(v_g0[:], v_win[0][:], tok[:])

        sig = sb([P, PACK, NQ], F32, "sig", "v_win0")
        for t in range(PACK):
            cols = slice(t * P, (t + 1) * P)
            s_ps = psum.tile([P, NQ], F32, name=f"s_ps{t}")
            nc.tensor.matmul_mx(
                s_ps[:], lhsT=u_codes[:, cols].bitcast(FP8X4), lhsT_scale=u_scales[:, cols],
                rhs=q_codes[:].bitcast(FP8X4), rhs_scale=q_scales[:], start=True, stop=True)
            nc.scalar.activation(sig[:, t, :], s_ps[:], ACT.Sigmoid, bias=bias[:, t:t + 1])

        turn_values(0, v_g0[:], "s_ps0", v01_bf[:, :P, :])
        v_g12 = sb([P, N], BF16, "v_g12", "q_raw")[:]
        gather_values(1, [(slice(0, N), gather_vector)], v_g12)
        turn_values(1, v_g12, "s_ps1", v01_bf[:, P:, :])

        y_bf = sb([P, NQ, PACK], BF16, "y_bf")
        halves = (slice(0, P), slice(P, NQ))
        for qs in halves:
            nc.vector.tensor_tensor(
                y_bf[:, qs].rearrange("p (r i) t -> p r t i", i=Y_RUN),
                sig[:, :, qs].rearrange("p t (r i) -> p r t i", i=Y_RUN),
                us_sb.unsqueeze(1).unsqueeze(3).to_broadcast([P, P // Y_RUN, PACK, Y_RUN]), ALU.mult)
        gather_values(2, [(slice(0, N - V2_SHARE), gather_scalar)], v_g12)
        y_codes = sb([P, NQ], U32, "y_codes")
        y_scales = sb([P, NQ], U8, "y_scales")
        for qs in halves:
            quantize(y_codes[:, qs], y_scales[:, qs], y_bf[:, qs, :])
        v01_codes, v01_scales = quantize_new("v01", v01_bf)
        gather_values(2, [(slice(N - V2_SHARE, N), gather_vector)], v_g12)

        def product(o_ps, h, codes, scales):
            rows = slice(h * P, (h + 1) * P)
            nc.tensor.matmul_mx(
                o_ps, lhsT=y_codes[:, rows].bitcast(FP8X4), lhsT_scale=y_scales[:, rows],
                rhs=codes.bitcast(FP8X4), rhs_scale=scales, start=True, stop=True)

        out_rows = out[0].rearrange("(h p) e -> p h e", p=P)
        o01_ps = [psum.tile([P, 2 * P], F32, name=f"o01_ps{h}", tag=f"s_ps{h}") for h in range(2)]
        for h in range(2):
            product(o01_ps[h][:], h, v01_codes[:], v01_scales[:])

        v_g3 = sb([P, N], BF16, "v_g3")
        gather_values(3, shared(V3_SHARE), v_g3)
        late = sb([P, 2 * 2 * P], F32, "late", "v_win3")
        o01_sb = late[:].rearrange("p (h e) -> p h e", h=2)
        v2_bf = late[:, 2 * P:].bitcast(BF16).rearrange("p (e t) -> p e t", t=PACK)
        turn_values(2, v_g12, "v_bank2", v2_bf, pieces=2)
        turn_values(3, v_g3[:], "v_bank3", v3_bf, pieces=2)
        for h in range(2):
            nc.vector.tensor_copy(o01_sb[:, h, :], o01_ps[h][:])
            nc.sync.dma_start(out_rows[:, h, :2 * P], o01_sb[:, h, :])
            if h == 0:
                v2_codes = sb([P, P], U32, "v2_codes")
                v2_scales = sb([P, P], U8, "v2_scales")
                for es in (slice(0, P // 2), slice(P // 2, P)):
                    quantize(v2_codes[:, es], v2_scales[:, es], v2_bf[:, es, :])
        o2_ps = psum.tile([P, 2, P], F32, name="o2_ps", tag="s_ps2")
        o2_sb = sb([P, 2, P], F32, "o2_sb")
        for h in range(2):
            product(o2_ps[:, h, :], h, v2_codes[:], v2_scales[:])
        nc.scalar.copy(o2_sb[:], o2_ps[:])
        nc.sync.dma_start(out_rows[:, :, 2 * P:3 * P], o2_sb[:])

        v3_codes = sb([P, P], U32, "v3_codes")
        v3_scales = sb([P, P], U8, "v3_scales")
        for es in (slice(0, P // 2), slice(P // 2, P)):
            quantize(v3_codes[:, es], v3_scales[:, es], v3_bf[:, es, :])
        for h, copy, bank in ((1, nc.vector.tensor_copy, "s_ps3"), (0, nc.scalar.copy, "kb_ps")):
            o3_ps = psum.tile([P, P], F32, name=f"o3_ps{h}", tag=bank)
            o3_sb = sb([P, P], F32, f"o3_sb{h}")
            product(o3_ps[:], h, v3_codes[:], v3_scales[:])
            copy(o3_sb[:], o3_ps[:])
            nc.sync.dma_start(out_rows[:, h, 3 * P:], o3_sb[:])
